import numpy as np, ml_dtypes
CORES = [9,25,41,57]
N = 4
BF = ml_dtypes.bfloat16
def f(rng, *shape):
    return (rng.standard_normal(shape, dtype=np.float32) * np.exp2(rng.integers(-2, 3, shape[:-1] + (1,)))).astype(BF)
def wide(rng, *shape):
    v = f(rng, *shape).astype(np.float32); k = shape[:-2] + (1, shape[-1])
    return (v * np.exp2(rng.integers(-6, 7, k)) * (rng.random(k) > 0.0625)).astype(BF)
def gentries(a):
    return np.ascontiguousarray(a.reshape(8, 16, -1).transpose(0, 2, 1)).reshape(8, -1)
def gtable(e):
    e = np.asarray(e); return np.ascontiguousarray(e.reshape(8, -1, 16).transpose(0, 2, 1)).reshape(128, -1).astype(np.int32)
WAY = "abc"; W = len(WAY)
IC, CG, CAPP, TOT, S = 4096, 512, 1024, 4096, 512
def numbers(a):
    return np.stack([gentries(u) for u in a])
def slots(a):
    return np.stack([gentries(u) for u in a]).reshape(N, N, CAPP)
def columns(t, a):
    e = slots(a); t = t.astype(np.float64)
    return np.stack([np.concatenate([t[q][:, e[q, r]] for q in range(N)], axis=1) for r in range(N)])
def sums(t, x):
    return np.stack([np.bincount(x, weights=t[o], minlength=TOT) for o in range(16)])
def home(p, a):
    e = slots(a); y = np.zeros((N, 16, IC), np.float64)
    for q in range(N):
        for r in range(N):
            y[q][:, e[q, r]] += p[r][:, q * CAPP:(q + 1) * CAPP]
    return y
def anyslots(rng):
    return np.argsort(rng.random((W, N, N, IC)), axis=-1)[..., :CAPP]
def anynumbers(rng):
    x = rng.integers(0, TOT, (W, N, 8, S)); few = rng.integers(0, TOT, (W, N, 8, 32))
    return np.where(rng.random(x.shape) < 0.5, np.take_along_axis(few, rng.integers(0, 32, x.shape), axis=-1), x)
def make(rng, x, e):
    o = np.argsort(x[0], axis=-1, kind="stable"); x = np.stack([np.take_along_axis(u, o, axis=-1) for u in x])
    ob = np.lexsort((rng.random(x[1].shape), x[1]), axis=-1)
    d = {"f" + c: f(rng, N, 16, IC) for c in WAY}
    d["v"] = (rng.standard_normal((N, 8, S)) * np.exp2(rng.integers(-1, 2, (N, 8, 1)))).astype(np.float32)
    for w, c in enumerate(WAY): d["x" + c] = np.stack([gtable(u) for u in x[w]])
    d["ob"] = np.stack([gtable(u) for u in ob])
    for w, c in enumerate(WAY): d["l" + c] = np.stack([gtable(u.reshape(8, CG)) for u in e[w]])
    return d
def setup_inputs(rng):
    return make(rng, anynumbers(rng), anyslots(rng))
def setup_inputs_runs(rng):
    x = anynumbers(rng); h = rng.integers(0, TOT, (W, N, 8, 1))
    for w in range(W): x[w, :, :, w * S // 8:w * S // 8 + S // 2] = h[w]
    x[0, :, 0:2] = h[0, :, 0:1]; x[1, :, 1:3] = h[1, :, 1:2]
    return make(rng, x, anyslots(rng))
def setup_inputs_apart(rng):
    x = np.argsort(rng.random((W, N, 8 * S // TOT, TOT)), axis=-1).reshape(W, N, 8, S)
    return make(rng, x, anyslots(rng))
def setup_inputs_ends(rng):
    x = rng.integers(0, N, (W, N, 8, S)) * CAPP + rng.integers(0, 2, (W, N, 8, S)) * (CAPP - 1)
    x = np.where(rng.random(x.shape) < 0.75, x, rng.integers(0, TOT, x.shape)); x[..., 0] = 0; x[..., 1] = TOT - 1
    e = 1 + np.argsort(rng.random((W, N, N, IC - 2)), axis=-1)[..., :CAPP]; e[..., 0] = IC - 1; e[..., -1] = 0
    return make(rng, x, e)
def setup_inputs_alike(rng):
    x = anynumbers(rng); x[:, :, 1:] = x[:, :, :1].copy()
    e = np.repeat(np.argsort(rng.random((W, N, 1, IC)), axis=-1)[..., :CAPP], N, axis=2)
    return make(rng, x, e)
def setup_inputs_spread(rng):
    d = setup_inputs(rng)
    for c in WAY[1:]: d["f" + c] = wide(rng, N, 16, IC)
    return d
def check_inputs(d):
    bad = []
    for c in WAY:
        x = numbers(d["x" + c]); e = slots(d["l" + c])
        if not np.isfinite(d["f" + c].astype(np.float32)).all(): bad.append("finite_f" + c)
        if x.min() < 0 or x.max() >= TOT: bad.append("range_x" + c)
        if e.min() < 0 or e.max() >= IC: bad.append("range_l" + c)
        if (np.diff(np.sort(e, axis=-1), axis=-1) == 0).any(): bad.append("different_l" + c)
    if not np.isfinite(d["v"]).all(): bad.append("finite_v")
    if (np.diff(numbers(d["xa"]), axis=-1) < 0).any(): bad.append("sorted_xa")
    o = numbers(d["ob"])
    if not (np.sort(o, axis=-1) == np.arange(S)).all(): bad.append("places_ob")
    elif (np.diff(np.take_along_axis(numbers(d["xb"]), o, axis=-1), axis=-1) < 0).any(): bad.append("sorted_xb_by_ob")
    return bad
def reference(fa, fb, fc, v, xa, xb, xc, ob, la, lb, lc):
    xi = numbers(xa).reshape(N, 8 * S); xj = numbers(xb).reshape(N, 8 * S)
    w = np.repeat(v.astype(np.float64).reshape(N, 1, 8 * S), 16, axis=1)
    for t, x, a in ((fc, xc, lc),):
        u = columns(t, a); x = numbers(x).reshape(N, 8 * S)
        w = w * np.stack([u[r][:, x[r]] for r in range(N)])
    u = columns(fb, lb)
    ya = fa.astype(np.float64) * home([sums(w[r] * u[r][:, xj[r]], xi[r]) for r in range(N)], la)
    u = columns(ya, la)
    yb = home([sums(w[r] * u[r][:, xi[r]], xj[r]) for r in range(N)], lb)
    return {"ya": ya.astype(np.float32), "yb": yb.astype(np.float32)}

@@ -1,0 +1,681 @@
+from concourse.mybir import AluOpType, ActivationFunctionType
+
+OP = AluOpType
+COPY = ActivationFunctionType.Copy
+IDENTITY = ActivationFunctionType.Identity
+ZW = 4728
+DC = 2048
+OWN = 2
+SIZES = {
+    "int32": {128: "Di Ei Gi Gs", 32: "tla tlb txa txb txc tob"},
+    "uint16": {256: "Lr"},
+    "bfloat16": {128: "E16", 512: "a1 a2 s1 s2 ssrc fag", 1024: "SELB CB LCB", 4096: "fcr fbr far Cw Bw W R fb16",
+                 4096 - DC: "fc16"},
+    "float32": {128: "E ident GRP vsel N1 N2 m3", 256: "m2", 520: "flA flB",
+                512: "X v8 vex vc vco xe xr mk w1 w2 scn scm RT PT RU PU LP OT LA LQ faS ac0 ac1 ac2 ac3 ya0 ya1 ya2 ya3 yo",
+                1024: "SEL", 1032: "pw0 pw1 pw2 pw3 qw", 4096: "Aw", ZW: "zA zB"},
+}
+SMALL = {
+    "int32": {4: "kri krs", 8: "kgi kgs k1 p15 hk", 32: "ba bb bd pii be bf bg pij nb nbi nhi nlo", 128: "vsi vss"},
+    "uint16": {32: "La Lb Lc ja jb jc jo pia pib snA snB offA offB", 128: "idx inva invb"},
+    "bfloat16": {4: "rsel"},
+    "float32": {4: "rm4", 8: "rm8 m0 m1 n0 hm hf hb w01", 32: "trash pif sa ta sb tb", 40: "yl ym", 64: "m4"},
+}
+SCRATCH = {n: ("sbuf", [128, c], d) for d, x in SIZES.items() for c, names in x.items() for n in names.split()}
+PLACE = {}
+for _d, _x in SMALL.items():
+    _at = 0
+    for _c, _names in _x.items():
+        for _n in _names.split():
+            PLACE[_n] = ("small_" + _d, _at, _c)
+            _at += -(-_c // 16) * 16
+    SCRATCH["small_" + _d] = ("sbuf", [128, _at], _d)
+for _t in ("la", "lb", "lc"):
+    SCRATCH["u" + _t] = ("sbuf", [128, 4, 8], "int32")
+    SCRATCH["tm" + _t[1]] = ("sbuf", [128, 4, 4, 8], "float32")
+for _b in range(8):
+    SCRATCH["pb%d" % _b] = ("psum", [128, 512], "float32")
+ENG = {"v": "sv", "s": "ss", "t": "st", "g": "sg"}
+SEMAPHORES = (list(ENG.values()) + ["dt" + t for t in ("la", "lb", "xa", "xb", "xc", "ob")] + ["du" + t for t in ("la", "lb", "lc")]
+              + ["dv", "dfb", "dfc", "dfe", "dfa", "dfg", "dya", "dyb", "ls"]
+              + ["%s%d" % (k, d) for k in "cpnq" for d in (1, 2, 3)])
+CYCLE, GATHER, SCATTER, WAKE, PE = 0.000913, 1.5, 3.2, 0.06, 0.5
+ISSUE, FIRST, HOP, RATE = 0.45, 1.0, 1.3, 55e3
+DMA_ISSUE, DMA_TIME, DMA_RATE = 0.07, 1.6, 180e3
+BYTES = {"float32": 4, "int32": 4, "bfloat16": 2, "uint16": 2}
+LEAN = {"list": 8.5, "inv": 5.0, "r": 0.6, "lb": 3.5, "vco": 2.0, "ib": 0.0, "ya": 0.0, "fas": 5.0, "own": 7.3, "wf": 0.0,
+        "ss": -2.5, "jc": -1.5, "vex": 0.0, "pw": 6.0, "red": 12.0}
+
+
+def op_time(op):
+    t = min(op["cost"].values()) if op["cost"] else 0.0
+    if op["kind"] == "send":
+        t += op["bytes"] / RATE + HOP
+    elif op["kind"] == "dma":
+        t += op["bytes"] / DMA_RATE + DMA_TIME
+    return t
+
+
+def order(ops):
+    n = len(ops)
+    pred = [set(op["after"]) for op in ops]
+    last = {}
+    for i, op in enumerate(ops):
+        both = [(v, True) for v in op["outs"] if v[0]] + [(v, False) for v in op["ins"] if v[0]]
+        for v, w in both:
+            for lo, hi, w2, j in last.setdefault(v[0], []):
+                if j != i and lo < v[2] and v[1] < hi and (w or w2):
+                    pred[i].add(j)
+        for v, w in both:
+            rec = last[v[0]]
+            if w:
+                rec[:] = [r for r in rec if not (v[1] <= r[0] and r[1] <= v[2])]
+            rec.append((v[1], v[2], w, i))
+    succ = [[] for _ in ops]
+    for i in range(n):
+        for j in pred[i]:
+            succ[j].append(i)
+    users = {}
+    for op in ops:
+        for b in op["banks"]:
+            users[b] = users.get(b, 0) + 1
+    prio = [0.0] * n
+    for i in reversed(range(n)):
+        prio[i] = op_time(ops[i]) + max([prio[k] + WAKE for k in succ[i]] or [0.0])
+    prio = [prio[i] + ops[i]["lean"] for i in range(n)]
+    free = {q: 0.0 for q in "vstgy"}
+    end = [None] * n
+    bank_of, bank_free = {}, {b: 0.0 for b in range(8)}
+    port, dma, first = 0.0, 0.0, True
+    out = []
+    ready = [i for i in range(n) if not pred[i]]
+    missing = [len(p) for p in pred]
+    chain = {}
+    for i, op in enumerate(ops):
+        if op["eng"] in "gy":
+            chain.setdefault(op["eng"], []).append(i)
+    while ready:
+        cand = []
+        for i in ready:
+            op = ops[i]
+            if op["eng"] in chain and chain[op["eng"]][0] != i:
+                continue
+            st = max([end[j] + WAKE for j in pred[i]] or [0.0])
+            bank = None
+            if op["eng"] == "t" and op["banks"] and op["banks"][0] not in bank_of:
+                idle = [b for b in bank_free if bank_free[b] is not None]
+                if not idle:
+                    continue
+                bank = min(idle, key=lambda b: bank_free[b])
+                st = max(st, bank_free[bank])
+            if op["eng"] == "-":
+                cand.append((st, i, "-", st, bank))
+                continue
+            best = None
+            for e in op["eng"]:
+                s1 = max(st, free[e])
+                f1 = s1 + op["cost"][e]
+                if best is None or f1 < best[0] - 0.01:
+                    best = (f1, i, e, s1, bank)
+            cand.append(best)
+        assert cand, "no call can go on"
+        f0, _, e0, _, _ = min(cand)
+        conflict = [c for c in cand if c[2] == e0 and c[3] < f0 - 1e-6] or [min(cand)]
+        f1, i, e, s1, bank = max(conflict, key=lambda c: (prio[c[1]], -c[1]))
+        op = ops[i]
+        ready.remove(i)
+        if op["eng"] in chain:
+            chain[op["eng"]].pop(0)
+        if bank is not None:
+            bank_of[op["banks"][0]] = bank
+            bank_free[bank] = None
+        end[i] = f1
+        if e != "-":
+            free[e] = f1
+        if op["kind"] == "dma":
+            dma = max(dma, f1) + op["bytes"] / DMA_RATE
+            end[i] = dma + DMA_TIME
+        elif op["kind"] == "send":
+            if first:
+                f1 += FIRST
+                first = False
+                free["g"] = f1
+            port = max(port, f1) + op["bytes"] / RATE
+            end[i] = port + HOP
+        for b in op["banks"]:
+            users[b] -= 1
+            if not users[b]:
+                bank_free[bank_of[b]] = f1 + WAKE
+        out.append((i, e, {b: "pb%d" % bank_of[b] for b in op["banks"]}))
+        for k in succ[i]:
+            missing[k] -= 1
+            if not missing[k]:
+                ready.append(k)
+    assert len(out) == n
+    return out
+
+
+def rank_program(g, core, T, topo):
+    me = T.rank_of(core)
+    if me is None:
+        return
+    N = len(T.cores)
+    queue = {"v": g.vector, "s": g.scalar, "t": g.tensor, "g": g, "y": g.sync}
+    count = {}
+    know = {e: {} for e in queue}
+    waited = {}
+    seen = {}
+    banks = {"pb%d" % b: {} for b in range(8)}
+    where = {}
+    ops = []
+    lean = [0.0]
+    turn = [0]
+    sent = {}
+
+    def wait(e, tok):
+        sem, val, _, kn = tok
+        if know[e].get(sem, 0) >= val:
+            return
+        queue[e].wait_ge(T.sem[sem], val)
+        waited[sem] = max(waited.get(sem, 0), val)
+        for k2, v2 in kn.items():
+            if know[e].get(k2, 0) < v2:
+                know[e][k2] = v2
+        know[e][sem] = val
+
+    def before(e, outs, ins):
+        for (n, lo, hi, _), w in [(x, True) for x in outs] + [(x, False) for x in ins]:
+            n = where.get(n, n)
+            if n in banks:
+                for e2 in list(banks[n]):
+                    if e2 != e:
+                        wait(e, banks[n].pop(e2))
+                continue
+            for lo2, hi2, w2, tok in seen.get(n, []):
+                if lo2 < hi and lo < hi2 and (w or w2):
+                    wait(e, tok)
+
+    def after(outs, ins, tok):
+        for (n, lo, hi, _), w in [(x, True) for x in outs] + [(x, False) for x in ins]:
+            n = where.get(n, n)
+            if n in banks:
+                banks[n][tok[2]] = tok
+                continue
+            old = seen.setdefault(n, [])
+            if w:
+                old[:] = [r for r in old if not (lo <= r[0] and r[1] <= hi)]
+            old.append((lo, hi, w, tok))
+
+    def emit(e, outs, ins, call):
+        before(e, outs, ins)
+        sem = ENG[e]
+        call(queue[e], e).then_inc(T.sem[sem], 1)
+        count[sem] = count.get(sem, 0) + 1
+        after(outs, ins, (sem, count[sem], e, dict(know[e])))
+
+    def emit_dmas(sem, items, extra):
+        before(items[0][0], [], extra)
+        kn = {}
+        for e, o, i in items:
+            before(e, [o] if o[0] else [], [i] if i[0] else [])
+            queue[e].dma_start(out=o[3](), in_=i[3]()).then_inc(T.sem[sem], 16)
+            count[sem] = count.get(sem, 0) + 16
+            for k2, v2 in know[e].items():
+                kn[k2] = max(kn.get(k2, 0), v2)
+        tok = (sem, count[sem], "d", kn)
+        done = []
+        for e, o, i in items:
+            if o[0] and o[:3] not in done:
+                done.append(o[:3])
+                after([o], [], tok)
+            if i[0]:
+                after([], [i], tok)
+
+    def emit_send(q, src, dst, sem):
+        to = T.cores[q]
+        before("g", [], [src])
+        rid, pid, _ = topo.addr(to)
+        g.remote_dma(out_ap=dst, in_ap=src[3](), remote_sem=T.sem["%s%d" % (sem, (q - me) % N)], local_sem=T.sem["ls"],
+                     pid=pid, routing_id=rid, dma_engine_mask=topo.mask(core, to))
+        count["ls"] = count.get("ls", 0) + len(topo.engines(core, to))
+
+    def emit_come(v, s, q):
+        count[s] = len(topo.engines(T.cores[q], core))
+        after([v], [], (s, count[s], "r", {}))
+
+    def V(name, lo=0, hi=None, step=1, p0=0, p1=128):
+        at = 0
+        if name in PLACE:
+            name, at, w = PLACE[name]
+            hi = w if hi is None else hi
+        elif hi is None:
+            hi = 512 if name[0] == "#" else SCRATCH[name][1][1]
+        lo, hi = lo + at, hi + at
+
+        def ap():
+            t = T[where.get(name, name)]
+            return t[p0:p1, lo:hi] if step == 1 else t[p0:p1, lo:hi:step]
+        return (name, lo, hi, ap)
+
+    def H(ap):
+        return (None, 0, 0, lambda: ap)
+
+    def group(name, b, lo=0, hi=None):
+        return V(name, lo, hi, p0=16 * b, p1=16 * b + 16)
+
+    def bank():
+        turn[0] += 1
+        return "#%d" % turn[0]
+
+    def op(eng, outs, ins, subs, cost, kind="c", nbytes=0, needs=()):
+        names = []
+        for v in outs + ins:
+            if v[0] and v[0][0] == "#" and v[0] not in names:
+                names.append(v[0])
+        ops.append({"eng": eng, "outs": outs, "ins": ins, "subs": subs, "cost": cost, "kind": kind, "bytes": nbytes,
+                    "banks": names, "after": list(needs), "lean": lean[0]})
+        return len(ops) - 1
+
+    def size(v):
+        return v[2] - v[1]
+
+    def narrow(*vs):
+        return all(v[0][0] != "#" and BYTES[SCRATCH[v[0]][2]] == 2 for v in vs)
+
+    def cyc(n):
+        return max(64, n) * CYCLE
+
+    def one(eng, outs, ins, call, cost):
+        op(eng, outs, ins, [(outs, ins, call)], cost)
+
+    def copy(o, i, e="vs"):
+        n = size(o)
+        cost = {"v": cyc(n * 0.5 if narrow(o, i) else n), "s": cyc(n)}
+        one(e, [o], [i], lambda q, x: q.tensor_copy(o[3](), i[3]()) if x == "v" else q.activation(o[3](), i[3](), COPY), cost)
+
+    def scaled(o, i, sc, b=None):
+        if b is None:
+            one("s", [o], [i, sc], lambda q, x: q.activation(o[3](), i[3](), COPY, scale=sc[3]()), {"s": cyc(size(o))})
+        else:
+            one("s", [o], [i, sc, b], lambda q, x: q.activation(o[3](), i[3](), IDENTITY, bias=b[3](), scale=sc[3]()),
+                {"s": cyc(size(o))})
+
+    def ts(o, i, s1, op0, s2=None, op1=None, n=None):
+        rd = [i] + [s for s in (s1, s2) if isinstance(s, tuple)]
+
+        def call(q, x):
+            a1 = s1[3]() if isinstance(s1, tuple) else s1
+            a2 = s2[3]() if isinstance(s2, tuple) else s2
+            if op1 is None:
+                return q.tensor_scalar(o[3](), i[3](), a1, None, op0)
+            return q.tensor_scalar(o[3](), i[3](), a1, a2, op0, op1)
+        one("v", [o], rd, call, {"v": cyc(size(i))})
+
+    def tt(o, a, b, f):
+        n = size(a) * (1 if a[0][0] == "#" or b[0][0] == "#" else 2)
+        one("v", [o], [a, b], lambda q, x: q.tensor_tensor(o[3](), a[3](), b[3](), f), {"v": cyc(n)})
+
+    def fill(o, c):
+        one("v", [o], [], lambda q, x: q.memset(o[3](), c), {"v": cyc(size(o) * (0.5 if narrow(o) else 1))})
+
+    def ind(w, l):
+        return w[3]().indirect(l[3]())
+
+    def pick(o, w, l, e="vs"):
+        n = size(l) * 16 * GATHER * CYCLE
+        one(e, [o], [w, l], lambda q, x: q.tensor_copy(o[3](), ind(w, l)) if x == "v" else q.activation(o[3](), ind(w, l), COPY),
+            {"v": n + 0.05, "s": n + 0.065})
+
+    def pick2(o, w, l, b, f):
+        one("v", [o], [w, l, b], lambda q, x: q.tensor_tensor(o[3](), ind(w, l), b[3](), f),
+            {"v": size(l) * 16 * GATHER * CYCLE + 0.05})
+
+    def put(w, l, i):
+        one("v", [w], [l, i], lambda q, x: q.tensor_copy(ind(w, l), i[3]()), {"v": size(l) * 16 * SCATTER * CYCLE + 0.05})
+
+    def mms(items):
+        outs, ins, subs, cost = [], [], [], 0.0
+        for o, l, r, a, z in items:
+            outs.append(o)
+            ins += [l, r]
+            subs.append(([o], [l, r], lambda q, x, o=o, l=l, r=r, a=a, z=z: q.matmul(o[3](), l[3](), r[3](), a, z)))
+            cost += max(64, size(r)) * (1 if narrow(l) else 4) * PE * CYCLE
+        op("t", outs, ins, subs, {"t": cost})
+
+    def mm(o, l, r):
+        mms([(o, l, r, True, True)])
+
+    def iota(o, pattern, base, cm, small=False):
+        if small:
+            call = lambda q, x: q.iota(o[3](), pattern, base, cm, allow_small_or_imprecise_dtypes=True)
+        else:
+            call = lambda q, x: q.iota(o[3](), pattern, base, cm)
+        one("g", [o], [], call, {"g": 0.13 + 2 * size(o) * CYCLE})
+
+    def zeros(o):
+        iota(o, [[0, size(o)]], 0, 0, True)
+
+    def dmas(sem, items, nbytes, extra=()):
+        e = items[0][0]
+        outs, ins = [], list(extra)
+        for _, o, i in items:
+            outs += [o] if o[0] and o[:3] not in [x[:3] for x in outs] else []
+            ins += [i] if i[0] else []
+        op(e, outs, ins, (sem, items, list(extra)), {e: DMA_ISSUE * len(items)}, "dma", nbytes)
+
+    def send(q, src, dst, sem):
+        sent[sem, (q - me) % N] = op("g", [], [src], (q, src, dst, sem), {"g": ISSUE}, "send",
+                                     128 * size(src) * BYTES[SCRATCH[src[0]][2]])
+
+    def expect(buf, width, sem):
+        for d in (1, 2, 3):
+            q, s = (me - d) % N, "%s%d" % (sem, d)
+            v = V(buf, q * width, (q + 1) * width)
+            op("-", [v], [], (v, s, q), {}, "come", 0, [sent[sem, d]])
+
+    ring = [(me + d) % N for d in (1, 2, 3, 0)]
+    come = [(me - d) % N for d in (0, 1, 2, 3)]
+
+    def U(t):
+        return ("u" + t, 0, 32, lambda: T["u" + t][:, :, :])
+
+    def table(t, e):
+        dmas("dt" + t, [(e, V("t" + t), H(T[t][:, :]))], 16384)
+
+    def table3(t, e):
+        dmas("du" + t, [(e, U(t), H(T[t][:, :]))], 16384)
+
+    table3("lc", "y")
+    dmas("dfb", [("s", V("fb16", p0=0, p1=16), H(T.fb[:, :]))], 131072)
+    dmas("dfe", [("y", V("fc16", p0=0, p1=16), H(T.fc[:, DC:4096]))], 65536)
+    table3("lb", "s")
+    dmas("dfc", [("y", group("fcr", b, 0, DC), H(T.fc[:, 0:DC])) for b in range(8)], 16 * DC * 2 * 8)
+    table("la", "y")
+    table("xa", "y")
+    table3("la", "y")
+    dmas("dv", [("y", V("v8", p0=0, p1=8), H(T.v[:, :]))], 16384)
+    for t in ("xc", "xb", "ob", "lb"):
+        table(t, "y")
+
+    iota(V("Di"), [[-1, 128]], 128, 1)
+    iota(V("k1"), [[0, 8]], 0, 1)
+    iota(V("kri"), [[-32, 4]], 0, 1)
+    iota(V("kgi"), [[-16, 8]], 0, 1)
+    iota(V("trash"), [[16, 32]], 4097, 1, True)
+    iota(V("w01"), [[1, 8]], 0, 0, True)
+    iota(V("vsi", p1=8), [[1, 128]], 0, -16)
+    iota(V("Gi"), [[-16, 8], [0, 16]], 0, 1)
+    iota(V("a1"), [[128, 4], [0, 128]], 0, 0, True)
+    iota(V("a2"), [[0, 4], [1, 128]], 8, 0, True)
+
+    fill(V("X"), 0.0)
+    ts(V("Ei"), V("Di"), 15, OP.bitwise_and)
+    ts(V("hk"), V("k1"), 4, OP.arith_shift_right, 1, OP.bitwise_and)
+    ts(V("p15"), V("k1"), 15, OP.bitwise_and)
+    ts(V("krs"), V("kri"), 5, OP.arith_shift_right)
+    ts(V("kgs"), V("kgi"), 4, OP.arith_shift_right)
+    ts(V("E16"), V("Ei"), 0, OP.is_equal)
+    ts(V("E"), V("Ei"), 0, OP.is_equal)
+    ts(V("hf"), V("hk"), 1, OP.mult)
+    ts(V("m0"), V("p15"), 0, OP.is_equal)
+    ts(V("m1"), V("p15"), 1, OP.is_equal)
+    ts(V("hb"), V("hf"), 512.0, OP.mult, V("m0", 0, 1), OP.mult)
+    ts(V("rm4"), V("krs"), 0, OP.is_equal)
+    ts(V("hm"), V("hk"), 0, OP.is_equal)
+    for b in range(8):
+        ts(V("X", 128 * (b % 4) + 16 * b, 128 * (b % 4) + 16 * b + 16), V("E", 0, 16),
+           V("hm" if b < 4 else "hf", 0, 1), OP.mult)
+    ts(V("rm8"), V("kgs"), 0, OP.is_equal)
+    ts(V("n0"), V("p15"), 0, OP.not_equal)
+    ts(V("N1"), V("Di"), 129, OP.is_equal, V("n0", 0, 1), OP.mult)
+    ts(V("N2"), V("Di"), 113, OP.is_equal, V("m0", 0, 1), OP.mult)
+    ts(V("ident"), V("Di"), 128, OP.is_equal)
+    ts(V("rsel"), V("krs"), 0, OP.is_equal)
+    ts(V("Gs"), V("Gi"), 4, OP.arith_shift_right)
+    ts(V("GRP"), V("Gs"), 0, OP.is_equal)
+    ts(V("vss", p1=8), V("vsi", p1=8), 4, OP.arith_shift_right)
+    ts(V("vsel", p1=8), V("vss", p1=8), 0, OP.is_equal)
+
+    def tiles_list(t, dst):
+        tm, u = "tm" + t[1], U(t)
+        for r in range(4):
+            ts((tm, r, r + 1, lambda r=r: T[tm][:, :, r, :]), u, V("rm4", r, r + 1), OP.mult)
+        p = bank()
+        mms([(V(p, 0, 32), V("X", 128 * b, 128 * b + 128), (tm, 0, 4, lambda b=b: T[tm][:, b, :, :]), b == 0, b == 3)
+             for b in range(4)])
+        copy(V(dst), V(p, 0, 32), "v")
+
+    tiles_list("lc", "Lc")
+    tiles_list("lb", "Lb")
+    for i in range(8):
+        for src, dst, lo in (("fc16", "fcr", DC), ("fb16", "fbr", 0)):
+            if 512 * i >= lo:
+                p = bank()
+                mm(V(p), V("E16", p1=16), V(src, 512 * i - lo, 512 * i - lo + 512, p1=16))
+                copy(V(dst, 512 * i, 512 * i + 512), V(p))
+
+    for r in ring:
+        pick(V("CB", 256 * r, 256 * r + 128), V("fcr"), V("Lc", 8 * r, 8 * r + 8))
+        pick(V("CB", 256 * r + 128, 256 * r + 256), V("fbr"), V("Lb", 8 * r, 8 * r + 8))
+        if r != me:
+            send(r, V("CB", 256 * r, 256 * r + 256), T["LCB"][:, 256 * me:256 * me + 256], "c")
+    expect("LCB", 256, "c")
+    for i in range(4):
+        zeros(V("zA", 1026 * i, 1026 * i + 1026))
+
+    dmas("dfa", [("y", group("far", b), H(T.fa[:, :])) for b in range(8)], 1 << 20, [V("LCB")])
+    dmas("dfg", [("y", group("fag", b), H(T.fa[:, 512 * b:512 * b + 512])) for b in range(8)], 131072)
+
+    for name in ("SELB", "SEL"):
+        for b in range(8):
+            scaled(V(name, 128 * b, 128 * b + 128), V("E"), V("rm8", b, b + 1))
+    lean[0] = LEAN["ss"]
+    scaled(V("s1"), V("a1"), V("m0", 0, 1), V("hb", 0, 1))
+    scaled(V("s2"), V("a2"), V("m1", 0, 1))
+    tt(V("ssrc"), V("s1"), V("s2"), OP.add)
+
+    def places(t, dst, a, b, d, e):
+        ts(V(a), V(t), 0x1F0, OP.bitwise_and)
+        ts(V(b), V(t), 5, OP.arith_shift_right, 0x70, OP.bitwise_and)
+        ts(V(d), V(t), 15, OP.bitwise_and)
+        ts(V(a), V(a), 8, OP.mult)
+        tt(V(b), V(a), V(b), OP.add)
+        tt(V(e), V(b), V(d), OP.add)
+        copy(V(dst), V(e), "v")
+
+    def runs(yl, sn, tr, snu, off, fl):
+        p = bank()
+        mms([(V(p, 0, 32), V("N1"), V(yl, 0, 32), True, False), (V(p, 0, 32), V("N2"), V(yl, 1, 33), False, True)])
+        tt(V(sn), V(p, 0, 32), V(yl, 0, 32), OP.is_equal)
+        copy(V(snu), V(sn), "v")
+        tt(V(tr), V(sn), V("trash"), OP.mult)
+        tt(V(tr), V(tr), V(yl, 0, 32), OP.max)
+        copy(V(off), V(tr), "v")
+        fill(V(fl, 0, 8), 0.0)
+        pick(V(fl, 8, 520), V("w01"), V(snu))
+
+    def lists(src, col, dst):
+        p = bank()
+        mms([(V(p, 4 * k, 4 * k + 4), V(src, 128 * col[k], 128 * col[k] + 128), V("rsel"), True, True) for k in range(32)])
+        for r in range(4):
+            copy(V(dst, 32 * r, 32 * r + 32), V(p, r, 128, 4), "v")
+
+    lean[0] = LEAN["vex"]
+    p = bank()
+    mm(V(p), V("vsel", p1=8), V("v8", p1=8))
+    copy(V("vex"), V(p))
+    lean[0] = LEAN["list"]
+    fill(V("yl"), 0.0)
+    ts(V("yl", 0, 32), V("txa"), 1, OP.add)
+    runs("yl", "sa", "ta", "snA", "offA", "flA")
+    lean[0] = LEAN["jc"]
+    copy(V("jc"), V("txc"), "v")
+    copy(V("jb"), V("txb"), "v")
+    lean[0] = LEAN["fas"]
+    tiles_list("la", "La")
+    lean[0] = LEAN["inv"]
+    places("tla", "pia", "ba", "bb", "bd", "pii")
+    copy(V("pif"), V("pii"), "v")
+    lean[0] = LEAN["wf"]
+    for i in range(4):
+        fill(V("W", 1024 * i, 1024 * i + 1024), 0.0)
+    lean[0] = LEAN["inv"]
+    put(V("W"), V("pia"), V("ssrc"))
+    p = bank()
+    mms([(V(p, 32 * i, 32 * i + 32), V("SEL", 128 * i, 128 * i + 128), V("pif"), True, True) for i in range(8)])
+    for k in range(8):
+        copy(V("Lr", 32 * k, 32 * k + 32), V(p, k, 256, 8), "v")
+    lean[0] = LEAN["r"]
+    for i in range(8):
+        pick(V("R", 512 * i, 512 * i + 512), V("W"), V("Lr", 32 * i, 32 * i + 32), "s")
+    lists("R", [(i % 8) * 4 + i // 8 for i in range(32)], "idx")
+    lean[0] = LEAN["ya"]
+    lists("W", list(range(32)), "inva")
+    lean[0] = 0.0
+
+    for n, q in enumerate(come):
+        buf = "CB" if q == me else "LCB"
+        for f, win in ((0, "Cw"), (1, "Bw")):
+            for h in range(2):
+                p = bank()
+                mms([(V(p, 128 * b, 128 * b + 128), V("SELB", 128 * (4 * h + b), 128 * (4 * h + b) + 128),
+                      V(buf, 256 * q + 128 * f, 256 * q + 128 * f + 128), True, True) for b in range(4)])
+                copy(V(win, 1024 * q + 512 * h, 1024 * q + 512 * h + 512), V(p))
+    pick2(V("vc"), V("Cw"), V("jc"), V("vex"), OP.mult)
+    pick2(V("w1"), V("Bw"), V("jb"), V("vc"), OP.mult)
+
+    def addruns(src, fl, off, z, scn):
+        o, a, b = V(scn), V(fl, 7, 519), V(src)
+        one("v", [o], [a, b], lambda q, x: q.tensor_tensor_scan(o[3](), a[3](), b[3](), 0.0, OP.mult, OP.add), {"v": cyc(512)})
+        put(V(z), V(off), V(scn))
+
+    def reduce(z, land, sem, RT, PT, pw):
+        lean[0] = LEAN["red"]
+        for q in ring[:3]:
+            p = bank()
+            mms([(V(p, 16 * b, 16 * b + 16), V(z, 1 + 1024 * q + 128 * b, 129 + 1024 * q + 128 * b), V("E", 0, 16), True, True)
+                 for b in range(8)])
+            copy(V(RT, 128 * q, 128 * q + 128), V(p, 0, 128))
+            p = bank()
+            o, i, idn = V(p, 0, 128), V(RT, 128 * q, 128 * q + 128), V("ident")
+            op("t", [o], [i, idn], [([o], [i, idn], lambda k, x, o=o, i=i: k.transpose(o[3](), i[3](), idn[3]()))],
+               {"t": 512 * PE * CYCLE})
+            copy(V(PT, 128 * q, 128 * q + 128), V(p, 0, 128))
+            send(q, V(PT, 128 * q, 128 * q + 128), T[land][:, 128 * me:128 * me + 128], sem)
+        lean[0] = LEAN["pw"]
+        for h in range(4):
+            p = bank()
+            c = 1 + 1024 * me + 256 * h
+            mm(V(p, 0, 256), V("E"), V(z, c, c + 256))
+            copy(V(pw, 8 + 256 * h, 264 + 256 * h), V(p, 0, 256))
+        lean[0] = 0.0
+        expect(land, 128, sem)
+
+    def spread(buf, q, win, at, parts):
+        w = 8 // parts
+        for h in range(parts):
+            p = bank()
+            mms([(V(p, 128 * b, 128 * b + 128), V("SEL", 128 * (w * h + b), 128 * (w * h + b) + 128),
+                  V(buf, 128 * q, 128 * q + 128), True, True) for b in range(w)])
+            copy(V(win, at + 128 * w * h, at + 128 * w * (h + 1)), V(p, 0, 128 * w))
+
+    addruns("w1", "flA", "offA", "zA", "scn")
+    zeros(V("fcr", 0, 2048))
+    reduce("zA", "LP", "p", "RT", "PT", "pw%d" % me)
+
+    def gather(q, lst, o, prev, own="pw%d" % me):
+        w, l = V(own if q == me else "pw%d" % q), V(lst, 32 * q, 32 * q + 32)
+        if prev is None:
+            pick(V(o), w, l)
+        else:
+            pick2(V(o), w, l, V(prev), OP.add)
+
+    zeros(V("fcr", 2048, 4096))
+    zeros(V("zB", 0, 2048))
+    for name in ("qw", "pw0", "pw1", "pw2", "pw3"):
+        fill(V(name, 0, 8), 0.0)
+    gather(me, "idx", "ac0", None)
+    lean[0] = LEAN["fas"]
+    pick(V("faS"), V("far"), V("La"))
+    lean[0] = 0.0
+    for n in (1, 2):
+        spread("LP", come[n], "pw%d" % come[n], 8, 4)
+        gather(come[n], "idx", "ac%d" % n, "ac%d" % (n - 1))
+    q = come[3]
+    spread("LP", q, "pw%d" % q, 8, 8)
+    for r in ring[:OWN] + [me] + ring[OWN:3]:
+        lo, hi = 128 * r, 128 * r + 128
+        lean[0] = LEAN["own"] if r == me else 0.0
+        pick2(V("ac3", lo, hi), V("pw%d" % q), V("idx", 32 * q + 8 * r, 32 * q + 8 * r + 8), V("ac2", lo, hi), OP.add)
+        tt(V("OT", lo, hi), V("ac3", lo, hi), V("faS", lo, hi), OP.mult)
+        if r != me:
+            send(r, V("OT", lo, hi), T["LA"][:, 128 * me:128 * me + 128], "n")
+    lean[0] = 0.0
+    expect("LA", 128, "n")
+    zeros(V("zB", 2048, 4104))
+
+    lean[0] = LEAN["lb"]
+    ts(V("nb"), V("txb"), 4096, OP.mult)
+    tt(V("nbi"), V("nb"), V("txa"), OP.add)
+    for k in range(16):
+        ts(("xe", k, k + 1, lambda k=k: T["xe"][:, k:512:16]), V("nbi"), V("E", k, k + 1), OP.mult)
+    p = bank()
+    mm(V(p), V("GRP"), V("xe"))
+    copy(V("xr"), V(p))
+    copy(V("jo"), V("tob"), "v")
+    for i in range(4):
+        pick2(V("mk", 128 * i, 128 * i + 128), V("xr"), V("jo", 8 * i, 8 * i + 8), V("E"), OP.mult)
+    tt(V("m2"), V("mk", 0, 512, 2), V("mk", 1, 512, 2), OP.add)
+    tt(V("m3"), V("m2", 0, 256, 2), V("m2", 1, 256, 2), OP.add)
+    tt(V("m4"), V("m3", 0, 128, 2), V("m3", 1, 128, 2), OP.add)
+    tt(V("nhi"), V("m4", 0, 64, 2), V("m4", 1, 64, 2), OP.add)
+    ts(V("nlo"), V("nhi"), 4095, OP.bitwise_and)
+    copy(V("ja"), V("nlo"), "v")
+    ts(V("nhi"), V("nhi"), 12, OP.arith_shift_right)
+    fill(V("ym"), 0.0)
+    ts(V("ym", 0, 32), V("nhi"), 1, OP.add)
+    runs("ym", "sb", "tb", "snB", "offB", "flB")
+    lean[0] = LEAN["vco"]
+    pick(V("vco"), V("vc"), V("jo"))
+    lean[0] = LEAN["ib"]
+    places("tlb", "pib", "be", "bf", "bg", "pij")
+    put(V("fcr"), V("pib"), V("ssrc"))
+    lists("fcr", list(range(32)), "invb")
+
+    lean[0] = LEAN["ya"]
+    gather(me, "inva", "ya0", None)
+    for n in (1, 2, 3):
+        gather(come[n], "inva", "ya%d" % n, "ya%d" % (n - 1))
+    tt(V("yo"), V("ya3"), V("fag"), OP.mult)
+    dmas("dya", [("y", H(T.ya[:, 512 * b:512 * b + 512]), group("yo", b)) for b in range(8)], 262144)
+    lean[0] = 0.0
+
+    spread("OT", me, "Aw", 1024 * me, 4)
+    for n in (1, 2, 3):
+        spread("LA", come[n], "Aw", 1024 * come[n], 4)
+    pick2(V("w2"), V("Aw"), V("ja"), V("vco"), OP.mult)
+    addruns("w2", "flB", "offB", "zB", "scm")
+    reduce("zB", "LQ", "q", "RU", "PU", "qw")
+
+    gather(me, "invb", "ac0", None, "qw")
+    for n in (1, 2, 3):
+        q = come[n]
+        spread("LQ", q, "pw%d" % q, 8, 4)
+        gather(q, "invb", "ac%d" % n, "ac%d" % (n - 1))
+    dmas("dyb", [("ys"[b % 2], H(T.yb[:, 512 * b:512 * b + 512]), group("ac3", b)) for b in range(8)], 262144)
+
+    for i, e, at in order(ops):
+        where.update(at)
+        o = ops[i]
+        if o["kind"] == "c":
+            for outs, ins, call in o["subs"]:
+                emit(e, outs, ins, call)
+        elif o["kind"] == "dma":
+            emit_dmas(*o["subs"])
+        elif o["kind"] == "send":
+            emit_send(*o["subs"])
+        else:
+            emit_come(*o["subs"])
+    for sem, n in count.items():
+        if waited.get(sem, 0) < n:
+            g.wait_ge(T.sem[sem], n)

@@ -1,25 +1,24 @@
-from concourse.mybir import AluOpType, ActivationFunctionType
+from concourse.mybir import AluOpType, ActivationFunctionType, AxisListType
 
 OP = AluOpType
 COPY = ActivationFunctionType.Copy
 IDENTITY = ActivationFunctionType.Identity
 ZW = 4728
-DC = 2048
 OWN = 2
 SIZES = {
-    "int32": {128: "Di Ei Gi Gs", 32: "tla tlb txa txb txc tob"},
+    "int32": {128: "Di Ei", 32: "tla tlb tlc txa txb txc tob", 512: "Tab"},
     "uint16": {256: "Lr"},
-    "bfloat16": {128: "E16", 512: "a1 a2 s1 s2 ssrc fag", 1024: "SELB CB LCB", 4096: "fcr fbr far Cw Bw W R fb16",
-                 4096 - DC: "fc16"},
-    "float32": {128: "E ident GRP vsel N1 N2 m3", 256: "m2", 520: "flA flB",
-                512: "X v8 vex vc vco xe xr mk w1 w2 scn scm RT PT RU PU LP OT LA LQ faS ac0 ac1 ac2 ac3 ya0 ya1 ya2 ya3 yo",
-                1024: "SEL", 1032: "pw0 pw1 pw2 pw3 qw", 4096: "Aw", ZW: "zA zB"},
+    "bfloat16": {128: "E32", 512: "ramp ssA ssB fag", 1024: "SELB CB LCB", 4096: "fcb FR far Cw Bw W R"},
+    "float32": {128: "E vsel N1 N2", 520: "flA flB",
+                512: "v8 vex vc vco w1 w2 scn scm PT PU LP OT LA LQ faS ac0 ac1 ac2 ac3 ya0 ya1 ya2 ya3 yo G yb0 yb1 yb2 yb3",
+                1024: "SEL", 1032: "pw0 pw1 pw2 pw3 qw0 qw1 qw2 qw3", 4096: "Aw", ZW: "zA zB"},
 }
 SMALL = {
-    "int32": {4: "kri krs", 8: "kgi kgs k1 p15 hk", 32: "ba bb bd pii be bf bg pij nb nbi nhi nlo", 128: "vsi vss"},
-    "uint16": {32: "La Lb Lc ja jb jc jo pia pib snA snB offA offB", 128: "idx inva invb"},
-    "bfloat16": {4: "rsel"},
-    "float32": {4: "rm4", 8: "rm8 m0 m1 n0 hm hf hb w01", 32: "trash pif sa ta sb tb", 40: "yl ym", 64: "m4"},
+    "int32": {8: "kgi kgs", 32: "ba bb bd pii be bf bg pij ca cb cc da db dc oa oc od nA nB nx", 128: "vsi vss"},
+    "uint16": {32: "La ja jb jc jo jq pia pib snA snB offA offB", 64: "L2", 128: "idx inva invb"},
+    "bfloat16": {8: "rsA rsB"},
+    "float32": {4: "rm4 hf n0 b1 b2 b3 bA bB c0 c1", 8: "rm8 w01", 32: "trash pif sa ta sb tb cd ce dd de ny nz",
+                40: "yl ym", 64: "F"},
 }
 SCRATCH = {n: ("sbuf", [128, c], d) for d, x in SIZES.items() for c, names in x.items() for n in names.split()}
 PLACE = {}
@@ -30,21 +29,23 @@ for _d, _x in SMALL.items():
             PLACE[_n] = ("small_" + _d, _at, _c)
             _at += -(-_c // 16) * 16
     SCRATCH["small_" + _d] = ("sbuf", [128, _at], _d)
-for _t in ("la", "lb", "lc"):
-    SCRATCH["u" + _t] = ("sbuf", [128, 4, 8], "int32")
-    SCRATCH["tm" + _t[1]] = ("sbuf", [128, 4, 4, 8], "float32")
+SCRATCH["tm"] = ("sbuf", [128, 4, 4, 2, 8], "float32")
+SCRATCH["T4"] = ("sbuf", [128, 16, 2, 16], "float32")
+SCRATCH["T1"] = ("sbuf", [128, 2, 2, 16], "float32")
 for _b in range(8):
     SCRATCH["pb%d" % _b] = ("psum", [128, 512], "float32")
 ENG = {"v": "sv", "s": "ss", "t": "st", "g": "sg"}
-SEMAPHORES = (list(ENG.values()) + ["dt" + t for t in ("la", "lb", "xa", "xb", "xc", "ob")] + ["du" + t for t in ("la", "lb", "lc")]
-              + ["dv", "dfb", "dfc", "dfe", "dfa", "dfg", "dya", "dyb", "ls"]
-              + ["%s%d" % (k, d) for k in "cpnq" for d in (1, 2, 3)])
-CYCLE, GATHER, SCATTER, WAKE, PE = 0.000913, 1.5, 3.2, 0.06, 0.5
+SEMAPHORES = (list(ENG.values()) + ["dt" + t for t in ("la", "lb", "lc", "xa", "xb", "xc", "ob")]
+              + ["df%d" % i for i in range(4)] + ["dv", "dfa", "dfe", "dfg", "dtab", "dya", "dyb0", "dyb1"]
+              + ["l" + k for k in "cpnq"] + ["%s%d" % (k, d) for k in "cpnq" for d in (1, 2, 3)])
+CYCLE, GATHER, SCATTER, WAKE, PE = 0.00087, 1.5, 3.2, 0.06, 0.5
 ISSUE, FIRST, HOP, RATE = 0.45, 1.0, 1.3, 55e3
 DMA_ISSUE, DMA_TIME, DMA_RATE = 0.07, 1.6, 180e3
 BYTES = {"float32": 4, "int32": 4, "bfloat16": 2, "uint16": 2}
-LEAN = {"list": 8.5, "inv": 5.0, "r": 0.6, "lb": 3.5, "vco": 2.0, "ib": 0.0, "ya": 0.0, "fas": 5.0, "own": 7.3, "wf": 0.0,
-        "ss": -2.5, "jc": -1.5, "vex": 0.0, "pw": 6.0, "red": 12.0}
+LEAN = {"list": -2.0, "inv": 0.0, "r": 0.0, "lb": 0.0, "vco": 0.0, "ib": 0.0, "ya": -1.0, "fas": 0.0, "own": 0.0, "wf": 5.0,
+        "ss": 0.0, "jc": 0.0, "vex": -4.0, "pw": 1.0, "red": 0.0, "sel": 1.0, "l2": 0.0}
+FULL = {"p": (0, 0, 0, 0), "n": (4, 0, 0, 0), "q": (0, 0, 0, 0)}
+ZB1 = 1536
 
 
 def op_time(op):
@@ -56,6 +57,14 @@ def op_time(op):
     return t
 
 
+def meet(a, b):
+    return a[1] < b[2] and b[1] < a[2] and a[3] < b[4] and b[3] < a[4]
+
+
+def covers(a, b):
+    return a[1] <= b[1] and b[2] <= a[2] and a[3] <= b[3] and b[4] <= a[4]
+
+
 def order(ops):
     n = len(ops)
     pred = [set(op["after"]) for op in ops]
@@ -63,14 +72,18 @@ def order(ops):
     for i, op in enumerate(ops):
         both = [(v, True) for v in op["outs"] if v[0]] + [(v, False) for v in op["ins"] if v[0]]
         for v, w in both:
-            for lo, hi, w2, j in last.setdefault(v[0], []):
-                if j != i and lo < v[2] and v[1] < hi and (w or w2):
+            for r, w2, j in last.setdefault(v[0], []):
+                if j != i and (w or w2) and meet(v, r):
                     pred[i].add(j)
         for v, w in both:
             rec = last[v[0]]
             if w:
-                rec[:] = [r for r in rec if not (v[1] <= r[0] and r[1] <= v[2])]
-            rec.append((v[1], v[2], w, i))
+                rec[:] = [x for x in rec if not covers(v, x[0])]
+            rec.append((v, w, i))
+    chain = {}
+    for i, op in enumerate(ops):
+        if op["eng"] in "gy":
+            chain.setdefault(op["eng"], []).append(i)
     succ = [[] for _ in ops]
     for i in range(n):
         for j in pred[i]:
@@ -80,20 +93,20 @@ def order(ops):
         for b in op["banks"]:
             users[b] = users.get(b, 0) + 1
     prio = [0.0] * n
+    behind = {a: b for c in chain.values() for a, b in zip(c, c[1:])}
     for i in reversed(range(n)):
         prio[i] = op_time(ops[i]) + max([prio[k] + WAKE for k in succ[i]] or [0.0])
+        if i in behind:
+            prio[i] = max(prio[i], min(ops[i]["cost"].values()) + prio[behind[i]])
     prio = [prio[i] + ops[i]["lean"] for i in range(n)]
     free = {q: 0.0 for q in "vstgy"}
     end = [None] * n
     bank_of, bank_free = {}, {b: 0.0 for b in range(8)}
+    bank_busy = {}
     port, dma, first = 0.0, 0.0, True
     out = []
     ready = [i for i in range(n) if not pred[i]]
     missing = [len(p) for p in pred]
-    chain = {}
-    for i, op in enumerate(ops):
-        if op["eng"] in "gy":
-            chain.setdefault(op["eng"], []).append(i)
     while ready:
         cand = []
         for i in ready:
@@ -101,6 +114,7 @@ def order(ops):
             if op["eng"] in chain and chain[op["eng"]][0] != i:
                 continue
             st = max([end[j] + WAKE for j in pred[i]] or [0.0])
+            st = max([st] + [bank_busy.get(b, 0.0) for b in op["banks"]])
             bank = None
             if op["eng"] == "t" and op["banks"] and op["banks"][0] not in bank_of:
                 idle = [b for b in bank_free if bank_free[b] is not None]
@@ -143,6 +157,7 @@ def order(ops):
             port = max(port, f1) + op["bytes"] / RATE
             end[i] = port + HOP
         for b in op["banks"]:
+            bank_busy[b] = f1 + WAKE
             users[b] -= 1
             if not users[b]:
                 bank_free[bank_of[b]] = f1 + WAKE
@@ -184,27 +199,27 @@ def rank_program(g, core, T, topo):
         know[e][sem] = val
 
     def before(e, outs, ins):
-        for (n, lo, hi, _), w in [(x, True) for x in outs] + [(x, False) for x in ins]:
-            n = where.get(n, n)
+        for v, w in [(x, True) for x in outs] + [(x, False) for x in ins]:
+            n = where.get(v[0], v[0])
             if n in banks:
                 for e2 in list(banks[n]):
                     if e2 != e:
                         wait(e, banks[n].pop(e2))
                 continue
-            for lo2, hi2, w2, tok in seen.get(n, []):
-                if lo2 < hi and lo < hi2 and (w or w2):
+            for r, w2, tok in seen.get(n, []):
+                if (w or w2) and meet(v, r):
                     wait(e, tok)
 
     def after(outs, ins, tok):
-        for (n, lo, hi, _), w in [(x, True) for x in outs] + [(x, False) for x in ins]:
-            n = where.get(n, n)
+        for v, w in [(x, True) for x in outs] + [(x, False) for x in ins]:
+            n = where.get(v[0], v[0])
             if n in banks:
                 banks[n][tok[2]] = tok
                 continue
             old = seen.setdefault(n, [])
             if w:
-                old[:] = [r for r in old if not (lo <= r[0] and r[1] <= hi)]
-            old.append((lo, hi, w, tok))
+                old[:] = [x for x in old if not covers(v, x[0])]
+            old.append((v, w, tok))
 
     def emit(e, outs, ins, call):
         before(e, outs, ins)
@@ -214,33 +229,27 @@ def rank_program(g, core, T, topo):
         after(outs, ins, (sem, count[sem], e, dict(know[e])))
 
     def emit_dmas(sem, items, extra):
-        before(items[0][0], [], extra)
         kn = {}
         for e, o, i in items:
-            before(e, [o] if o[0] else [], [i] if i[0] else [])
-            queue[e].dma_start(out=o[3](), in_=i[3]()).then_inc(T.sem[sem], 16)
+            before(e, [o] if o[0] else [], ([i] if i[0] else []) + extra)
+            queue[e].dma_start(out=o[5](), in_=i[5]()).then_inc(T.sem[sem], 16)
             count[sem] = count.get(sem, 0) + 16
             for k2, v2 in know[e].items():
                 kn[k2] = max(kn.get(k2, 0), v2)
         tok = (sem, count[sem], "d", kn)
-        done = []
         for e, o, i in items:
-            if o[0] and o[:3] not in done:
-                done.append(o[:3])
-                after([o], [], tok)
-            if i[0]:
-                after([], [i], tok)
+            after([o] if o[0] else [], [i] if i[0] else [], tok)
 
     def emit_send(q, src, dst, sem):
         to = T.cores[q]
         before("g", [], [src])
         rid, pid, _ = topo.addr(to)
-        g.remote_dma(out_ap=dst, in_ap=src[3](), remote_sem=T.sem["%s%d" % (sem, (q - me) % N)], local_sem=T.sem["ls"],
+        g.remote_dma(out_ap=dst, in_ap=src[5](), remote_sem=T.sem["%s%d" % (sem, (q - me) % N)], local_sem=T.sem["l" + sem],
                      pid=pid, routing_id=rid, dma_engine_mask=topo.mask(core, to))
-        count["ls"] = count.get("ls", 0) + len(topo.engines(core, to))
+        count["l" + sem] = count.get("l" + sem, 0) + len(topo.engines(core, to))
 
-    def emit_come(v, s, q):
-        count[s] = len(topo.engines(T.cores[q], core))
+    def emit_come(v, s, n):
+        count[s] = n or count[s]
         after([v], [], (s, count[s], "r", {}))
 
     def V(name, lo=0, hi=None, step=1, p0=0, p1=128):
@@ -255,13 +264,19 @@ def rank_program(g, core, T, topo):
         def ap():
             t = T[where.get(name, name)]
             return t[p0:p1, lo:hi] if step == 1 else t[p0:p1, lo:hi:step]
-        return (name, lo, hi, ap)
+        return (name, lo, hi, p0, p1, ap, len(range(lo, hi, step)))
+
+    def X(name, ap, n):
+        return (name, 0, 1, 0, 128, ap, n)
 
     def H(ap):
-        return (None, 0, 0, lambda: ap)
+        return (None, 0, 0, 0, 0, lambda: ap, 0)
 
     def group(name, b, lo=0, hi=None):
         return V(name, lo, hi, p0=16 * b, p1=16 * b + 16)
+
+    def col(name, j=0, p0=0, p1=128):
+        return V(name, j, j + 1, p0=p0, p1=p1)
 
     def bank():
         turn[0] += 1
@@ -276,9 +291,6 @@ def rank_program(g, core, T, topo):
                     "banks": names, "after": list(needs), "lean": lean[0]})
         return len(ops) - 1
 
-    def size(v):
-        return v[2] - v[1]
-
     def narrow(*vs):
         return all(v[0][0] != "#" and BYTES[SCRATCH[v[0]][2]] == 2 for v in vs)
 
@@ -288,191 +300,192 @@ def rank_program(g, core, T, topo):
     def one(eng, outs, ins, call, cost):
         op(eng, outs, ins, [(outs, ins, call)], cost)
 
+    def copies(pairs, e="vs"):
+        subs, cost = [], {"v": 0.0, "s": 0.0}
+        for o, i in pairs:
+            subs.append(([o], [i], lambda q, x, o=o, i=i: q.tensor_copy(o[5](), i[5]()) if x == "v"
+                         else q.activation(o[5](), i[5](), COPY)))
+            cost["v"] += cyc(o[6] * 0.5 if narrow(o, i) else o[6])
+            cost["s"] += cyc(o[6])
+        op(e, [o for o, _ in pairs], [i for _, i in pairs], subs, cost)
+
     def copy(o, i, e="vs"):
-        n = size(o)
-        cost = {"v": cyc(n * 0.5 if narrow(o, i) else n), "s": cyc(n)}
-        one(e, [o], [i], lambda q, x: q.tensor_copy(o[3](), i[3]()) if x == "v" else q.activation(o[3](), i[3](), COPY), cost)
+        copies([(o, i)], e)
 
-    def scaled(o, i, sc, b=None):
-        if b is None:
-            one("s", [o], [i, sc], lambda q, x: q.activation(o[3](), i[3](), COPY, scale=sc[3]()), {"s": cyc(size(o))})
-        else:
-            one("s", [o], [i, sc, b], lambda q, x: q.activation(o[3](), i[3](), IDENTITY, bias=b[3](), scale=sc[3]()),
-                {"s": cyc(size(o))})
+    def scaled(o, i, sc, b=None, e="vs"):
+        def call(q, x):
+            if x == "v":
+                if b is None:
+                    return q.tensor_scalar(o[5](), i[5](), sc[5](), None, OP.mult)
+                return q.tensor_scalar(o[5](), i[5](), sc[5](), b[5](), OP.mult, OP.add)
+            if b is None:
+                return q.activation(o[5](), i[5](), COPY, scale=sc[5]())
+            return q.activation(o[5](), i[5](), IDENTITY, bias=b[5](), scale=sc[5]())
+        one(e, [o], [i, sc] + ([b] if b else []), call, {"v": cyc(o[6]), "s": cyc(o[6])})
 
-    def ts(o, i, s1, op0, s2=None, op1=None, n=None):
+    def ts(o, i, s1, op0, s2=None, op1=None):
         rd = [i] + [s for s in (s1, s2) if isinstance(s, tuple)]
 
         def call(q, x):
-            a1 = s1[3]() if isinstance(s1, tuple) else s1
-            a2 = s2[3]() if isinstance(s2, tuple) else s2
+            a1 = s1[5]() if isinstance(s1, tuple) else s1
+            a2 = s2[5]() if isinstance(s2, tuple) else s2
             if op1 is None:
-                return q.tensor_scalar(o[3](), i[3](), a1, None, op0)
-            return q.tensor_scalar(o[3](), i[3](), a1, a2, op0, op1)
-        one("v", [o], rd, call, {"v": cyc(size(i))})
+                return q.tensor_scalar(o[5](), i[5](), a1, None, op0)
+            return q.tensor_scalar(o[5](), i[5](), a1, a2, op0, op1)
+        one("v", [o], rd, call, {"v": cyc(i[6])})
 
     def tt(o, a, b, f):
-        n = size(a) * (1 if a[0][0] == "#" or b[0][0] == "#" else 2)
-        one("v", [o], [a, b], lambda q, x: q.tensor_tensor(o[3](), a[3](), b[3](), f), {"v": cyc(n)})
+        n = a[6] * (1 if a[0][0] == "#" or b[0][0] == "#" else 2)
+        one("v", [o], [a, b], lambda q, x: q.tensor_tensor(o[5](), a[5](), b[5](), f), {"v": cyc(n)})
+
+    def turned(o, i):
+        one("v", [o], [i], lambda q, x: q.transpose(o[5](), i[5]()), {"v": cyc(i[6])})
 
     def fill(o, c):
-        one("v", [o], [], lambda q, x: q.memset(o[3](), c), {"v": cyc(size(o) * (0.5 if narrow(o) else 1))})
+        one("v", [o], [], lambda q, x: q.memset(o[5](), c), {"v": cyc(o[6] * (0.5 if narrow(o) else 1))})
 
     def ind(w, l):
-        return w[3]().indirect(l[3]())
+        return w[5]().indirect(l[5]())
 
     def pick(o, w, l, e="vs"):
-        n = size(l) * 16 * GATHER * CYCLE
-        one(e, [o], [w, l], lambda q, x: q.tensor_copy(o[3](), ind(w, l)) if x == "v" else q.activation(o[3](), ind(w, l), COPY),
+        n = l[6] * 16 * GATHER * CYCLE
+        one(e, [o], [w, l], lambda q, x: q.tensor_copy(o[5](), ind(w, l)) if x == "v" else q.activation(o[5](), ind(w, l), COPY),
             {"v": n + 0.05, "s": n + 0.065})
 
     def pick2(o, w, l, b, f):
-        one("v", [o], [w, l, b], lambda q, x: q.tensor_tensor(o[3](), ind(w, l), b[3](), f),
-            {"v": size(l) * 16 * GATHER * CYCLE + 0.05})
+        one("v", [o], [w, l, b], lambda q, x: q.tensor_tensor(o[5](), ind(w, l), b[5](), f),
+            {"v": l[6] * 16 * GATHER * CYCLE + 0.05})
 
     def put(w, l, i):
-        one("v", [w], [l, i], lambda q, x: q.tensor_copy(ind(w, l), i[3]()), {"v": size(l) * 16 * SCATTER * CYCLE + 0.05})
+        one("v", [w], [l, i], lambda q, x: q.tensor_copy(ind(w, l), i[5]()), {"v": l[6] * 16 * SCATTER * CYCLE + 0.05})
 
     def mms(items):
         outs, ins, subs, cost = [], [], [], 0.0
         for o, l, r, a, z in items:
             outs.append(o)
             ins += [l, r]
-            subs.append(([o], [l, r], lambda q, x, o=o, l=l, r=r, a=a, z=z: q.matmul(o[3](), l[3](), r[3](), a, z)))
-            cost += max(64, size(r)) * (1 if narrow(l) else 4) * PE * CYCLE
+            subs.append(([o], [l, r], lambda q, x, o=o, l=l, r=r, a=a, z=z: q.matmul(o[5](), l[5](), r[5](), a, z)))
+            cost += max(64, r[6]) * (1 if narrow(l) else 4) * PE * CYCLE
         op("t", outs, ins, subs, {"t": cost})
 
     def mm(o, l, r):
         mms([(o, l, r, True, True)])
 
-    def iota(o, pattern, base, cm, small=False):
-        if small:
-            call = lambda q, x: q.iota(o[3](), pattern, base, cm, allow_small_or_imprecise_dtypes=True)
+    def iota(o, pattern, base, cm):
+        if SCRATCH[o[0]][2] == "int32":
+            call = lambda q, x: q.iota(o[5](), pattern, base, cm)
         else:
-            call = lambda q, x: q.iota(o[3](), pattern, base, cm)
-        one("g", [o], [], call, {"g": 0.13 + 2 * size(o) * CYCLE})
+            call = lambda q, x: q.iota(o[5](), pattern, base, cm, allow_small_or_imprecise_dtypes=True)
+        one("g", [o], [], call, {"g": 0.13 + 2 * o[6] * CYCLE})
 
     def zeros(o):
-        iota(o, [[0, size(o)]], 0, 0, True)
+        iota(o, [[0, o[6]]], 0, 0)
 
     def dmas(sem, items, nbytes, extra=()):
         e = items[0][0]
-        outs, ins = [], list(extra)
-        for _, o, i in items:
-            outs += [o] if o[0] and o[:3] not in [x[:3] for x in outs] else []
-            ins += [i] if i[0] else []
-        op(e, outs, ins, (sem, items, list(extra)), {e: DMA_ISSUE * len(items)}, "dma", nbytes)
+        outs = [o for _, o, _ in items if o[0]]
+        ins = list(extra) + [i for _, _, i in items if i[0]]
+        op(e, outs, ins, (sem, items, list(extra)), {e: DMA_ISSUE * len([1 for x in items if x[0] == e])}, "dma", nbytes)
 
     def send(q, src, dst, sem):
         sent[sem, (q - me) % N] = op("g", [], [src], (q, src, dst, sem), {"g": ISSUE}, "send",
-                                     128 * size(src) * BYTES[SCRATCH[src[0]][2]])
+                                     128 * src[6] * BYTES[SCRATCH[src[0]][2]])
 
     def expect(buf, width, sem):
         for d in (1, 2, 3):
             q, s = (me - d) % N, "%s%d" % (sem, d)
             v = V(buf, q * width, (q + 1) * width)
-            op("-", [v], [], (v, s, q), {}, "come", 0, [sent[sem, d]])
+            op("-", [v], [], (v, s, len(topo.engines(T.cores[q], core))), {}, "come", 0, [sent[sem, d]])
+
+    def left(sem):
+        v = ("left" + sem, 0, 1, 0, 128, None, 1)
+        op("-", [v], [], (v, "l" + sem, 0), {}, "come", 0, [sent[sem, d] for d in (1, 2, 3)])
+        return v
 
     ring = [(me + d) % N for d in (1, 2, 3, 0)]
     come = [(me - d) % N for d in (0, 1, 2, 3)]
-
-    def U(t):
-        return ("u" + t, 0, 32, lambda: T["u" + t][:, :, :])
+    low, high = {"p0": 0, "p1": 64}, {"p0": 64, "p1": 128}
 
     def table(t, e):
         dmas("dt" + t, [(e, V("t" + t), H(T[t][:, :]))], 16384)
 
-    def table3(t, e):
-        dmas("du" + t, [(e, U(t), H(T[t][:, :]))], 16384)
-
-    table3("lc", "y")
-    dmas("dfb", [("s", V("fb16", p0=0, p1=16), H(T.fb[:, :]))], 131072)
-    dmas("dfe", [("y", V("fc16", p0=0, p1=16), H(T.fc[:, DC:4096]))], 65536)
-    table3("lb", "s")
-    dmas("dfc", [("y", group("fcr", b, 0, DC), H(T.fc[:, 0:DC])) for b in range(8)], 16 * DC * 2 * 8)
-    table("la", "y")
-    table("xa", "y")
-    table3("la", "y")
-    dmas("dv", [("y", V("v8", p0=0, p1=8), H(T.v[:, :]))], 16384)
-    for t in ("xc", "xb", "ob", "lb"):
+    for i in range(4):
+        lo, hi = 1024 * i, 1024 * i + 1024
+        dmas("df%d" % i, [("y", V("fcb", lo, hi, p0=0, p1=16), H(T.fc[:, lo:hi])),
+                          ("y", V("fcb", lo, hi, p0=16, p1=32), H(T.fb[:, lo:hi]))], 65536)
+    table("lc", "s")
+    table("lb", "s")
+    for t in ("la", "xa"):
         table(t, "y")
+    dmas("dv", [("y", V("v8", p0=0, p1=8), H(T.v[:, :]))], 16384)
+    for t in ("xc", "xb", "ob"):
+        table(t, "y")
+    dmas("dfa", [("y", group("far", b), H(T.fa[:, :])) for b in range(3)], 3 << 17)
 
     iota(V("Di"), [[-1, 128]], 128, 1)
-    iota(V("k1"), [[0, 8]], 0, 1)
-    iota(V("kri"), [[-32, 4]], 0, 1)
     iota(V("kgi"), [[-16, 8]], 0, 1)
-    iota(V("trash"), [[16, 32]], 4097, 1, True)
-    iota(V("w01"), [[1, 8]], 0, 0, True)
+    iota(V("trash"), [[16, 32]], 4097, 1)
+    iota(V("w01"), [[1, 8]], 0, 0)
     iota(V("vsi", p1=8), [[1, 128]], 0, -16)
-    iota(V("Gi"), [[-16, 8], [0, 16]], 0, 1)
-    iota(V("a1"), [[128, 4], [0, 128]], 0, 0, True)
-    iota(V("a2"), [[0, 4], [1, 128]], 8, 0, True)
+    iota(V("ramp"), [[1, 512]], -256, 0)
+    zeros(V("Tab"))
+    rows = [("Tab", 0, 512, 0, 128, lambda f=f: T["Tab"][f:128:16, :], 512) for f in (0, 1)]
+    dmas("dtab", [("y", rows[0], H(T.xa[:, :])), ("y", rows[1], H(T.xb[:, :]))], 32768)
 
-    fill(V("X"), 0.0)
     ts(V("Ei"), V("Di"), 15, OP.bitwise_and)
-    ts(V("hk"), V("k1"), 4, OP.arith_shift_right, 1, OP.bitwise_and)
-    ts(V("p15"), V("k1"), 15, OP.bitwise_and)
-    ts(V("krs"), V("kri"), 5, OP.arith_shift_right)
     ts(V("kgs"), V("kgi"), 4, OP.arith_shift_right)
-    ts(V("E16"), V("Ei"), 0, OP.is_equal)
     ts(V("E"), V("Ei"), 0, OP.is_equal)
-    ts(V("hf"), V("hk"), 1, OP.mult)
-    ts(V("m0"), V("p15"), 0, OP.is_equal)
-    ts(V("m1"), V("p15"), 1, OP.is_equal)
-    ts(V("hb"), V("hf"), 512.0, OP.mult, V("m0", 0, 1), OP.mult)
-    ts(V("rm4"), V("krs"), 0, OP.is_equal)
-    ts(V("hm"), V("hk"), 0, OP.is_equal)
-    for b in range(8):
-        ts(V("X", 128 * (b % 4) + 16 * b, 128 * (b % 4) + 16 * b + 16), V("E", 0, 16),
-           V("hm" if b < 4 else "hf", 0, 1), OP.mult)
     ts(V("rm8"), V("kgs"), 0, OP.is_equal)
-    ts(V("n0"), V("p15"), 0, OP.not_equal)
-    ts(V("N1"), V("Di"), 129, OP.is_equal, V("n0", 0, 1), OP.mult)
-    ts(V("N2"), V("Di"), 113, OP.is_equal, V("m0", 0, 1), OP.mult)
-    ts(V("ident"), V("Di"), 128, OP.is_equal)
-    ts(V("rsel"), V("krs"), 0, OP.is_equal)
-    ts(V("Gs"), V("Gi"), 4, OP.arith_shift_right)
-    ts(V("GRP"), V("Gs"), 0, OP.is_equal)
+    for f in (0, 1):
+        ts(V("E32", 64 * f, 64 * f + 64), V("E", 0, 64), col("rm8", f), OP.mult)
+    tt(V("rm4"), V("rm8", 0, 8, 2), V("rm8", 1, 8, 2), OP.add)
+    one("v", [col("hf")], [V("rm8")], lambda q, x: q.tensor_reduce(col("hf")[5](), V("rm8", 1, 8, 2)[5](), AxisListType.X, OP.add),
+        {"v": cyc(4)})
+    ts(col("n0"), col("E", 0), 0, OP.is_equal)
+    ts(V("N1"), V("Di"), 129, OP.is_equal, col("n0"), OP.mult)
+    ts(V("N2"), V("Di"), 113, OP.is_equal, col("E", 0), OP.mult)
     ts(V("vss", p1=8), V("vsi", p1=8), 4, OP.arith_shift_right)
     ts(V("vsel", p1=8), V("vss", p1=8), 0, OP.is_equal)
 
-    def tiles_list(t, dst):
-        tm, u = "tm" + t[1], U(t)
-        for r in range(4):
-            ts((tm, r, r + 1, lambda r=r: T[tm][:, :, r, :]), u, V("rm4", r, r + 1), OP.mult)
-        p = bank()
-        mms([(V(p, 0, 32), V("X", 128 * b, 128 * b + 128), (tm, 0, 4, lambda b=b: T[tm][:, b, :, :]), b == 0, b == 3)
-             for b in range(4)])
-        copy(V(dst), V(p, 0, 32), "v")
-
-    tiles_list("lc", "Lc")
-    tiles_list("lb", "Lb")
     for i in range(8):
-        for src, dst, lo in (("fc16", "fcr", DC), ("fb16", "fbr", 0)):
-            if 512 * i >= lo:
-                p = bank()
-                mm(V(p), V("E16", p1=16), V(src, 512 * i - lo, 512 * i - lo + 512, p1=16))
-                copy(V(dst, 512 * i, 512 * i + 512), V(p))
+        p = bank()
+        mm(V(p), V("E32", p1=32), V("fcb", 512 * i, 512 * i + 512, p1=32))
+        copy(V("FR", 512 * i, 512 * i + 512), V(p))
+
+    def quarter(name, a, lo, hi):
+        return V(name, lo, hi, p0=32 * a, p1=32 * a + 32)
 
     for r in ring:
-        pick(V("CB", 256 * r, 256 * r + 128), V("fcr"), V("Lc", 8 * r, 8 * r + 8))
-        pick(V("CB", 256 * r + 128, 256 * r + 256), V("fbr"), V("Lb", 8 * r, 8 * r + 8))
+        lean[0] = LEAN["l2"]
+        copies([(quarter("L2", a, 16 * r, 16 * r + 16), quarter("tl" + "cb"[a // 2], r, 16 * (a % 2), 16 * (a % 2) + 16))
+                for a in range(4)], "v")
+        lean[0] = 0.0
+        pick(V("CB", 256 * r, 256 * r + 256), V("FR"), V("L2", 16 * r, 16 * r + 16))
         if r != me:
             send(r, V("CB", 256 * r, 256 * r + 256), T["LCB"][:, 256 * me:256 * me + 256], "c")
     expect("LCB", 256, "c")
     for i in range(4):
         zeros(V("zA", 1026 * i, 1026 * i + 1026))
 
-    dmas("dfa", [("y", group("far", b), H(T.fa[:, :])) for b in range(8)], 1 << 20, [V("LCB")])
+    dmas("dfe", [("y", group("far", b), H(T.fa[:, :])) for b in range(3, 8)], 5 << 17, [left("c")])
     dmas("dfg", [("y", group("fag", b), H(T.fa[:, 512 * b:512 * b + 512])) for b in range(8)], 131072)
 
-    for name in ("SELB", "SEL"):
-        for b in range(8):
-            scaled(V(name, 128 * b, 128 * b + 128), V("E"), V("rm8", b, b + 1))
+    lean[0] = LEAN["sel"]
+    for b in range(8):
+        scaled(V("SELB", 128 * b, 128 * b + 128), V("E"), col("rm8", b))
+    for b in range(8):
+        for h in (0, 1):
+            scaled(V("SEL", 128 * b + 64 * h, 128 * b + 64 * h + 64), V("E", 0, 64), col("rm8", (b + 4 * h) % 8))
     lean[0] = LEAN["ss"]
-    scaled(V("s1"), V("a1"), V("m0", 0, 1), V("hb", 0, 1))
-    scaled(V("s2"), V("a2"), V("m1", 0, 1))
-    tt(V("ssrc"), V("s1"), V("s2"), OP.add)
+    ts(col("b1"), col("hf"), 512.0, OP.mult, 264.0, OP.add)
+    ts(col("b2"), col("hf"), -512.0, OP.mult, 776.0, OP.add)
+    for name, o in (("A", 0), ("B", 4)):
+        ts(col("b3"), col("b1"), col("E", o + 1), OP.mult)
+        ts(col("b" + name), col("b2"), col("E", o + 2), OP.mult, col("b3"), OP.add)
+        scaled(V("ss" + name), V("ramp"), col("E", o), col("b" + name))
+        for h in (0, 1):
+            ts(col("c%d" % h), col("E", o), col("E", o + 1 + h), OP.add)
+            ts(V("rs" + name, 4 * h, 4 * h + 4), V("rm4"), col("c%d" % h), OP.mult)
 
     def places(t, dst, a, b, d, e):
         ts(V(a), V(t), 0x1F0, OP.bitwise_and)
@@ -483,7 +496,15 @@ def rank_program(g, core, T, topo):
         tt(V(e), V(b), V(d), OP.add)
         copy(V(dst), V(e), "v")
 
-    def runs(yl, sn, tr, snu, off, fl):
+    def runs(x, w, yl, sn, tr, snu, off, fl):
+        a, b, c, d, e = w.split()
+        fill(V(yl, 32, 40), 0.0)
+        ts(V(a), V(x), 0xC9F, OP.bitwise_and)
+        ts(V(b), V(x), 3, OP.arith_shift_right, 0x60, OP.bitwise_and)
+        ts(V(c), V(x), 0x60, OP.bitwise_and)
+        ts(V(d), V(c), 8, OP.mult, 1, OP.add)
+        tt(V(e), V(a), V(b), OP.add)
+        tt(V(yl, 0, 32), V(e), V(d), OP.add)
         p = bank()
         mms([(V(p, 0, 32), V("N1"), V(yl, 0, 32), True, False), (V(p, 0, 32), V("N2"), V(yl, 1, 33), False, True)])
         tt(V(sn), V(p, 0, 32), V(yl, 0, 32), OP.is_equal)
@@ -494,25 +515,23 @@ def rank_program(g, core, T, topo):
         fill(V(fl, 0, 8), 0.0)
         pick(V(fl, 8, 520), V("w01"), V(snu))
 
-    def lists(src, col, dst):
+    def lists(src, at, rs, dst):
         p = bank()
-        mms([(V(p, 4 * k, 4 * k + 4), V(src, 128 * col[k], 128 * col[k] + 128), V("rsel"), True, True) for k in range(32)])
-        for r in range(4):
-            copy(V(dst, 32 * r, 32 * r + 32), V(p, r, 128, 4), "v")
+        mms([(V(p, k, 256, 32), V(src, 128 * at[k], 128 * at[k] + 128), V(rs), True, True) for k in range(32)])
+        copies([(V(dst, **low), V(p, 0, 128, **low)), (V(dst, **high), V(p, 128, 256, **high))], "v")
 
     lean[0] = LEAN["vex"]
     p = bank()
     mm(V(p), V("vsel", p1=8), V("v8", p1=8))
     copy(V("vex"), V(p))
     lean[0] = LEAN["list"]
-    fill(V("yl"), 0.0)
-    ts(V("yl", 0, 32), V("txa"), 1, OP.add)
-    runs("yl", "sa", "ta", "snA", "offA", "flA")
+    runs("txa", "ca cb cc cd ce", "yl", "sa", "ta", "snA", "offA", "flA")
     lean[0] = LEAN["jc"]
     copy(V("jc"), V("txc"), "v")
     copy(V("jb"), V("txb"), "v")
     lean[0] = LEAN["fas"]
-    tiles_list("la", "La")
+    for r in range(4):
+        copies([(quarter("La", a, 8 * r, 8 * r + 8), quarter("tla", r, 8 * a, 8 * a + 8)) for a in range(4)], "v")
     lean[0] = LEAN["inv"]
     places("tla", "pia", "ba", "bb", "bd", "pii")
     copy(V("pif"), V("pii"), "v")
@@ -520,17 +539,19 @@ def rank_program(g, core, T, topo):
     for i in range(4):
         fill(V("W", 1024 * i, 1024 * i + 1024), 0.0)
     lean[0] = LEAN["inv"]
-    put(V("W"), V("pia"), V("ssrc"))
+    put(V("W"), V("pia"), V("ssA"))
+    for b in range(8):
+        scaled(("tm", b, b + 1, 0, 128, lambda b=b: T["tm"][:, b // 2, :, b % 2, :], 32), V("pif"), col("rm8", b))
     p = bank()
-    mms([(V(p, 32 * i, 32 * i + 32), V("SEL", 128 * i, 128 * i + 128), V("pif"), True, True) for i in range(8)])
+    mm(V(p, 0, 256), V("E"), ("tm", 0, 8, 0, 128, lambda: T["tm"][:, :, :, :, :], 256))
     for k in range(8):
         copy(V("Lr", 32 * k, 32 * k + 32), V(p, k, 256, 8), "v")
     lean[0] = LEAN["r"]
     for i in range(8):
-        pick(V("R", 512 * i, 512 * i + 512), V("W"), V("Lr", 32 * i, 32 * i + 32), "s")
-    lists("R", [(i % 8) * 4 + i // 8 for i in range(32)], "idx")
+        pick(V("R", 512 * i, 512 * i + 512), V("W"), V("Lr", 32 * i, 32 * i + 32))
+    lists("R", [(i % 8) * 4 + i // 8 for i in range(32)], "rsA", "idx")
     lean[0] = LEAN["ya"]
-    lists("W", list(range(32)), "inva")
+    lists("W", list(range(32)), "rsA", "inva")
     lean[0] = 0.0
 
     for n, q in enumerate(come):
@@ -538,131 +559,132 @@ def rank_program(g, core, T, topo):
         for f, win in ((0, "Cw"), (1, "Bw")):
             for h in range(2):
                 p = bank()
-                mms([(V(p, 128 * b, 128 * b + 128), V("SELB", 128 * (4 * h + b), 128 * (4 * h + b) + 128),
-                      V(buf, 256 * q + 128 * f, 256 * q + 128 * f + 128), True, True) for b in range(4)])
+                mms([(V(p, 256 * c, 256 * c + 256), V("SELB", 128 * (4 * f + 2 * c + h), 128 * (4 * f + 2 * c + h) + 128),
+                      V(buf, 256 * q, 256 * q + 256), True, True) for c in range(2)])
                 copy(V(win, 1024 * q + 512 * h, 1024 * q + 512 * h + 512), V(p))
     pick2(V("vc"), V("Cw"), V("jc"), V("vex"), OP.mult)
     pick2(V("w1"), V("Bw"), V("jb"), V("vc"), OP.mult)
 
     def addruns(src, fl, off, z, scn):
         o, a, b = V(scn), V(fl, 7, 519), V(src)
-        one("v", [o], [a, b], lambda q, x: q.tensor_tensor_scan(o[3](), a[3](), b[3](), 0.0, OP.mult, OP.add), {"v": cyc(512)})
+        one("v", [o], [a, b], lambda q, x: q.tensor_tensor_scan(o[5](), a[5](), b[5](), 0.0, OP.mult, OP.add), {"v": cyc(512)})
         put(V(z), V(off), V(scn))
 
-    def reduce(z, land, sem, RT, PT, pw):
-        lean[0] = LEAN["red"]
-        for q in ring[:3]:
+    def reduce(z, land, sem, PT):
+        for q in ring:
+            lean[0] = LEAN["pw" if q == me else "red"]
             p = bank()
             mms([(V(p, 16 * b, 16 * b + 16), V(z, 1 + 1024 * q + 128 * b, 129 + 1024 * q + 128 * b), V("E", 0, 16), True, True)
                  for b in range(8)])
-            copy(V(RT, 128 * q, 128 * q + 128), V(p, 0, 128))
-            p = bank()
-            o, i, idn = V(p, 0, 128), V(RT, 128 * q, 128 * q + 128), V("ident")
-            op("t", [o], [i, idn], [([o], [i, idn], lambda k, x, o=o, i=i: k.transpose(o[3](), i[3](), idn[3]()))],
-               {"t": 512 * PE * CYCLE})
-            copy(V(PT, 128 * q, 128 * q + 128), V(p, 0, 128))
-            send(q, V(PT, 128 * q, 128 * q + 128), T[land][:, 128 * me:128 * me + 128], sem)
-        lean[0] = LEAN["pw"]
-        for h in range(4):
-            p = bank()
-            c = 1 + 1024 * me + 256 * h
-            mm(V(p, 0, 256), V("E"), V(z, c, c + 256))
-            copy(V(pw, 8 + 256 * h, 264 + 256 * h), V(p, 0, 256))
+            turned(V(PT, 128 * q, 128 * q + 128), V(p, 0, 128))
+            if q != me:
+                send(q, V(PT, 128 * q, 128 * q + 128), T[land][:, 128 * me:128 * me + 128], sem)
         lean[0] = 0.0
         expect(land, 128, sem)
 
-    def spread(buf, q, win, at, parts):
-        w = 8 // parts
-        for h in range(parts):
+    def spread(buf, q, win, at, dx, full):
+        for m in range(4):
+            src = V(buf, 128 * q, 128 * q + 128)
             p = bank()
-            mms([(V(p, 128 * b, 128 * b + 128), V("SEL", 128 * (w * h + b), 128 * (w * h + b) + 128),
-                  V(buf, 128 * q, 128 * q + 128), True, True) for b in range(w)])
-            copy(V(win, at + 128 * w * h, at + 128 * w * (h + 1)), V(p, 0, 128 * w))
+            mm(V(p, 0, 128), V("SEL", 128 * m, 128 * m + 128), src)
+            here, there = (at[m], at[m] + 128), (at[m] + dx, at[m] + dx + 128)
+            if m < full:
+                copy(V(win, *here), V(p, 0, 128))
+                p = bank()
+                mm(V(p, 0, 128), V("SEL", 128 * (m + 4), 128 * (m + 4) + 128), src)
+                copy(V(win, *there), V(p, 0, 128))
+            else:
+                copies([(V(win, *here), V(p, 0, 128)), (V(win, *there, **low), V(p, 0, 128, **high)),
+                        (V(win, *there, **high), V(p, 0, 128, **low))])
+
+    def sums(buf, n, win, sem):
+        spread(buf, come[n], win + str(come[n]), [8 + 128 * m for m in range(4)], 512, FULL[sem][n])
+
+    def factor(buf, n):
+        q = come[n]
+        spread(buf, q, "Aw", [1024 * q + 512 * (m % 2) + 128 * (m // 2) for m in range(4)], 256, FULL["n"][n])
 
     addruns("w1", "flA", "offA", "zA", "scn")
-    zeros(V("fcr", 0, 2048))
-    reduce("zA", "LP", "p", "RT", "PT", "pw%d" % me)
+    reduce("zA", "LP", "p", "PT")
+    zeros(V("zB", 0, ZB1))
 
-    def gather(q, lst, o, prev, own="pw%d" % me):
-        w, l = V(own if q == me else "pw%d" % q), V(lst, 32 * q, 32 * q + 32)
-        if prev is None:
-            pick(V(o), w, l)
+    def gather(win, n, lst, acc, lo=0, hi=32):
+        q = come[n]
+        o, w, l = V(acc + str(n), 16 * lo, 16 * hi), V(win + str(q)), V(lst, 32 * q + lo, 32 * q + hi)
+        if n == 0:
+            pick(o, w, l)
         else:
-            pick2(V(o), w, l, V(prev), OP.add)
+            pick2(o, w, l, V(acc + str(n - 1), 16 * lo, 16 * hi), OP.add)
 
-    zeros(V("fcr", 2048, 4096))
-    zeros(V("zB", 0, 2048))
-    for name in ("qw", "pw0", "pw1", "pw2", "pw3"):
-        fill(V(name, 0, 8), 0.0)
-    gather(me, "idx", "ac0", None)
+    for q in range(4):
+        fill(V("pw%d" % q, 0, 8), 0.0)
+        fill(V("qw%d" % q, 0, 8), 0.0)
     lean[0] = LEAN["fas"]
     pick(V("faS"), V("far"), V("La"))
     lean[0] = 0.0
-    for n in (1, 2):
-        spread("LP", come[n], "pw%d" % come[n], 8, 4)
-        gather(come[n], "idx", "ac%d" % n, "ac%d" % (n - 1))
-    q = come[3]
-    spread("LP", q, "pw%d" % q, 8, 8)
+    for n in range(4):
+        sums("LP" if n else "PT", n, "pw", "p")
+        if n < 3:
+            gather("pw", n, "idx", "ac")
     for r in ring[:OWN] + [me] + ring[OWN:3]:
         lo, hi = 128 * r, 128 * r + 128
         lean[0] = LEAN["own"] if r == me else 0.0
-        pick2(V("ac3", lo, hi), V("pw%d" % q), V("idx", 32 * q + 8 * r, 32 * q + 8 * r + 8), V("ac2", lo, hi), OP.add)
+        gather("pw", 3, "idx", "ac", 8 * r, 8 * r + 8)
         tt(V("OT", lo, hi), V("ac3", lo, hi), V("faS", lo, hi), OP.mult)
         if r != me:
             send(r, V("OT", lo, hi), T["LA"][:, 128 * me:128 * me + 128], "n")
     lean[0] = 0.0
     expect("LA", 128, "n")
-    zeros(V("zB", 2048, 4104))
+    zeros(V("zB", ZB1, 4104))
 
     lean[0] = LEAN["lb"]
-    ts(V("nb"), V("txb"), 4096, OP.mult)
-    tt(V("nbi"), V("nb"), V("txa"), OP.add)
-    for k in range(16):
-        ts(("xe", k, k + 1, lambda k=k: T["xe"][:, k:512:16]), V("nbi"), V("E", k, k + 1), OP.mult)
-    p = bank()
-    mm(V(p), V("GRP"), V("xe"))
-    copy(V("xr"), V(p))
-    copy(V("jo"), V("tob"), "v")
-    for i in range(4):
-        pick2(V("mk", 128 * i, 128 * i + 128), V("xr"), V("jo", 8 * i, 8 * i + 8), V("E"), OP.mult)
-    tt(V("m2"), V("mk", 0, 512, 2), V("mk", 1, 512, 2), OP.add)
-    tt(V("m3"), V("m2", 0, 256, 2), V("m2", 1, 256, 2), OP.add)
-    tt(V("m4"), V("m3", 0, 128, 2), V("m3", 1, 128, 2), OP.add)
-    tt(V("nhi"), V("m4", 0, 64, 2), V("m4", 1, 64, 2), OP.add)
-    ts(V("nlo"), V("nhi"), 4095, OP.bitwise_and)
-    copy(V("ja"), V("nlo"), "v")
-    ts(V("nhi"), V("nhi"), 12, OP.arith_shift_right)
-    fill(V("ym"), 0.0)
-    ts(V("ym", 0, 32), V("nhi"), 1, OP.add)
-    runs("ym", "sb", "tb", "snB", "offB", "flB")
+    ts(V("oa"), V("tob"), 15, OP.bitwise_and)
+    ts(V("oc"), V("tob"), 4, OP.arith_shift_right)
+    ts(V("oa"), V("oa"), 32, OP.mult)
+    tt(V("od"), V("oa"), V("oc"), OP.add)
+    copies([(V("jq", h, 32, 2), V("od", 16 * h, 16 * h + 16)) for h in (0, 1)], "v")
+    pick(V("G"), V("Tab"), V("jq"))
+    turned(X("T4", lambda: T["T4"][:, :, :, :], 512), V("G"))
+    for h in (0, 1):
+        turned(("T1", h, h + 1, 0, 128, lambda h=h: T["T1"][:, h, :, :], 32), X("T4", lambda h=h: T["T4"][:, :, h, 0:2], 32))
+    for h in (0, 1):
+        turned(V("F", 32 * h, 32 * h + 32), ("T1", 0, 2, 0, 128, lambda h=h: T["T1"][:, :, h, :], 32))
+    copy(V("nB"), V("F", 1, 64, 2), "v")
+    runs("nB", "da db dc dd de", "ym", "sb", "tb", "snB", "offB", "flB")
+    copy(V("nA", **high), V("F", 0, 64, 2, **high), "v")
+    ts(V("nx", **high), V("nA", **high), 256, OP.bitwise_and)
+    ts(V("ny", **high), V("nx", **high), -2, OP.mult, 256, OP.add)
+    tt(V("nz", **high), V("ny", **high), V("F", 0, 64, 2, **high), OP.add)
+    copies([(V("ja", **low), V("F", 0, 64, 2, **low)), (V("ja", **high), V("nz", **high))], "v")
     lean[0] = LEAN["vco"]
+    copy(V("jo"), V("tob"), "v")
     pick(V("vco"), V("vc"), V("jo"))
     lean[0] = LEAN["ib"]
     places("tlb", "pib", "be", "bf", "bg", "pij")
-    put(V("fcr"), V("pib"), V("ssrc"))
-    lists("fcr", list(range(32)), "invb")
+    put(V("W"), V("pib"), V("ssB"))
+    lists("W", list(range(32)), "rsB", "invb")
 
     lean[0] = LEAN["ya"]
-    gather(me, "inva", "ya0", None)
-    for n in (1, 2, 3):
-        gather(come[n], "inva", "ya%d" % n, "ya%d" % (n - 1))
+    for n in range(4):
+        gather("pw", n, "inva", "ya")
     tt(V("yo"), V("ya3"), V("fag"), OP.mult)
     dmas("dya", [("y", H(T.ya[:, 512 * b:512 * b + 512]), group("yo", b)) for b in range(8)], 262144)
     lean[0] = 0.0
 
-    spread("OT", me, "Aw", 1024 * me, 4)
-    for n in (1, 2, 3):
-        spread("LA", come[n], "Aw", 1024 * come[n], 4)
+    for n in range(4):
+        factor("LA" if n else "OT", n)
     pick2(V("w2"), V("Aw"), V("ja"), V("vco"), OP.mult)
     addruns("w2", "flB", "offB", "zB", "scm")
-    reduce("zB", "LQ", "q", "RU", "PU", "qw")
+    reduce("zB", "LQ", "q", "PU")
 
-    gather(me, "invb", "ac0", None, "qw")
-    for n in (1, 2, 3):
-        q = come[n]
-        spread("LQ", q, "pw%d" % q, 8, 4)
-        gather(q, "invb", "ac%d" % n, "ac%d" % (n - 1))
-    dmas("dyb", [("ys"[b % 2], H(T.yb[:, 512 * b:512 * b + 512]), group("ac3", b)) for b in range(8)], 262144)
+    for n in range(4):
+        sums("LQ" if n else "PU", n, "qw", "q")
+        if n < 3:
+            gather("qw", n, "invb", "yb")
+    for h in (0, 1):
+        gather("qw", 3, "invb", "yb", 16 * h, 16 * h + 16)
+        dmas("dyb%d" % h, [("ys"[b % 2], H(T.yb[:, 512 * b + 256 * h:512 * b + 256 * h + 256]),
+                            group("yb3", b, 256 * h, 256 * h + 256)) for b in range(8)], 131072)
 
     for i, e, at in order(ops):
         where.update(at)

@@ -4,21 +4,20 @@ OP = AluOpType
 COPY = ActivationFunctionType.Copy
 IDENTITY = ActivationFunctionType.Identity
 ZW = 4728
-OWN = 2
 SIZES = {
     "int32": {128: "Di Ei", 32: "tla tlb tlc txa txb txc tob", 512: "Tab"},
     "uint16": {256: "Lr"},
-    "bfloat16": {128: "E32", 512: "ramp ssA ssB fag", 1024: "SELB CB LCB", 4096: "fcb FR far Cw Bw W R"},
-    "float32": {128: "E vsel N1 N2", 520: "flA flB",
+    "bfloat16": {128: "E32", 512: "ssA ssB fag", 1024: "CB LCB", 4096: "FR far W R", 12288: "CW"},
+    "float32": {128: "E vsel N1 N2 eye", 9 * 1032 + 520: "win",
                 512: "v8 vex vc vco w1 w2 scn scm PT PU LP OT LA LQ faS ac0 ac1 ac2 ac3 ya0 ya1 ya2 ya3 yo G yb0 yb1 yb2 yb3",
-                1024: "SEL", 1032: "pw0 pw1 pw2 pw3 qw0 qw1 qw2 qw3", 4096: "Aw", ZW: "zA zB"},
+                4096: "Aw", ZW: "zA zB"},
 }
 SMALL = {
-    "int32": {8: "kgi kgs", 32: "ba bb bd pii be bf bg pij ca cb cc da db dc oa oc od nA nB nx", 128: "vsi vss"},
+    "int32": {8: "kgi kgs", 32: "ba bb be bf pij ca cb cc da db dc oa oc od nA nB nx"},
     "uint16": {32: "La ja jb jc jo jq pia pib snA snB offA offB", 64: "L2", 128: "idx inva invb"},
     "bfloat16": {8: "rsA rsB"},
-    "float32": {4: "rm4 hf n0 b1 b2 b3 bA bB c0 c1", 8: "rm8 w01", 32: "trash pif sa ta sb tb cd ce dd de ny nz",
-                40: "yl ym", 64: "F"},
+    "float32": {4: "rm4 hf hu n0 b1 b2 b3 b4 bA bB c0 c1 c2 c3", 8: "rm8 w01",
+                32: "trash pif sa ta sb tb bd bg cd ce dd de ny nz laf", 40: "yl ym", 64: "F lf"},
 }
 SCRATCH = {n: ("sbuf", [128, c], d) for d, x in SIZES.items() for c, names in x.items() for n in names.split()}
 PLACE = {}
@@ -29,6 +28,10 @@ for _d, _x in SMALL.items():
             PLACE[_n] = ("small_" + _d, _at, _c)
             _at += -(-_c // 16) * 16
     SCRATCH["small_" + _d] = ("sbuf", [128, _at], _d)
+for _i, _n in enumerate("pw0 pw1 pw2 pw3 qw0 qw1 qw2 qw3 flA flB".split()):
+    PLACE[_n] = ("win", 1032 * _i, 1032 if _i < 8 else 520)
+SCRATCH["SEL"] = ("sbuf", [128, 8, 2, 64], "float32")
+SCRATCH["SELB"] = ("sbuf", [128, 4, 2, 64], "bfloat16")
 SCRATCH["tm"] = ("sbuf", [128, 4, 4, 2, 8], "float32")
 SCRATCH["T4"] = ("sbuf", [128, 16, 2, 16], "float32")
 SCRATCH["T1"] = ("sbuf", [128, 2, 2, 16], "float32")
@@ -36,25 +39,45 @@ for _b in range(8):
     SCRATCH["pb%d" % _b] = ("psum", [128, 512], "float32")
 ENG = {"v": "sv", "s": "ss", "t": "st", "g": "sg"}
 SEMAPHORES = (list(ENG.values()) + ["dt" + t for t in ("la", "lb", "lc", "xa", "xb", "xc", "ob")]
-              + ["df%d" % i for i in range(4)] + ["dv", "dfa", "dfe", "dfg", "dtab", "dya", "dyb0", "dyb1"]
+              + ["df%d" % i for i in range(4)] + ["drep", "dv", "dfa", "dfe", "dfg", "dtab", "dya", "dyb0", "dyb1"]
               + ["l" + k for k in "cpnq"] + ["%s%d" % (k, d) for k in "cpnq" for d in (1, 2, 3)])
-CYCLE, GATHER, SCATTER, WAKE, PE = 0.00087, 1.5, 3.2, 0.06, 0.5
-ISSUE, FIRST, HOP, RATE = 0.45, 1.0, 1.3, 55e3
-DMA_ISSUE, DMA_TIME, DMA_RATE = 0.07, 1.6, 180e3
-BYTES = {"float32": 4, "int32": 4, "bfloat16": 2, "uint16": 2}
-LEAN = {"list": -2.0, "inv": 0.0, "r": 0.0, "lb": 0.0, "vco": 0.0, "ib": 0.0, "ya": -1.0, "fas": 0.0, "own": 0.0, "wf": 5.0,
-        "ss": 0.0, "jc": 0.0, "vex": -4.0, "pw": 1.0, "red": 0.0, "sel": 1.0, "l2": 0.0}
-FULL = {"p": (0, 0, 0, 0), "n": (4, 0, 0, 0), "q": (0, 0, 0, 0)}
-ZB1 = 1536
-
-
-def op_time(op):
-    t = min(op["cost"].values()) if op["cost"] else 0.0
-    if op["kind"] == "send":
-        t += op["bytes"] / RATE + HOP
-    elif op["kind"] == "dma":
-        t += op["bytes"] / DMA_RATE + DMA_TIME
-    return t
+PLAN = {
+    "start": (0.0, 0.01, "v"), "za": (0.5, 0.5, "s"), "biasA": (1.0, 0.01, "v"), "wf0": (1.5, 0.2, "v"), "ssA": (2.2, 0, "v"),
+    "front": (2.3, 0.14, "svsvsvss"), "l1": (4.1, 0.1, "s"), "l2": (4.4, 0.1, "s"), "l3": (6.3, 0.1, "s"), "l0": (6.6, 0.1, "s"),
+    "placeA": (4.6, 0.01, "v"), "wf1": (4.8, 0.01, "v"), "putA": (5.5, 0, "v"), "c0": (7.0, 0.05, "s"), "b0": (7.5, 0.05, "s"),
+    "vex": (5.6, 0.01, "s"), "next": (7.0, 0.01, "v"), "runsA": (7.4, 0.01, "s"), "jc": (9.0, 0.01, "v"), "tm": (6.0, 0.01, "s"),
+    "lr": (8.9, 0, "v"), "c1": (9.1, 0.05, "sv"), "b1": (9.6, 0.05, "sv"), "c2": (10.3, 0.05, "sv"), "b2": (10.8, 0.05, "sv"),
+    "c3": (11.5, 0.05, "sv"), "b3": (12.0, 0.05, "s"), "vc": (12.1, 0, "v"), "w1": (12.9, 0.5, "v"), "r": (13.0, 0.75, "s"),
+    "rs": (1.5, 0.01, "s"), "zero": (8.85, 0.01, "v"), "redA": (15.5, 0.3, "v"), "la": (16.5, 0.3, "v"), "ownA": (18.5, 0.3, "vv"),
+    "idx": (19.0, 0.5, "v"), "fas": (19.1, 0, "s"), "ac0": (20.2, 0, "v"), "p1": (19.8, 0.1, "s"), "ac1": (21.2, 0, "v"),
+    "p2": (20.6, 0.1, "s"), "ac2": (22.0, 0, "v"), "p3": (21.8, 0.1, "sv"), "ot": (23.0, 0.2, "v"), "inva": (24.0, 0.3, "v"),
+    "ssB": (17.7, 0.01, "v"), "ob": (18.0, 0.01, "v"), "tab": (24.0, 0, "s"), "turn": (25.0, 0.01, "v"), "runsB": (25.5, 0.01, "s"),
+    "ja": (26.5, 0.01, "v"), "vco": (25.0, 0.01, "s"), "n0": (24.5, 0.2, "s"), "n1": (26.5, 0.1, "s"), "n2": (27.7, 0.1, "s"),
+    "n3": (28.9, 0.1, "sv"), "placeB": (27.0, 0.01, "v"), "putB": (27.5, 0.7, "v"), "invb": (31.0, 0.3, "v"), "w2": (30.0, 0.5, "v"),
+    "ya0": (30.5, 0.1, "s"), "ya": (34.1, 0.3, "v"), "redB": (33.5, 0.3, "v"), "ownB": (36.5, 0.3, "s"), "yb0": (37.5, 0, "s"),
+    "q1": (37.0, 0.1, "s"), "yb1": (38.5, 0, "v"), "q2": (38.2, 0.1, "s"), "yb2": (39.7, 0, "v"), "q3": (39.4, 0.1, "sv"),
+    "yb3": (40.5, 0.1, "v"), "lf": (3.5, 0, "v"),
+}
+FULL = {"p": ("", "pp", "pp", "ts"), "n": ("tt", "pp", "pp", "ts"), "q": ("", "pp", "pp", "ts")}
+FINE = (2, 2, 2, 1)
+CUTS = (0, 1024, 2048, 3072, 4096)
+NFA = 3
+OWN = 2
+WF0, ZA0, ZB0, ZB1 = 3, 1024, 512, 2048
+YA, YB, IB, YAG = 2, 2, 2, True
+PLAN.update({'start': (1.0, 0.01, 'ssvs'), 'za': (2.1, 0.5, 'svv'), 'biasA': (1.0, 0.01, 'vss'), 'wf0': (1.1, 0.2, 'v'), 'ssA': (1.95, 0, 'vs'), 'front': (2.05, 0.14, 'svsvsvss'), 'l1': (3.95, 0.15, 's'), 'l2': (4.4, 0.1, 'sssv'), 'l3': (5.05, 0.1, 'sv'), 'l0': (4.06, 0.1, 's'), 'placeA': (4.6, 0.3, 'sv'), 'wf1': (6.05, 0.01, 'vs'), 'putA': (5.4, 0, 'v'), 'c0': (7.45, 0.05, 's'), 'b0': (4.6, 0.05, 's'), 'vex': (4.95, 0.5, 'sssv'), 'next': (6.9, 0.4, 'sssv'), 'runsA': (7.05, 0, 'svs'), 'jc': (9.35, 0.01, 'vs'), 'tm': (7.4, 0.01, 's'), 'lr': (9.65, 0, 'ssvs'), 'c1': (9.75, 0.05, 'sv'), 'b1': (10.1, 0.01, 'sv'), 'c2': (10.3, 0.05, 'sv'), 'b2': (10.7, 0.05, 'sv'), 'c3': (10.5, 0.3, 'vs'), 'b3': (12.25, 0.05, 'vs'), 'vc': (12.5, 0.3, 'vsss'), 'w1': (12.9, 0.5, 'sv'), 'r': (13.0, 0, 's'), 'rsA': (16.4, 0.05, 'v'), 'zero': (20.25, 0.15, 'svv'), 'redA': (15.4, 0.3, 's'), 'la': (15.5, 0.3, 'v'), 'ownA': (18.6, 0.15, 'vv'), 'idx': (19.35, 0.5, 'v'), 'fas': (17.1, 0.1, 'ssv'), 'ac0': (21.0, 0.75, 'v'), 'p1': (20.15, 0.01, 's'), 'ac1': (21.35, 0.3, 'v'), 'p2': (20.35, 0.1, 's'), 'ac2': (23.15, 0, 'v'), 'p3': (21.05, 0.1, 'sv'), 'ot': (23.0, 0.2, 'v'), 'inva': (24.0, 0.3, 'vsss'), 'ssB': (12.7, 0.75, 'sssv'), 'ob': (15.8, 0.2, 'sssv'), 'tab': (16.15, 0.75, 's'), 'turn': (20.5, 0.2, 'ssvs'), 'runsB': (26.6, 0.01, 's'), 'ja': (26.9, 0.01, 'ssv'), 'vco': (24.25, 0.01, 'sv'), 'n0': (25.0, 0.2, 'sssv'), 'n1': (28.0, 0, 'svs'), 'n2': (29.2, 0.2, 's'), 'n3': (31.6, 0.2, 'sv'), 'placeB': (26.9, 0.01, 'vsss'), 'putB': (27.9, 0.7, 'v'), 'invb': (33.4, 0.4, 'v'), 'w2': (28.1, 0.5, 'svs'), 'ya0': (32.5, 0.1, 'ssvs'), 'ya': (34.35, 0.3, 'v'), 'redB': (33.6, 0.3, 'vsss'), 'ownB': (35.15, 0.1, 's'), 'yb0': (33.1, 0, 'sssv'), 'q1': (37.25, 0.1, 'v'), 'yb1': (39.15, 0.01, 'ssvs'), 'q2': (37.8, 0.15, 'ssvs'), 'yb2': (41.65, 0, 'vsss'), 'q3': (40.0, 0.4, 'sssv'), 'yb3': (39.25, 0.1, 'v')})
+FULL = {'n': ('tp', 'pp', 'pp', 'pp'), 'q': ('', 'pp', 'ss', 'st'), 'p': ('', 'pp', 'tp', 'pt')}
+IB, WF0, YB, OWN, ZB1, YAG, YA, ZA0, ZB0, FINE = 1, 4, 2, 1, 1536, True, 1, 512, 0, (2, 2, 2, 2)
+NFA, TILED, YAG, YB = 2, True, False, 1
+PLAN = {'start': (0.0, 0.2, 'sv'), 'za': (0.0, 0.01, 's'), 'biasA': (0.5, 0.2, 'v'), 'wf0': (1.35, 0.2, 'ssv'), 'ssA': (3.35, 0.05, 'v'), 'front': (1.65, 0.14, 'svsvsvss'), 'l1': (4.2, 0, 'ssvs'), 'l2': (0.5, 0.1, 'svv'), 'l3': (7.15, 0.01, 'ssv'), 'l0': (4.96, 0.3, 'ssv'), 'placeA': (5.35, 0.3, 'svs'), 'wf1': (5.3, 0.5, 'svv'), 'putA': (4.9, 0.5, 'ssvs'), 'c0': (7.45, 0.05, 's'), 'b0': (7.25, 0.3, 'ssv'), 'vex': (4.7, 0.5, 'ssv'), 'next': (6.8, 0.4, 'vss'), 'runsA': (6.85, 0, 'svs'), 'jc': (6.65, 0.5, 'svv'), 'tm': (7.4, 0.01, 's'), 'lr': (9.4, 0.01, 'vs'), 'c1': (7.95, 0.01, 'svv'), 'b1': (10.85, 0, 'svv'), 'c2': (9.55, 0.05, 'sv'), 'b2': (10.2, 0.05, 'sv'), 'c3': (10.5, 0.3, 'vsss'), 'b3': (11.25, 0.1, 'vs'), 'vc': (7.5, 0.3, 'sssv'), 'w1': (12.15, 0.3, 'vss'), 'r': (14.25, 0, 's'), 'rs': (1.0, 0.4, 'vss'), 'zero': (1.05, 0.01, 'ssvs'), 'redA': (14.65, 0.3, 'vsss'), 'la': (12.75, 0.3, 'sssv'), 'ownA': (17.35, 0.1, 'vv'), 'idx': (17.6, 0.5, 'ssvs'), 'fas': (15.85, 0.75, 'vss'), 'ac0': (16.2, 0.75, 'v'), 'p1': (20.15, 0.01, 's'), 'ac1': (19.2, 0.4, 'sssv'), 'p2': (20.25, 0.1, 's'), 'ac2': (18.25, 0.01, 'vss'), 'p3': (21.15, 0.1, 'svs'), 'ot': (23.4, 0.4, 'vss'), 'inva': (24.0, 0.3, 'svs'), 'ssB': (12.7, 0.05, 'v'), 'ob': (15.55, 0.05, 'svs'), 'tab': (16.3, 0.75, 'sv'), 'turn': (19.65, 0.2, 'sssv'), 'runsB': (26.6, 0.01, 'ssvs'), 'ja': (26.65, 0.01, 'vs'), 'vco': (26.15, 0.1, 'ssv'), 'n0': (25.25, 0.01, 'sssv'), 'n1': (27.8, 0.4, 'vsss'), 'n2': (29.55, 0.2, 's'), 'n3': (31.75, 0.15, 'svv'), 'placeB': (26.65, 0.01, 'ssv'), 'putB': (27.45, 0, 'svv'), 'invb': (33.3, 0.15, 'v'), 'w2': (30.65, 0.75, 'svv'), 'ya0': (32.85, 0.15, 'sv'), 'ya': (34.2, 0.3, 'sssv'), 'redB': (33.6, 0.3, 's'), 'ownB': (34.6, 0.1, 'ssv'), 'yb0': (32.35, 0.3, 'sssv'), 'q1': (35.5, 0, 'v'), 'yb1': (37.4, 0.15, 'ssvs'), 'q2': (35.7, 0.2, 'sssv'), 'yb2': (41.9, 0.3, 'vsss'), 'q3': (40.25, 0.4, 'sssv'), 'yb3': (35.25, 0.05, 'v'), 'lf': (2.85, 0.3, 'vs')}
+FULL = {'n': ('pt', 'pp', 'tp', 'pp'), 'q': ('', 'pp', 'ss', 'st'), 'p': ('', 'pt', 'pt', 'pt')}
+NFA, WF0 = 3, 3
+TILA, VDMA, TM, REP = True, False, 8, 0
+PLAN.update({"idx0": (19.0, 0, "v"), "idx1": (19.0, 0, "v"), "idx2": (19.0, 0, "v"),
+             "tmm": (9.5, 0, "v"), "x0": (6, .1, "s"), "x1": (9, .1, "s"), "x2": (10.2, .1, "s"), "x3": (11.4, .1, "sv")})
+PLAN = {'start': (0.58, 0.05, 'vss'), 'za': (0.1, 0.01, 'sssv'), 'biasA': (0.83, 0.1, 's'), 'wf0': (1.1, 0.01, 'vsss'), 'ssA': (3.05, 0.3, 'sv'), 'front': (2.23, 0.01, 'svsvsvss'), 'l1': (3.67, 0.9, 'v'), 'l2': (4.27, 0.15, 's'), 'l3': (4.87, 0.15, 'svv'), 'l0': (3.65, 0.2, 's'), 'placeA': (4.6, 0.15, 'vs'), 'wf1': (4.62, 0.15, 'ssv'), 'putA': (6.12, 0, 'v'), 'c0': (6.38, 0, 'v'), 'b0': (6.37, 0.15, 'v'), 'vex': (0.02, 0.3, 'vss'), 'next': (0.8, 0.4, 's'), 'runsA': (4.65, 0.15, 'ssv'), 'jc': (5.46, 0.1, 'vsss'), 'tm': (5.73, 0.001, 's'), 'lr': (4.55, 0, 's'), 'c1': (1.65, 0.01, 'vs'), 'b1': (5.88, 0.15, 'v'), 'c2': (7.25, 0.01, 'svs'), 'b2': (5.22, 0.75, 'v'), 'c3': (7.49, 0.15, 'v'), 'b3': (7.79, 0, 'sssv'), 'vc': (5.49, 0.75, 'sssv'), 'w1': (3.43, 0.2, 'vs'), 'r': (12.18, 0.1, 'sssssvss'), 'rs': (1.0, 0.1, 'sssv'), 'zero': (1.05, 0.4, 'ssvs'), 'redA': (12.5, 0.1, 'ssv'), 'la': (7.77, 0.05, 'svv'), 'ownA': (13.04, 0.15, 'ssv'), 'idx': (18.49, 0, 'svv'), 'fas': (18.45, 0.2, 'vss'), 'ac0': (10.12, 0.1, 'vss'), 'p1': (18.73, 0.2, 'sv'), 'ac1': (20.2, 0.3, 'vss'), 'p2': (20.48, 0.15, 'ssv'), 'ac2': (21.32, 0.05, 's'), 'p3': (21.42, 0, 'ssv'), 'ot': (22.2, 0.4, 'sssv'), 'inva': (24.52, 0.3, 'vs'), 'ssB': (9.25, 0.5, 's'), 'ob': (13.18, 0.3, 's'), 'tab': (19.87, 0.75, 'svv'), 'turn': (19.53, 0.75, 'vsss'), 'runsB': (26.65, 0.01, 'sv'), 'ja': (26.52, 0.2, 'ssv'), 'vco': (21.8, 0.3, 'svs'), 'n0': (24.57, 0.01, 's'), 'n1': (27.12, 0.01, 'svs'), 'n2': (29.85, 0.2, 'ssvs'), 'n3': (32.13, 0.05, 'svv'), 'placeB': (26.63, 0.01, 'svs'), 'putB': (26.97, 0.2, 'ssvs'), 'invb': (32.7, 0.3, 'vss'), 'w2': (29.35, 0.75, 'svv'), 'ya0': (33.4, 0.1, 's'), 'ya': (33.82, 0.3, 'v'), 'redB': (33.18, 0.3, 'vs'), 'ownB': (38.45, 0.01, 's'), 'yb0': (23.7, 0.01, 'vsss'), 'q1': (38.77, 0.05, 'svv'), 'yb1': (44.6, 0.1, 'ssvs'), 'q2': (42.85, 0.15, 'ssv'), 'yb2': (45.9, 0.01, 'vsss'), 'q3': (47.05, 0.75, 'svv'), 'yb3': (42.33, 0.4, 'vs'), 'lf': (5.42, 0.2, 'sssv'), 'idx0': (6.8, 0, 'vsss'), 'idx1': (14.67, 0.4, 'vss'), 'idx2': (14.78, 0, 'v'), 'tmm': (7.78, 0.1, 'svs'), 'x0': (4.81, 0.15, 'ssv'), 'x1': (6.75, 0.05, 'sssv'), 'x2': (6.97, 0, 's'), 'x3': (7.35, 0.01, 'sv')}
+FULL = {'n': ('pp', 'pp', 'ps', 'ps'), 'q': ('', 'pp', 'sp', 'ps'), 'p': ('', 'sp', 'sp', 'ps')}
+TILED, TILA, TM, VDMA, NFA, ZA0, IB, ZB1, YB, FINE, ZB0, YA, WF0, REP, OWN = False, True, 8, True, 0, 512, 1, 1536, 1, (2, 2, 1, 1), 0, 1, 3, 0, 1
 
 
 def meet(a, b):
@@ -66,108 +89,23 @@ def covers(a, b):
 
 
 def order(ops):
-    n = len(ops)
-    pred = [set(op["after"]) for op in ops]
-    last = {}
+    turn, last, tail = [], {}, {}
     for i, op in enumerate(ops):
+        pred = set(op["after"])
         both = [(v, True) for v in op["outs"] if v[0]] + [(v, False) for v in op["ins"] if v[0]]
         for v, w in both:
-            for r, w2, j in last.setdefault(v[0], []):
-                if j != i and (w or w2) and meet(v, r):
-                    pred[i].add(j)
+            pred.update(j for r, w2, j in last.setdefault(v[0], []) if (w or w2 or v[0][0] == "#") and meet(v, r))
         for v, w in both:
             rec = last[v[0]]
             if w:
                 rec[:] = [x for x in rec if not covers(v, x[0])]
             rec.append((v, w, i))
-    chain = {}
-    for i, op in enumerate(ops):
-        if op["eng"] in "gy":
-            chain.setdefault(op["eng"], []).append(i)
-    succ = [[] for _ in ops]
-    for i in range(n):
-        for j in pred[i]:
-            succ[j].append(i)
-    users = {}
-    for op in ops:
-        for b in op["banks"]:
-            users[b] = users.get(b, 0) + 1
-    prio = [0.0] * n
-    behind = {a: b for c in chain.values() for a, b in zip(c, c[1:])}
-    for i in reversed(range(n)):
-        prio[i] = op_time(ops[i]) + max([prio[k] + WAKE for k in succ[i]] or [0.0])
-        if i in behind:
-            prio[i] = max(prio[i], min(ops[i]["cost"].values()) + prio[behind[i]])
-    prio = [prio[i] + ops[i]["lean"] for i in range(n)]
-    free = {q: 0.0 for q in "vstgy"}
-    end = [None] * n
-    bank_of, bank_free = {}, {b: 0.0 for b in range(8)}
-    bank_busy = {}
-    port, dma, first = 0.0, 0.0, True
-    out = []
-    ready = [i for i in range(n) if not pred[i]]
-    missing = [len(p) for p in pred]
-    while ready:
-        cand = []
-        for i in ready:
-            op = ops[i]
-            if op["eng"] in chain and chain[op["eng"]][0] != i:
-                continue
-            st = max([end[j] + WAKE for j in pred[i]] or [0.0])
-            st = max([st] + [bank_busy.get(b, 0.0) for b in op["banks"]])
-            bank = None
-            if op["eng"] == "t" and op["banks"] and op["banks"][0] not in bank_of:
-                idle = [b for b in bank_free if bank_free[b] is not None]
-                if not idle:
-                    continue
-                bank = min(idle, key=lambda b: bank_free[b])
-                st = max(st, bank_free[bank])
-            if op["eng"] == "-":
-                cand.append((st, i, "-", st, bank))
-                continue
-            best = None
-            for e in op["eng"]:
-                s1 = max(st, free[e])
-                f1 = s1 + op["cost"][e]
-                if best is None or f1 < best[0] - 0.01:
-                    best = (f1, i, e, s1, bank)
-            cand.append(best)
-        assert cand, "no call can go on"
-        f0, _, e0, _, _ = min(cand)
-        conflict = [c for c in cand if c[2] == e0 and c[3] < f0 - 1e-6] or [min(cand)]
-        f1, i, e, s1, bank = max(conflict, key=lambda c: (prio[c[1]], -c[1]))
-        op = ops[i]
-        ready.remove(i)
-        if op["eng"] in chain:
-            chain[op["eng"]].pop(0)
-        if bank is not None:
-            bank_of[op["banks"][0]] = bank
-            bank_free[bank] = None
-        end[i] = f1
-        if e != "-":
-            free[e] = f1
-        if op["kind"] == "dma":
-            dma = max(dma, f1) + op["bytes"] / DMA_RATE
-            end[i] = dma + DMA_TIME
-        elif op["kind"] == "send":
-            if first:
-                f1 += FIRST
-                first = False
-                free["g"] = f1
-            port = max(port, f1) + op["bytes"] / RATE
-            end[i] = port + HOP
-        for b in op["banks"]:
-            bank_busy[b] = f1 + WAKE
-            users[b] -= 1
-            if not users[b]:
-                bank_free[bank_of[b]] = f1 + WAKE
-        out.append((i, e, {b: "pb%d" % bank_of[b] for b in op["banks"]}))
-        for k in succ[i]:
-            missing[k] -= 1
-            if not missing[k]:
-                ready.append(k)
-    assert len(out) == n
-    return out
+        c = "g" if op["eng"] == "g" else "d" if op["kind"] == "dma" else None
+        if c:
+            pred.update(tail.get(c, ()))
+            tail[c] = (i,)
+        turn.append(max([op["turn"]] + [turn[j] for j in pred if j != i]))
+    return sorted(range(len(ops)), key=lambda i: (turn[i], i))
 
 
 def rank_program(g, core, T, topo):
@@ -183,8 +121,7 @@ def rank_program(g, core, T, topo):
     banks = {"pb%d" % b: {} for b in range(8)}
     where = {}
     ops = []
-    lean = [0.0]
-    turn = [0]
+    part = {"turn": 0.0, "step": 0.0, "queues": "v", "n": 0, "tiles": 0}
     sent = {}
 
     def wait(e, tok):
@@ -227,6 +164,8 @@ def rank_program(g, core, T, topo):
         call(queue[e], e).then_inc(T.sem[sem], 1)
         count[sem] = count.get(sem, 0) + 1
         after(outs, ins, (sem, count[sem], e, dict(know[e])))
+        if e == "g" and outs[0][3]:
+            wait(e, (sem, count[sem], e, {}))
 
     def emit_dmas(sem, items, extra):
         kn = {}
@@ -264,50 +203,48 @@ def rank_program(g, core, T, topo):
         def ap():
             t = T[where.get(name, name)]
             return t[p0:p1, lo:hi] if step == 1 else t[p0:p1, lo:hi:step]
-        return (name, lo, hi, p0, p1, ap, len(range(lo, hi, step)))
+        return (name, lo, hi, p0, p1, ap)
 
-    def X(name, ap, n):
-        return (name, 0, 1, 0, 128, ap, n)
+    def X(name, index, lo=0, hi=8):
+        return (name, lo, hi, 0, 128, lambda: T[name][index])
 
     def H(ap):
-        return (None, 0, 0, 0, 0, lambda: ap, 0)
+        return (None, 0, 0, 0, 0, lambda: ap)
 
     def group(name, b, lo=0, hi=None):
         return V(name, lo, hi, p0=16 * b, p1=16 * b + 16)
 
-    def col(name, j=0, p0=0, p1=128):
-        return V(name, j, j + 1, p0=p0, p1=p1)
+    def quarter(name, a, lo, hi):
+        return V(name, lo, hi, p0=32 * a, p1=32 * a + 32)
+
+    def col(name, j=0):
+        return V(name, j, j + 1)
 
     def bank():
-        turn[0] += 1
-        return "#%d" % turn[0]
+        part["tiles"] += 1
+        return "#%d" % part["tiles"]
 
-    def op(eng, outs, ins, subs, cost, kind="c", nbytes=0, needs=()):
-        names = []
-        for v in outs + ins:
-            if v[0] and v[0][0] == "#" and v[0] not in names:
-                names.append(v[0])
-        ops.append({"eng": eng, "outs": outs, "ins": ins, "subs": subs, "cost": cost, "kind": kind, "bytes": nbytes,
-                    "banks": names, "after": list(needs), "lean": lean[0]})
+    def now(name):
+        part["turn"], part["step"], part["queues"] = PLAN[name]
+        part["n"] = 0
+
+    def op(eng, outs, ins, subs, kind="c", needs=()):
+        if eng == "vs":
+            eng = part["queues"][part["n"] % len(part["queues"])]
+            part["n"] += 1
+        ops.append({"eng": eng, "outs": outs, "ins": ins, "subs": subs, "kind": kind, "after": list(needs),
+                    "turn": part["turn"] if eng in "vst" else 0.0})
+        if eng in "vst":
+            part["turn"] += part["step"]
         return len(ops) - 1
 
-    def narrow(*vs):
-        return all(v[0][0] != "#" and BYTES[SCRATCH[v[0]][2]] == 2 for v in vs)
-
-    def cyc(n):
-        return max(64, n) * CYCLE
-
-    def one(eng, outs, ins, call, cost):
-        op(eng, outs, ins, [(outs, ins, call)], cost)
+    def one(eng, outs, ins, call):
+        op(eng, outs, ins, [(outs, ins, call)])
 
     def copies(pairs, e="vs"):
-        subs, cost = [], {"v": 0.0, "s": 0.0}
-        for o, i in pairs:
-            subs.append(([o], [i], lambda q, x, o=o, i=i: q.tensor_copy(o[5](), i[5]()) if x == "v"
-                         else q.activation(o[5](), i[5](), COPY)))
-            cost["v"] += cyc(o[6] * 0.5 if narrow(o, i) else o[6])
-            cost["s"] += cyc(o[6])
-        op(e, [o for o, _ in pairs], [i for _, i in pairs], subs, cost)
+        op(e, [o for o, _ in pairs], [i for _, i in pairs],
+           [([o], [i], lambda q, x, o=o, i=i: q.tensor_copy(o[5](), i[5]()) if x == "v" else q.activation(o[5](), i[5](), COPY))
+            for o, i in pairs])
 
     def copy(o, i, e="vs"):
         copies([(o, i)], e)
@@ -321,7 +258,7 @@ def rank_program(g, core, T, topo):
             if b is None:
                 return q.activation(o[5](), i[5](), COPY, scale=sc[5]())
             return q.activation(o[5](), i[5](), IDENTITY, bias=b[5](), scale=sc[5]())
-        one(e, [o], [i, sc] + ([b] if b else []), call, {"v": cyc(o[6]), "s": cyc(o[6])})
+        one(e, [o], [i, sc] + ([b] if b else []), call)
 
     def ts(o, i, s1, op0, s2=None, op1=None):
         rd = [i] + [s for s in (s1, s2) if isinstance(s, tuple)]
@@ -332,281 +269,350 @@ def rank_program(g, core, T, topo):
             if op1 is None:
                 return q.tensor_scalar(o[5](), i[5](), a1, None, op0)
             return q.tensor_scalar(o[5](), i[5](), a1, a2, op0, op1)
-        one("v", [o], rd, call, {"v": cyc(i[6])})
+        one("v", [o], rd, call)
 
     def tt(o, a, b, f):
-        n = a[6] * (1 if a[0][0] == "#" or b[0][0] == "#" else 2)
-        one("v", [o], [a, b], lambda q, x: q.tensor_tensor(o[5](), a[5](), b[5](), f), {"v": cyc(n)})
+        one("v", [o], [a, b], lambda q, x: q.tensor_tensor(o[5](), a[5](), b[5](), f))
 
     def turned(o, i):
-        one("v", [o], [i], lambda q, x: q.transpose(o[5](), i[5]()), {"v": cyc(i[6])})
+        one("v", [o], [i], lambda q, x: q.transpose(o[5](), i[5]()))
 
     def fill(o, c):
-        one("v", [o], [], lambda q, x: q.memset(o[5](), c), {"v": cyc(o[6] * (0.5 if narrow(o) else 1))})
+        one("v", [o], [], lambda q, x: q.memset(o[5](), c))
+
+    def line(o, i, a, b=0.0):
+        rd = [i] + [s for s in (a, b) if isinstance(s, tuple)]
+
+        def call(q, x):
+            a1 = a[5]() if isinstance(a, tuple) else a
+            b1 = b[5]() if isinstance(b, tuple) else b
+            if x == "v":
+                return q.tensor_scalar(o[5](), i[5](), a1, b1, OP.mult, OP.add)
+            return q.activation(o[5](), i[5](), IDENTITY, bias=b1, scale=a1)
+        one("vs", [o], rd, call)
+
+    def eight(o, c):
+        line(o, V("E", 0, 8), 0.0, c)
 
     def ind(w, l):
         return w[5]().indirect(l[5]())
 
-    def pick(o, w, l, e="vs"):
-        n = l[6] * 16 * GATHER * CYCLE
-        one(e, [o], [w, l], lambda q, x: q.tensor_copy(o[5](), ind(w, l)) if x == "v" else q.activation(o[5](), ind(w, l), COPY),
-            {"v": n + 0.05, "s": n + 0.065})
+    def pick(o, w, l):
+        one("vs", [o], [w, l],
+            lambda q, x: q.tensor_copy(o[5](), ind(w, l)) if x == "v" else q.activation(o[5](), ind(w, l), COPY))
 
     def pick2(o, w, l, b, f):
-        one("v", [o], [w, l, b], lambda q, x: q.tensor_tensor(o[5](), ind(w, l), b[5](), f),
-            {"v": l[6] * 16 * GATHER * CYCLE + 0.05})
+        one("v", [o], [w, l, b], lambda q, x: q.tensor_tensor(o[5](), ind(w, l), b[5](), f))
 
     def put(w, l, i):
-        one("v", [w], [l, i], lambda q, x: q.tensor_copy(ind(w, l), i[5]()), {"v": l[6] * 16 * SCATTER * CYCLE + 0.05})
+        one("v", [w], [l, i], lambda q, x: q.tensor_copy(ind(w, l), i[5]()))
 
     def mms(items):
-        outs, ins, subs, cost = [], [], [], 0.0
-        for o, l, r, a, z in items:
-            outs.append(o)
-            ins += [l, r]
-            subs.append(([o], [l, r], lambda q, x, o=o, l=l, r=r, a=a, z=z: q.matmul(o[5](), l[5](), r[5](), a, z)))
-            cost += max(64, r[6]) * (1 if narrow(l) else 4) * PE * CYCLE
-        op("t", outs, ins, subs, {"t": cost})
+        op("t", [o for o, _, _, _, _ in items], [x for _, l, r, _, _ in items for x in (l, r)],
+           [([o], [l, r], lambda q, x, o=o, l=l, r=r, a=a, z=z: q.matmul(o[5](), l[5](), r[5](), a, z))
+            for o, l, r, a, z in items])
 
     def mm(o, l, r):
         mms([(o, l, r, True, True)])
 
     def iota(o, pattern, base, cm):
         if SCRATCH[o[0]][2] == "int32":
-            call = lambda q, x: q.iota(o[5](), pattern, base, cm)
+            one("g", [o], [], lambda q, x: q.iota(o[5](), pattern, base, cm))
         else:
-            call = lambda q, x: q.iota(o[5](), pattern, base, cm, allow_small_or_imprecise_dtypes=True)
-        one("g", [o], [], call, {"g": 0.13 + 2 * o[6] * CYCLE})
+            one("g", [o], [], lambda q, x: q.iota(o[5](), pattern, base, cm, allow_small_or_imprecise_dtypes=True))
 
-    def zeros(o):
-        iota(o, [[0, o[6]]], 0, 0)
+    def zeros(name, lo, hi):
+        if lo < hi:
+            iota(V(name, lo, hi), [[0, hi - lo]], 0, 0)
 
-    def dmas(sem, items, nbytes, extra=()):
-        e = items[0][0]
+    def diagonal(o, ones, pattern, base):
+        one("g", [o], [ones], lambda q, x: q.affine_select(o[5](), ones[5](), pattern, OP.is_equal, 0.0, base, 1))
+
+    def dmas(sem, items, extra=()):
         outs = [o for _, o, _ in items if o[0]]
         ins = list(extra) + [i for _, _, i in items if i[0]]
-        op(e, outs, ins, (sem, items, list(extra)), {e: DMA_ISSUE * len([1 for x in items if x[0] == e])}, "dma", nbytes)
+        op("y", outs, ins, (sem, items, list(extra)), "dma")
 
     def send(q, src, dst, sem):
-        sent[sem, (q - me) % N] = op("g", [], [src], (q, src, dst, sem), {"g": ISSUE}, "send",
-                                     128 * src[6] * BYTES[SCRATCH[src[0]][2]])
+        sent[sem, (q - me) % N] = op("g", [], [src], (q, src, dst, sem), "send")
 
     def expect(buf, width, sem):
         for d in (1, 2, 3):
             q, s = (me - d) % N, "%s%d" % (sem, d)
             v = V(buf, q * width, (q + 1) * width)
-            op("-", [v], [], (v, s, len(topo.engines(T.cores[q], core))), {}, "come", 0, [sent[sem, d]])
+            op("-", [v], [], (v, s, len(topo.engines(T.cores[q], core))), "come", [sent[sem, d]])
 
     def left(sem):
-        v = ("left" + sem, 0, 1, 0, 128, None, 1)
-        op("-", [v], [], (v, "l" + sem, 0), {}, "come", 0, [sent[sem, d] for d in (1, 2, 3)])
+        v = ("left" + sem, 0, 1, 0, 128, None)
+        op("-", [v], [], (v, "l" + sem, 0), "come", [sent[sem, d] for d in (1, 2, 3)])
         return v
 
     ring = [(me + d) % N for d in (1, 2, 3, 0)]
     come = [(me - d) % N for d in (0, 1, 2, 3)]
     low, high = {"p0": 0, "p1": 64}, {"p0": 64, "p1": 128}
+    every = slice(None)
 
     def table(t, e):
-        dmas("dt" + t, [(e, V("t" + t), H(T[t][:, :]))], 16384)
+        dmas("dt" + t, [(e, V("t" + t), H(T[t][:, :]))])
 
-    for i in range(4):
-        lo, hi = 1024 * i, 1024 * i + 1024
-        dmas("df%d" % i, [("y", V("fcb", lo, hi, p0=0, p1=16), H(T.fc[:, lo:hi])),
-                          ("y", V("fcb", lo, hi, p0=16, p1=32), H(T.fb[:, lo:hi]))], 65536)
-    table("lc", "s")
+    for i, (lo, hi) in enumerate(zip(CUTS, CUTS[1:])):
+        hi = min(hi, 4096 - REP)
+        if lo < hi:
+            dmas("df%d" % i, [("y", V("CW", 8192 + lo, 8192 + hi, p0=0, p1=16), H(T.fc[:, lo:hi])),
+                              ("s", V("CW", 8192 + lo, 8192 + hi, p0=16, p1=32), H(T.fb[:, lo:hi]))])
+    table("lc", "y")
     table("lb", "s")
+    if REP:
+        dmas("drep", [("ys"[b % 2], group("FR", b, 4096 - REP, 4096), H(T["f" + "cb"[b // 4]][:, 4096 - REP:4096]))
+                      for b in range(8)])
     for t in ("la", "xa"):
         table(t, "y")
-    dmas("dv", [("y", V("v8", p0=0, p1=8), H(T.v[:, :]))], 16384)
+    if not VDMA:
+        dmas("dv", [("y", V("v8", p0=0, p1=8), H(T.v[:, :]))])
     for t in ("xc", "xb", "ob"):
         table(t, "y")
-    dmas("dfa", [("y", group("far", b), H(T.fa[:, :])) for b in range(3)], 3 << 17)
+    if VDMA:
+        dmas("dv", [("y", X("vex", (slice(o, 128, 16), every), 0, 512), H(T.v[:, :])) for o in range(16)])
+    if NFA:
+        dmas("dfa", [("y", group("far", b), H(T.fa[:, :])) for b in range(NFA)])
 
+    now("start")
+    fill(V("G"), 1.0)
     iota(V("Di"), [[-1, 128]], 128, 1)
     iota(V("kgi"), [[-16, 8]], 0, 1)
-    iota(V("trash"), [[16, 32]], 4097, 1)
+    for a in (0, 1):
+        iota(V("Tab", 256 * a, 256 * a + 256), [[1, 32], [32, 4], [128, 2]], 256 * a - 256, 0)
+    iota(quarter("Tab", me, 0, 512), [[1, 512]], -256, 0)
+    if TILED or TILA or not YA:
+        diagonal(V("eye"), V("G", 0, 128), [[-1, 128]], 0)
+    if not VDMA:
+        diagonal(V("vsel", p1=8), V("G", 0, 128, p1=8), [[-1, 8], [0, 16]], 0)
+    iota(V("trash"), [[16, 32]], 4096, 1)
     iota(V("w01"), [[1, 8]], 0, 0)
-    iota(V("vsi", p1=8), [[1, 128]], 0, -16)
-    iota(V("ramp"), [[1, 512]], -256, 0)
-    zeros(V("Tab"))
-    rows = [("Tab", 0, 512, 0, 128, lambda f=f: T["Tab"][f:128:16, :], 512) for f in (0, 1)]
-    dmas("dtab", [("y", rows[0], H(T.xa[:, :])), ("y", rows[1], H(T.xb[:, :]))], 32768)
-
+    for i in (0, 1):
+        diagonal(X("SELB", (every, every, i, every), i, i + 1), V("G", 0, 256), [[-16, 4], [0, 4], [-1, 16]], -64 * i)
     ts(V("Ei"), V("Di"), 15, OP.bitwise_and)
     ts(V("kgs"), V("kgi"), 4, OP.arith_shift_right)
     ts(V("E"), V("Ei"), 0, OP.is_equal)
     ts(V("rm8"), V("kgs"), 0, OP.is_equal)
     for f in (0, 1):
         ts(V("E32", 64 * f, 64 * f + 64), V("E", 0, 64), col("rm8", f), OP.mult)
-    tt(V("rm4"), V("rm8", 0, 8, 2), V("rm8", 1, 8, 2), OP.add)
-    one("v", [col("hf")], [V("rm8")], lambda q, x: q.tensor_reduce(col("hf")[5](), V("rm8", 1, 8, 2)[5](), AxisListType.X, OP.add),
-        {"v": cyc(4)})
+    now("za")
+    for lo in range(0, ZA0, 512):
+        one("vs", [V("zA", lo, lo + 512)], [V("G")], lambda q, x, o=V("zA", lo, lo + 512): q.memset(o[5](), 0.0) if x == "v"
+            else q.activation(o[5](), V("G")[5](), COPY, scale=0.0))
+    now("zero")
+    fill(V("yl", 32, 81, 48), -1.0)
+    fill(V("win", 0, 8 * 1032, 1032), 0.0)
+    fill(V("win", 8 * 1032 + 7, 9 * 1032 + 8, 1032), 0.0)
+    now("next")
     ts(col("n0"), col("E", 0), 0, OP.is_equal)
     ts(V("N1"), V("Di"), 129, OP.is_equal, col("n0"), OP.mult)
     ts(V("N2"), V("Di"), 113, OP.is_equal, col("E", 0), OP.mult)
-    ts(V("vss", p1=8), V("vsi", p1=8), 4, OP.arith_shift_right)
-    ts(V("vsel", p1=8), V("vss", p1=8), 0, OP.is_equal)
 
-    for i in range(8):
+    now("front")
+    for i in range(8 - REP // 512):
         p = bank()
-        mm(V(p), V("E32", p1=32), V("fcb", 512 * i, 512 * i + 512, p1=32))
+        mm(V(p), V("E32", p1=32), V("CW", 8192 + 512 * i, 8704 + 512 * i, p1=32))
         copy(V("FR", 512 * i, 512 * i + 512), V(p))
 
-    def quarter(name, a, lo, hi):
-        return V(name, lo, hi, p0=32 * a, p1=32 * a + 32)
+    def tiled(dst, src, readers, w):
+        p = bank()
+        mms([(quarter(p, a, w * r, w * r + w), V("eye", 32 * r, 32 * r + 32), V(src, w * a, w * a + w), True, True)
+             for r in readers for a in range(4)])
+        copies([(V(dst, w * r, w * r + w), V(p, w * r, w * r + w)) for r in readers] if len(readers) < 4
+               else [(V(dst), V(p, 0, 4 * w))], "v")
 
+    now("lf")
+    if TILED:
+        copy(V("lf", 0, 32), V("tlc"), "v")
+        copy(V("lf", 32, 64), V("tlb"), "v")
     for r in ring:
-        lean[0] = LEAN["l2"]
-        copies([(quarter("L2", a, 16 * r, 16 * r + 16), quarter("tl" + "cb"[a // 2], r, 16 * (a % 2), 16 * (a % 2) + 16))
-                for a in range(4)], "v")
-        lean[0] = 0.0
+        now("l%d" % ((r - me) % N))
+        if not TILED:
+            copies([(quarter("L2", a, 16 * r, 16 * r + 16), quarter("tl" + "cb"[a // 2], r, 16 * (a % 2), 16 * (a % 2) + 16))
+                    for a in range(4)], "v")
+        elif r == ring[0]:
+            tiled("L2", "lf", list(range(4)), 16)
         pick(V("CB", 256 * r, 256 * r + 256), V("FR"), V("L2", 16 * r, 16 * r + 16))
         if r != me:
             send(r, V("CB", 256 * r, 256 * r + 256), T["LCB"][:, 256 * me:256 * me + 256], "c")
     expect("LCB", 256, "c")
-    for i in range(4):
-        zeros(V("zA", 1026 * i, 1026 * i + 1026))
+    for lo in range(ZA0, 4096, 1024):
+        zeros("zA", lo, min(lo + 1024, 4096))
+    diagonal(X("SEL", (every, every, 0, every), 0, 1), V("G"), [[-16, 8], [0, 4], [-1, 16]], 0)
+    diagonal(X("SEL", (every, slice(0, 4), 1, every), 1, 2), V("G", 0, 256), [[-16, 4], [0, 4], [-1, 16]], -64)
+    diagonal(X("SEL", (every, slice(4, 8), 1, every), 2, 3), V("G", 0, 256), [[-16, 4], [0, 4], [-1, 16]], 0)
+    zeros("zB", 0, ZB0)
 
-    dmas("dfe", [("y", group("far", b), H(T.fa[:, :])) for b in range(3, 8)], 5 << 17, [left("c")])
-    dmas("dfg", [("y", group("fag", b), H(T.fa[:, 512 * b:512 * b + 512])) for b in range(8)], 131072)
+    if NFA < 8:
+        dmas("dfe", [("y", group("far", b), H(T.fa[:, :])) for b in range(NFA, 8)], [left("c")])
 
-    lean[0] = LEAN["sel"]
-    for b in range(8):
-        scaled(V("SELB", 128 * b, 128 * b + 128), V("E"), col("rm8", b))
-    for b in range(8):
+    now("biasA")
+    one("v", [col("hf")], [V("rm8")], lambda q, x: q.tensor_reduce(col("hf")[5](), V("rm8", 1, 8, 2)[5](), AxisListType.X, OP.add))
+    tt(V("rm4"), V("rm8", 0, 8, 2), V("rm8", 1, 8, 2), OP.add)
+    line(col("b1"), col("hf"), 512.0, 264.0)
+    line(col("b2"), col("hf"), -512.0, 776.0)
+    copy(quarter("b2", me, 0, 1), quarter("b1", me, 0, 1))
+    for name, o, b in (("A", 0, "b3"), ("B", 4, "b4")):
+        line(col(b), col("b1"), col("E", o + 1))
+        line(col("b" + name), col("b2"), col("E", o + 2), col(b))
+    now("rs")
+    for name, o, c in (("A", 0, ("c0", "c1")), ("B", 4, ("c2", "c3"))):
         for h in (0, 1):
-            scaled(V("SEL", 128 * b + 64 * h, 128 * b + 64 * h + 64), V("E", 0, 64), col("rm8", (b + 4 * h) % 8))
-    lean[0] = LEAN["ss"]
-    ts(col("b1"), col("hf"), 512.0, OP.mult, 264.0, OP.add)
-    ts(col("b2"), col("hf"), -512.0, OP.mult, 776.0, OP.add)
+            line(col(c[h]), col("E", o), 1.0, col("E", o + 1 + h))
+            line(V("rs" + name, 4 * h, 4 * h + 4), V("rm4"), col(c[h]))
     for name, o in (("A", 0), ("B", 4)):
-        ts(col("b3"), col("b1"), col("E", o + 1), OP.mult)
-        ts(col("b" + name), col("b2"), col("E", o + 2), OP.mult, col("b3"), OP.add)
-        scaled(V("ss" + name), V("ramp"), col("E", o), col("b" + name))
-        for h in (0, 1):
-            ts(col("c%d" % h), col("E", o), col("E", o + 1 + h), OP.add)
-            ts(V("rs" + name, 4 * h, 4 * h + 4), V("rm4"), col("c%d" % h), OP.mult)
+        now("ss" + name)
+        line(V("ss" + name), V("Tab"), col("E", o), col("b" + name))
+    dmas("dfg", [("y", group("fag", b), H(T.fa[:, 512 * b:512 * b + 512])) for b in range(8)])
+    dmas("dtab", [("y", X("Tab", (slice(f, 128, 16), every), 0, 512), H(T["x" + "ab"[f]][:, :])) for f in (0, 1)])
 
     def places(t, dst, a, b, d, e):
-        ts(V(a), V(t), 0x1F0, OP.bitwise_and)
+        ts(V(a), V(t), 0x70, OP.bitwise_and)
         ts(V(b), V(t), 5, OP.arith_shift_right, 0x70, OP.bitwise_and)
-        ts(V(d), V(t), 15, OP.bitwise_and)
-        ts(V(a), V(a), 8, OP.mult)
-        tt(V(b), V(a), V(b), OP.add)
-        tt(V(e), V(b), V(d), OP.add)
+        tt(V(d), V(a), V(b), OP.subtract)
+        ts(V(d), V(d), 31, OP.mult)
+        tt(V(e), V(d), V(t), OP.add)
         copy(V(dst), V(e), "v")
 
-    def runs(x, w, yl, sn, tr, snu, off, fl):
-        a, b, c, d, e = w.split()
-        fill(V(yl, 32, 40), 0.0)
-        ts(V(a), V(x), 0xC9F, OP.bitwise_and)
-        ts(V(b), V(x), 3, OP.arith_shift_right, 0x60, OP.bitwise_and)
-        ts(V(c), V(x), 0x60, OP.bitwise_and)
-        ts(V(d), V(c), 8, OP.mult, 1, OP.add)
-        tt(V(e), V(a), V(b), OP.add)
-        tt(V(yl, 0, 32), V(e), V(d), OP.add)
+    def runs(x, yl, sn, tr, snu, off, fl):
+        copy(V(yl, 0, 32), x, "v")
         p = bank()
         mms([(V(p, 0, 32), V("N1"), V(yl, 0, 32), True, False), (V(p, 0, 32), V("N2"), V(yl, 1, 33), False, True)])
         tt(V(sn), V(p, 0, 32), V(yl, 0, 32), OP.is_equal)
         copy(V(snu), V(sn), "v")
+        pick(V(fl, 8, 520), V("w01"), V(snu))
         tt(V(tr), V(sn), V("trash"), OP.mult)
         tt(V(tr), V(tr), V(yl, 0, 32), OP.max)
         copy(V(off), V(tr), "v")
-        fill(V(fl, 0, 8), 0.0)
-        pick(V(fl, 8, 520), V("w01"), V(snu))
 
-    def lists(src, at, rs, dst):
+    def lists(src, rs, dst, parts):
         p = bank()
-        mms([(V(p, k, 256, 32), V(src, 128 * at[k], 128 * at[k] + 128), V(rs), True, True) for k in range(32)])
+        at = [128 * (4 * (k % 8) + k // 8) for k in range(32)]
+        for i, name in enumerate(parts):
+            now(name)
+            mms([(V(p, k, 256, 32), V(src, at[k], at[k] + 128), V(rs), True, True) for k in range(32)
+                 if k % 8 * len(parts) // 8 == i])
         copies([(V(dst, **low), V(p, 0, 128, **low)), (V(dst, **high), V(p, 128, 256, **high))], "v")
 
-    lean[0] = LEAN["vex"]
-    p = bank()
-    mm(V(p), V("vsel", p1=8), V("v8", p1=8))
-    copy(V("vex"), V(p))
-    lean[0] = LEAN["list"]
-    runs("txa", "ca cb cc cd ce", "yl", "sa", "ta", "snA", "offA", "flA")
-    lean[0] = LEAN["jc"]
-    copy(V("jc"), V("txc"), "v")
-    copy(V("jb"), V("txb"), "v")
-    lean[0] = LEAN["fas"]
-    for r in range(4):
+    now("vex")
+    if not VDMA:
+        p = bank()
+        mm(V(p), V("vsel", p1=8), V("v8", p1=8))
+        copy(V("vex"), V(p))
+    now("runsA")
+    runs(V("txa"), "yl", "sa", "ta", "snA", "offA", "flA")
+    now("jc")
+    ts(col("hu"), col("Di"), 192, OP.is_ge, 4096, OP.mult)
+    ts(V("jc"), V("txc"), col("hu"), OP.add)
+    ts(V("jb"), V("txb"), col("hu"), OP.add)
+    now("la")
+    if TILA:
+        copy(V("laf"), V("tla"), "v")
+        tiled("La", "laf", list(range(4)), 8)
+    for r in range(0 if TILA else 4):
         copies([(quarter("La", a, 8 * r, 8 * r + 8), quarter("tla", r, 8 * a, 8 * a + 8)) for a in range(4)], "v")
-    lean[0] = LEAN["inv"]
-    places("tla", "pia", "ba", "bb", "bd", "pii")
-    copy(V("pif"), V("pii"), "v")
-    lean[0] = LEAN["wf"]
-    for i in range(4):
-        fill(V("W", 1024 * i, 1024 * i + 1024), 0.0)
-    lean[0] = LEAN["inv"]
+    now("placeA")
+    places("tla", "pia", "ba", "bb", "bd", "pif")
+    now("wf0")
+    for i in range(8):
+        if i == WF0:
+            now("wf1")
+        fill(V("W", 512 * i, 512 * i + 512), 0.0)
+    now("putA")
     put(V("W"), V("pia"), V("ssA"))
+    now("tm")
     for b in range(8):
-        scaled(("tm", b, b + 1, 0, 128, lambda b=b: T["tm"][:, b // 2, :, b % 2, :], 32), V("pif"), col("rm8", b))
+        scaled(X("tm", (every, b // 2, every, b % 2, every), b, b + 1), V("pif"), col("rm8", b))
     p = bank()
-    mm(V(p, 0, 256), V("E"), ("tm", 0, 8, 0, 128, lambda: T["tm"][:, :, :, :, :], 256))
-    for k in range(8):
-        copy(V("Lr", 32 * k, 32 * k + 32), V(p, k, 256, 8), "v")
-    lean[0] = LEAN["r"]
+    now("tmm")
+    w = 8 // TM
+    mms([(V(p, 32 * k, 32 * k + 32 * w), V("E"), X("tm", (every,) * 4 + (slice(k, k + w),)), True, True) for k in range(0, 8, w)])
+    now("lr")
+    if w == 1:
+        copy(V("Lr"), V(p, 0, 256), "v")
+    else:
+        copies([(V("Lr", 32 * k, 256, 1) if 0 else V("Lr", 32 * k, 32 * k + 32),
+                 V(p, 32 * w * (k // w) + k % w, 32 * w * (k // w + 1), w)) for k in range(8)], "v")
+    now("r")
     for i in range(8):
         pick(V("R", 512 * i, 512 * i + 512), V("W"), V("Lr", 32 * i, 32 * i + 32))
-    lists("R", [(i % 8) * 4 + i // 8 for i in range(32)], "rsA", "idx")
-    lean[0] = LEAN["ya"]
-    lists("W", list(range(32)), "rsA", "inva")
-    lean[0] = 0.0
+    lists("R", "rsA", "idx", ["idx0", "idx1", "idx2", "idx"])
+    lists("W", "rsA", "inva", ["inva"])
 
     for n, q in enumerate(come):
         buf = "CB" if q == me else "LCB"
-        for f, win in ((0, "Cw"), (1, "Bw")):
-            for h in range(2):
-                p = bank()
-                mms([(V(p, 256 * c, 256 * c + 256), V("SELB", 128 * (4 * f + 2 * c + h), 128 * (4 * f + 2 * c + h) + 128),
-                      V(buf, 256 * q, 256 * q + 256), True, True) for c in range(2)])
-                copy(V(win, 1024 * q + 512 * h, 1024 * q + 512 * h + 512), V(p))
-    pick2(V("vc"), V("Cw"), V("jc"), V("vex"), OP.mult)
-    pick2(V("w1"), V("Bw"), V("jb"), V("vc"), OP.mult)
+        now("x" + str(n))
+        for h in range(2):
+            p, at = bank(), 4096 + 1024 * q + 512 * h
+            mms([(V(p, 256 * c, 256 * c + 256), X("SELB", (every, 2 * c + h, every, every)), V(buf, 256 * q, 256 * q + 256),
+                  True, True) for c in range(2)])
+            copy(V("CW", at, at + 512), V(p))
+        for name, dx, src, dst in (("c", 4096, low, high), ("b", -4096, high, low)):
+            now(name + str(n))
+            w = 512 * FINE[n]
+            for at in range(4096 + 1024 * q, 5120 + 1024 * q, w):
+                copy(V("CW", at + dx, at + dx + w, **dst), V("CW", at, at + w, **src))
+    now("vc")
+    pick2(V("vc"), X("CW", (every, slice(4096, 12288)), 4096, 12288), V("jc"), V("vex"), OP.mult)
 
     def addruns(src, fl, off, z, scn):
         o, a, b = V(scn), V(fl, 7, 519), V(src)
-        one("v", [o], [a, b], lambda q, x: q.tensor_tensor_scan(o[5](), a[5](), b[5](), 0.0, OP.mult, OP.add), {"v": cyc(512)})
+        one("v", [o], [a, b], lambda q, x: q.tensor_tensor_scan(o[5](), a[5](), b[5](), 0.0, OP.mult, OP.add))
         put(V(z), V(off), V(scn))
 
-    def reduce(z, land, sem, PT):
-        for q in ring:
-            lean[0] = LEAN["pw" if q == me else "red"]
+    def reduce(z, land, sem, PT, win, name):
+        now("red" + name)
+        for q in ring[:3]:
             p = bank()
-            mms([(V(p, 16 * b, 16 * b + 16), V(z, 1 + 1024 * q + 128 * b, 129 + 1024 * q + 128 * b), V("E", 0, 16), True, True)
+            mms([(V(p, 16 * b, 16 * b + 16), V(z, 1024 * q + b, 1024 * q + 1024, 8), V("E", 0, 16), True, True)
                  for b in range(8)])
             turned(V(PT, 128 * q, 128 * q + 128), V(p, 0, 128))
-            if q != me:
-                send(q, V(PT, 128 * q, 128 * q + 128), T[land][:, 128 * me:128 * me + 128], sem)
-        lean[0] = 0.0
+            send(q, V(PT, 128 * q, 128 * q + 128), T[land][:, 128 * me:128 * me + 128], sem)
+        now("own" + name)
+        for h in range(2):
+            p = bank()
+            mm(V(p), V("E"), V(z, 1024 * me + 512 * h, 1024 * me + 512 * h + 512))
+            copy(V(win + str(me), 8 + 512 * h, 520 + 512 * h), V(p))
         expect(land, 128, sem)
 
-    def spread(buf, q, win, at, dx, full):
-        for m in range(4):
-            src = V(buf, 128 * q, 128 * q + 128)
-            p = bank()
-            mm(V(p, 0, 128), V("SEL", 128 * m, 128 * m + 128), src)
-            here, there = (at[m], at[m] + 128), (at[m] + dx, at[m] + dx + 128)
-            if m < full:
-                copy(V(win, *here), V(p, 0, 128))
+    def spread(buf, q, win, at, dx, parts, full):
+        src = V(buf, 128 * q, 128 * q + 128)
+        for ms, how in zip(parts, full):
+            w = 128 * len(ms)
+            here, there = (at[ms[0]], at[ms[0]] + w), (at[ms[0]] + dx, at[ms[0]] + dx + w)
+            for x, to in ((0, here), (4, there))[:2 if how == "t" else 1]:
                 p = bank()
-                mm(V(p, 0, 128), V("SEL", 128 * (m + 4), 128 * (m + 4) + 128), src)
-                copy(V(win, *there), V(p, 0, 128))
-            else:
-                copies([(V(win, *here), V(p, 0, 128)), (V(win, *there, **low), V(p, 0, 128, **high)),
-                        (V(win, *there, **high), V(p, 0, 128, **low))])
+                mms([(V(p, 128 * j, 128 * j + 128), X("SEL", (every, m + x, every, every)), src, True, True)
+                     for j, m in enumerate(ms)])
+                if how == "p":
+                    copies([(V(win, *here), V(p, 0, w)), (V(win, *there, **low), V(p, 0, w, **high)),
+                            (V(win, *there, **high), V(p, 0, w, **low))])
+                else:
+                    copy(V(win, *to), V(p, 0, w))
+            if how == "s":
+                copy(V(win, *there, **low), V(win, *here, **high))
+                copy(V(win, *there, **high), V(win, *here, **low))
 
     def sums(buf, n, win, sem):
-        spread(buf, come[n], win + str(come[n]), [8 + 128 * m for m in range(4)], 512, FULL[sem][n])
+        full = FULL[sem][n]
+        w = 4 // len(full)
+        now(sem + str(n))
+        spread(buf, come[n], win + str(come[n]), [8 + 128 * m for m in range(4)], 512,
+               [range(i, i + w) for i in range(0, 4, w)], full)
 
     def factor(buf, n):
-        q = come[n]
-        spread(buf, q, "Aw", [1024 * q + 512 * (m % 2) + 128 * (m // 2) for m in range(4)], 256, FULL["n"][n])
+        q, full = come[n], FULL["n"][n]
+        now("n" + str(n))
+        spread(buf, q, "Aw", [1024 * q + 512 * (m % 2) + 128 * (m // 2) for m in range(4)], 256,
+               [(0, 2), (1, 3)] if len(full) == 2 else [(m,) for m in range(4)], full)
 
+    now("w1")
+    pick2(V("w1"), V("CW", 0, 8192), V("jb"), V("vc"), OP.mult)
     addruns("w1", "flA", "offA", "zA", "scn")
-    reduce("zA", "LP", "p", "PT")
-    zeros(V("zB", 0, ZB1))
+    reduce("zA", "LP", "p", "PT", "pw", "A")
+    zeros("zB", ZB0, ZB1)
 
     def gather(win, n, lst, acc, lo=0, hi=32):
         q = come[n]
@@ -616,88 +622,116 @@ def rank_program(g, core, T, topo):
         else:
             pick2(o, w, l, V(acc + str(n - 1), 16 * lo, 16 * hi), OP.add)
 
-    for q in range(4):
-        fill(V("pw%d" % q, 0, 8), 0.0)
-        fill(V("qw%d" % q, 0, 8), 0.0)
-    lean[0] = LEAN["fas"]
+    now("fas")
     pick(V("faS"), V("far"), V("La"))
-    lean[0] = 0.0
     for n in range(4):
-        sums("LP" if n else "PT", n, "pw", "p")
+        if n:
+            sums("LP", n, "pw", "p")
         if n < 3:
+            now("ac%d" % n)
             gather("pw", n, "idx", "ac")
+    now("ot")
     for r in ring[:OWN] + [me] + ring[OWN:3]:
         lo, hi = 128 * r, 128 * r + 128
-        lean[0] = LEAN["own"] if r == me else 0.0
         gather("pw", 3, "idx", "ac", 8 * r, 8 * r + 8)
         tt(V("OT", lo, hi), V("ac3", lo, hi), V("faS", lo, hi), OP.mult)
         if r != me:
             send(r, V("OT", lo, hi), T["LA"][:, 128 * me:128 * me + 128], "n")
-    lean[0] = 0.0
     expect("LA", 128, "n")
-    zeros(V("zB", ZB1, 4104))
+    zeros("zB", ZB1, 4096)
 
-    lean[0] = LEAN["lb"]
+    now("ob")
     ts(V("oa"), V("tob"), 15, OP.bitwise_and)
     ts(V("oc"), V("tob"), 4, OP.arith_shift_right)
     ts(V("oa"), V("oa"), 32, OP.mult)
     tt(V("od"), V("oa"), V("oc"), OP.add)
-    copies([(V("jq", h, 32, 2), V("od", 16 * h, 16 * h + 16)) for h in (0, 1)], "v")
+    copies([(V("jq", h, 32, 2), V("od", 16 * h, 16 * h + 16)) for h in (0, 1)] + [(V("jo"), V("tob"))], "v")
+    now("tab")
     pick(V("G"), V("Tab"), V("jq"))
-    turned(X("T4", lambda: T["T4"][:, :, :, :], 512), V("G"))
+    now("turn")
+    turned(X("T4", (every,) * 4), V("G"))
     for h in (0, 1):
-        turned(("T1", h, h + 1, 0, 128, lambda h=h: T["T1"][:, h, :, :], 32), X("T4", lambda h=h: T["T4"][:, :, h, 0:2], 32))
+        turned(X("T1", (every, h, every, every), h, h + 1), X("T4", (every, every, h, slice(0, 2))))
     for h in (0, 1):
-        turned(V("F", 32 * h, 32 * h + 32), ("T1", 0, 2, 0, 128, lambda h=h: T["T1"][:, :, h, :], 32))
-    copy(V("nB"), V("F", 1, 64, 2), "v")
-    runs("nB", "da db dc dd de", "ym", "sb", "tb", "snB", "offB", "flB")
+        turned(V("F", 32 * h, 32 * h + 32), X("T1", (every, every, h, every)))
+    now("runsB")
+    runs(V("F", 1, 64, 2), "ym", "sb", "tb", "snB", "offB", "flB")
+    now("ja")
     copy(V("nA", **high), V("F", 0, 64, 2, **high), "v")
     ts(V("nx", **high), V("nA", **high), 256, OP.bitwise_and)
     ts(V("ny", **high), V("nx", **high), -2, OP.mult, 256, OP.add)
     tt(V("nz", **high), V("ny", **high), V("F", 0, 64, 2, **high), OP.add)
     copies([(V("ja", **low), V("F", 0, 64, 2, **low)), (V("ja", **high), V("nz", **high))], "v")
-    lean[0] = LEAN["vco"]
-    copy(V("jo"), V("tob"), "v")
+    now("vco")
     pick(V("vco"), V("vc"), V("jo"))
-    lean[0] = LEAN["ib"]
+    now("placeB")
     places("tlb", "pib", "be", "bf", "bg", "pij")
-    put(V("W"), V("pib"), V("ssB"))
-    lists("W", list(range(32)), "rsB", "invb")
+    now("putB")
+    for lo in range(0, 32, 32 // IB):
+        put(V("W"), V("pib", lo, lo + 32 // IB), V("ssB", 16 * lo, 16 * lo + 512 // IB))
+    lists("W", "rsB", "invb", ["invb"])
 
-    lean[0] = LEAN["ya"]
-    for n in range(4):
-        gather("pw", n, "inva", "ya")
-    tt(V("yo"), V("ya3"), V("fag"), OP.mult)
-    dmas("dya", [("y", H(T.ya[:, 512 * b:512 * b + 512]), group("yo", b)) for b in range(8)], 262144)
-    lean[0] = 0.0
+    now("ya0")
+    gather("pw", 0, "inva", "ya")
+    if YA == 0:
+        for n in (1, 2, 3):
+            pick(V("ya%d" % n), V("pw%d" % come[n]), V("inva", 32 * come[n], 32 * come[n] + 32))
+        now("ya")
+        p = bank()
+        for n in range(4):
+            mms([(V(p), V("eye"), V("ya%d" % n), n == 0, n == 3)])
+        tt(V("yo"), V(p), V("fag"), OP.mult)
+    now("ya")
+    for lo in range(0, 32, 32 // YA) if YA else ():
+        hi = lo + 32 // YA
+        for n in (1, 2, 3):
+            gather("pw", n, "inva", "ya", lo, hi)
+        tt(V("yo", 16 * lo, 16 * hi), V("ya3", 16 * lo, 16 * hi), V("fag", 16 * lo, 16 * hi), OP.mult)
 
     for n in range(4):
         factor("LA" if n else "OT", n)
+    now("w2")
     pick2(V("w2"), V("Aw"), V("ja"), V("vco"), OP.mult)
     addruns("w2", "flB", "offB", "zB", "scm")
-    reduce("zB", "LQ", "q", "PU")
+    reduce("zB", "LQ", "q", "PU", "qw", "B")
+    dmas("dya", [("y", H(T.ya[:, 512 * b:512 * b + 512]), group("yo", b)) for b in range(8)], [left("q")] if YAG else [])
 
     for n in range(4):
-        sums("LQ" if n else "PU", n, "qw", "q")
+        if n:
+            sums("LQ", n, "qw", "q")
+        now("yb%d" % n)
         if n < 3:
             gather("qw", n, "invb", "yb")
-    for h in (0, 1):
-        gather("qw", 3, "invb", "yb", 16 * h, 16 * h + 16)
-        dmas("dyb%d" % h, [("ys"[b % 2], H(T.yb[:, 512 * b + 256 * h:512 * b + 256 * h + 256]),
-                            group("yb3", b, 256 * h, 256 * h + 256)) for b in range(8)], 131072)
+    for h in range(YB):
+        lo, hi = 512 * h // YB, 512 * (h + 1) // YB
+        gather("qw", 3, "invb", "yb", lo // 16, hi // 16)
+        dmas("dyb%d" % h, [("ys"[b % 2], H(T.yb[:, 512 * b + lo:512 * b + hi]), group("yb3", b, lo, hi)) for b in range(8)])
 
-    for i, e, at in order(ops):
-        where.update(at)
+    users = {}
+    for o in ops:
+        for n in {v[0] for v in o["outs"] + o["ins"] if v[0] and v[0][0] == "#"}:
+            users[n] = users.get(n, 0) + 1
+    free = list(banks)
+    for i in order(ops):
         o = ops[i]
+        tiles = {v[0] for v in o["outs"] + o["ins"] if v[0] and v[0][0] == "#"}
+        for n in tiles:
+            if n not in where:
+                assert free, "no bank"
+                where[n] = free.pop(0)
         if o["kind"] == "c":
             for outs, ins, call in o["subs"]:
-                emit(e, outs, ins, call)
+                emit(o["eng"], outs, ins, call)
         elif o["kind"] == "dma":
             emit_dmas(*o["subs"])
         elif o["kind"] == "send":
             emit_send(*o["subs"])
         else:
             emit_come(*o["subs"])
+        for n in tiles:
+            users[n] -= 1
+            if not users[n]:
+                free.append(where[n])
     for sem, n in count.items():
         if waited.get(sem, 0) < n:
             g.wait_ge(T.sem[sem], n)

@@ -5,19 +5,19 @@ COPY = ActivationFunctionType.Copy
 IDENTITY = ActivationFunctionType.Identity
 ZW = 4728
 SIZES = {
-    "int32": {128: "Di Ei", 32: "tla tlb tlc txa txb txc tob", 512: "Tab"},
+    "int32": {128: "Di Ei", 32: "tla tlb tlc txa txb txc tob", 512: "Tab ramp"},
     "uint16": {256: "Lr"},
     "bfloat16": {128: "E32", 512: "ssA ssB fag", 1024: "CB LCB", 4096: "FR far W R", 12288: "CW"},
-    "float32": {128: "E vsel N1 N2 eye", 9 * 1032 + 520: "win",
-                512: "v8 vex vc vco w1 w2 scn scm PT PU LP OT LA LQ faS ac0 ac1 ac2 ac3 ya0 ya1 ya2 ya3 yo G yb0 yb1 yb2 yb3",
+    "float32": {128: "E N1 N2 eye", 9 * 1032 + 520: "win",
+                512: "vex vc vco w1 w2 scn scm PT PU LP OT LA LQ faS ac0 ac1 ac2 ac3 ya0 ya1 ya2 ya3 yo G yb0 yb1 yb2 yb3",
                 4096: "Aw", ZW: "zA zB"},
 }
 SMALL = {
-    "int32": {8: "kgi kgs", 32: "ba bb be bf pij ca cb cc da db dc oa oc od nA nB nx"},
-    "uint16": {32: "La ja jb jc jo jq pia pib snA snB offA offB", 64: "L2", 128: "idx inva invb"},
+    "int32": {8: "kgi kgs", 32: "be bf pij oa oc od nA nx kp"},
+    "uint16": {32: "La ja jb jc jo jp jq pia pib snA snB offA offB", 64: "L2", 128: "idx inva invb"},
     "bfloat16": {8: "rsA rsB"},
-    "float32": {4: "rm4 hf hu n0 b1 b2 b3 b4 bA bB c0 c1 c2 c3", 8: "rm8 w01",
-                32: "trash pif sa ta sb tb bd bg cd ce dd de ny nz laf", 40: "yl ym", 64: "F lf"},
+    "float32": {4: "rm4 hf hu p16 n0 b1 b2 b3 b4 bA bB c0 c1 c2 c3", 8: "rm8 w01",
+                32: "trash pif sa ta sb tb bg ny nz", 40: "yl ym", 64: "F lf"},
 }
 SCRATCH = {n: ("sbuf", [128, c], d) for d, x in SIZES.items() for c, names in x.items() for n in names.split()}
 PLACE = {}
@@ -30,7 +30,7 @@ for _d, _x in SMALL.items():
     SCRATCH["small_" + _d] = ("sbuf", [128, _at], _d)
 for _i, _n in enumerate("pw0 pw1 pw2 pw3 qw0 qw1 qw2 qw3 flA flB".split()):
     PLACE[_n] = ("win", 1032 * _i, 1032 if _i < 8 else 520)
-SCRATCH["SEL"] = ("sbuf", [128, 8, 2, 64], "float32")
+SCRATCH["SEL"] = ("sbuf", [128, 4, 2, 64], "float32")
 SCRATCH["SELB"] = ("sbuf", [128, 4, 2, 64], "bfloat16")
 SCRATCH["tm"] = ("sbuf", [128, 4, 4, 2, 8], "float32")
 SCRATCH["T4"] = ("sbuf", [128, 16, 2, 16], "float32")
@@ -39,45 +39,35 @@ for _b in range(8):
     SCRATCH["pb%d" % _b] = ("psum", [128, 512], "float32")
 ENG = {"v": "sv", "s": "ss", "t": "st", "g": "sg"}
 SEMAPHORES = (list(ENG.values()) + ["dt" + t for t in ("la", "lb", "lc", "xa", "xb", "xc", "ob")]
-              + ["df%d" % i for i in range(4)] + ["drep", "dv", "dfa", "dfe", "dfg", "dtab", "dya", "dyb0", "dyb1"]
-              + ["l" + k for k in "cpnq"] + ["%s%d" % (k, d) for k in "cpnq" for d in (1, 2, 3)])
+              + ["df0", "df1", "df2", "df3", "drep", "dv", "dfa", "dfg", "dramp", "dtab", "dw"]
+              + ["d" + k + str(n) for k in "cb" for n in range(3)] + ["dx%d" % i for i in range(1, 11)]
+              + ["dya", "dyb0", "dyb1"] + ["l" + k for k in "cpnq"] + ["%s%d" % (k, d) for k in "cpnq" for d in (1, 2, 3)])
+
 PLAN = {
-    "start": (0.0, 0.01, "v"), "za": (0.5, 0.5, "s"), "biasA": (1.0, 0.01, "v"), "wf0": (1.5, 0.2, "v"), "ssA": (2.2, 0, "v"),
-    "front": (2.3, 0.14, "svsvsvss"), "l1": (4.1, 0.1, "s"), "l2": (4.4, 0.1, "s"), "l3": (6.3, 0.1, "s"), "l0": (6.6, 0.1, "s"),
-    "placeA": (4.6, 0.01, "v"), "wf1": (4.8, 0.01, "v"), "putA": (5.5, 0, "v"), "c0": (7.0, 0.05, "s"), "b0": (7.5, 0.05, "s"),
-    "vex": (5.6, 0.01, "s"), "next": (7.0, 0.01, "v"), "runsA": (7.4, 0.01, "s"), "jc": (9.0, 0.01, "v"), "tm": (6.0, 0.01, "s"),
-    "lr": (8.9, 0, "v"), "c1": (9.1, 0.05, "sv"), "b1": (9.6, 0.05, "sv"), "c2": (10.3, 0.05, "sv"), "b2": (10.8, 0.05, "sv"),
-    "c3": (11.5, 0.05, "sv"), "b3": (12.0, 0.05, "s"), "vc": (12.1, 0, "v"), "w1": (12.9, 0.5, "v"), "r": (13.0, 0.75, "s"),
-    "rs": (1.5, 0.01, "s"), "zero": (8.85, 0.01, "v"), "redA": (15.5, 0.3, "v"), "la": (16.5, 0.3, "v"), "ownA": (18.5, 0.3, "vv"),
-    "idx": (19.0, 0.5, "v"), "fas": (19.1, 0, "s"), "ac0": (20.2, 0, "v"), "p1": (19.8, 0.1, "s"), "ac1": (21.2, 0, "v"),
-    "p2": (20.6, 0.1, "s"), "ac2": (22.0, 0, "v"), "p3": (21.8, 0.1, "sv"), "ot": (23.0, 0.2, "v"), "inva": (24.0, 0.3, "v"),
-    "ssB": (17.7, 0.01, "v"), "ob": (18.0, 0.01, "v"), "tab": (24.0, 0, "s"), "turn": (25.0, 0.01, "v"), "runsB": (25.5, 0.01, "s"),
-    "ja": (26.5, 0.01, "v"), "vco": (25.0, 0.01, "s"), "n0": (24.5, 0.2, "s"), "n1": (26.5, 0.1, "s"), "n2": (27.7, 0.1, "s"),
-    "n3": (28.9, 0.1, "sv"), "placeB": (27.0, 0.01, "v"), "putB": (27.5, 0.7, "v"), "invb": (31.0, 0.3, "v"), "w2": (30.0, 0.5, "v"),
-    "ya0": (30.5, 0.1, "s"), "ya": (34.1, 0.3, "v"), "redB": (33.5, 0.3, "v"), "ownB": (36.5, 0.3, "s"), "yb0": (37.5, 0, "s"),
-    "q1": (37.0, 0.1, "s"), "yb1": (38.5, 0, "v"), "q2": (38.2, 0.1, "s"), "yb2": (39.7, 0, "v"), "q3": (39.4, 0.1, "sv"),
-    "yb3": (40.5, 0.1, "v"), "lf": (3.5, 0, "v"),
+    "start": (0, 0, ""), "za": (0, 0, "sv"), "biasA": (0, 0.75, "s"), "next": (0, 0.01, ""), "selb": (0.6, 0.5, "s"),
+    "wf": (1, 0, "vsv"), "wd": (1, 0, ""), "vex": (2, 0, ""), "ramp": (2, 0, ""), "ssA": (2, 0, "s"),
+    "lf": (3, 0, ""), "front": (3, 0, "sv"), "rsA": (3, 0, "s"), "l1": (3, 0, "v"), "jc": (3.3, 0.15, ""),
+    "runsA": (3.4, 0.5, "s"), "l2": (4, 0, "s"), "l3": (4, 0, "s"), "placeA": (4, 0, ""), "zero": (4, 0.5, ""),
+    "lt": (4, 0, ""), "l0": (4, 0, "v"),
+    "tm": (4.5, 0, "sssv"), "putA": (5, 0, ""), "x0": (5, 0, "s"), "c0": (5, 0, ""), "b0": (5, 0, ""), "rows": (5.1, 0, ""),
+    "ob": (6, 0, ""), "tmm": (6, 0, ""), "lr": (6.6, 0, ""), "r0": (7, 0, "v"),
+    "x1": (7, 0, "s"), "c1": (7, 0, ""), "b1": (7, 0, ""), "x2": (7, 0.1, "s"), "c2": (7, 0, "v"), "b2": (7, 0, "v"),
+    "far": (7.2, 0, ""), "x3": (7.3, 0, "sv"), "c3": (7, 0, "sv"), "vc": (7, 0, ""), "la": (7.4, 0, ""), "b3": (7.5, 0, "s"),
+    "w1": (8, 0, ""), "r": (8, 0.5, "ssssssv"), "idx0": (9, 0, ""), "idx1": (10, 0, ""), "fag": (10, 0, ""), "tab": (10, 0, "s"),
+    "placeB": (10.7, 0.2, ""), "redA": (11.1, 0.1, ""), "turn": (11.5, 0, ""), "ownA": (12, 0, "s"), "ja": (13, 0, ""),
+    "fas": (14, 0, "s"), "idx2": (15, 0, ""), "idx3": (15, 0, ""), "ac0": (15, 0, "v"), "p1": (16, 0, "sv"), "p2": (17, 0, "s"),
+    "ac1": (18, 0, ""), "p3": (18.2, 0, "vs"), "ac2": (20, 0, ""), "ot": (22, 0.4, ""), "vco": (22, 0, "s"), "ssB": (23, 0, "s"),
+    "inva": (24.4, 0, ""), "runsB": (24.7, 0.4, "s"), "n0": (24.78, 0.15, "vs"), "rsB": (25, 0, "s"), "n1": (26, 0.5, "s"),
+    "n2": (28, 0, "sv"), "putB": (28, 0, ""), "n3": (28, 0, "sv"), "w2": (30, 0, ""), "jp": (31, 0, ""), "invb": (32, 0, ""),
+    "ya0": (32, 0, "s"), "redB": (33.11, 0.3, ""), "ya": (34, 0.4, ""), "yo": (35, 0, ""), "ownB": (36, 0, "s"),
+    "yb0": (37, 0, "v"), "q1": (37.3, 0, "svs"), "q2": (41, 0.15, "svs"), "yb1": (42, 0, ""), "q3": (42, 0.2, "svs"),
+    "yb2": (43, 0, ""), "yb3": (44, 0, ""),
 }
-FULL = {"p": ("", "pp", "pp", "ts"), "n": ("tt", "pp", "pp", "ts"), "q": ("", "pp", "pp", "ts")}
-FINE = (2, 2, 2, 1)
-CUTS = (0, 1024, 2048, 3072, 4096)
-NFA = 3
-OWN = 2
-WF0, ZA0, ZB0, ZB1 = 3, 1024, 512, 2048
-YA, YB, IB, YAG = 2, 2, 2, True
-PLAN.update({'start': (1.0, 0.01, 'ssvs'), 'za': (2.1, 0.5, 'svv'), 'biasA': (1.0, 0.01, 'vss'), 'wf0': (1.1, 0.2, 'v'), 'ssA': (1.95, 0, 'vs'), 'front': (2.05, 0.14, 'svsvsvss'), 'l1': (3.95, 0.15, 's'), 'l2': (4.4, 0.1, 'sssv'), 'l3': (5.05, 0.1, 'sv'), 'l0': (4.06, 0.1, 's'), 'placeA': (4.6, 0.3, 'sv'), 'wf1': (6.05, 0.01, 'vs'), 'putA': (5.4, 0, 'v'), 'c0': (7.45, 0.05, 's'), 'b0': (4.6, 0.05, 's'), 'vex': (4.95, 0.5, 'sssv'), 'next': (6.9, 0.4, 'sssv'), 'runsA': (7.05, 0, 'svs'), 'jc': (9.35, 0.01, 'vs'), 'tm': (7.4, 0.01, 's'), 'lr': (9.65, 0, 'ssvs'), 'c1': (9.75, 0.05, 'sv'), 'b1': (10.1, 0.01, 'sv'), 'c2': (10.3, 0.05, 'sv'), 'b2': (10.7, 0.05, 'sv'), 'c3': (10.5, 0.3, 'vs'), 'b3': (12.25, 0.05, 'vs'), 'vc': (12.5, 0.3, 'vsss'), 'w1': (12.9, 0.5, 'sv'), 'r': (13.0, 0, 's'), 'rsA': (16.4, 0.05, 'v'), 'zero': (20.25, 0.15, 'svv'), 'redA': (15.4, 0.3, 's'), 'la': (15.5, 0.3, 'v'), 'ownA': (18.6, 0.15, 'vv'), 'idx': (19.35, 0.5, 'v'), 'fas': (17.1, 0.1, 'ssv'), 'ac0': (21.0, 0.75, 'v'), 'p1': (20.15, 0.01, 's'), 'ac1': (21.35, 0.3, 'v'), 'p2': (20.35, 0.1, 's'), 'ac2': (23.15, 0, 'v'), 'p3': (21.05, 0.1, 'sv'), 'ot': (23.0, 0.2, 'v'), 'inva': (24.0, 0.3, 'vsss'), 'ssB': (12.7, 0.75, 'sssv'), 'ob': (15.8, 0.2, 'sssv'), 'tab': (16.15, 0.75, 's'), 'turn': (20.5, 0.2, 'ssvs'), 'runsB': (26.6, 0.01, 's'), 'ja': (26.9, 0.01, 'ssv'), 'vco': (24.25, 0.01, 'sv'), 'n0': (25.0, 0.2, 'sssv'), 'n1': (28.0, 0, 'svs'), 'n2': (29.2, 0.2, 's'), 'n3': (31.6, 0.2, 'sv'), 'placeB': (26.9, 0.01, 'vsss'), 'putB': (27.9, 0.7, 'v'), 'invb': (33.4, 0.4, 'v'), 'w2': (28.1, 0.5, 'svs'), 'ya0': (32.5, 0.1, 'ssvs'), 'ya': (34.35, 0.3, 'v'), 'redB': (33.6, 0.3, 'vsss'), 'ownB': (35.15, 0.1, 's'), 'yb0': (33.1, 0, 'sssv'), 'q1': (37.25, 0.1, 'v'), 'yb1': (39.15, 0.01, 'ssvs'), 'q2': (37.8, 0.15, 'ssvs'), 'yb2': (41.65, 0, 'vsss'), 'q3': (40.0, 0.4, 'sssv'), 'yb3': (39.25, 0.1, 'v')})
-FULL = {'n': ('tp', 'pp', 'pp', 'pp'), 'q': ('', 'pp', 'ss', 'st'), 'p': ('', 'pp', 'tp', 'pt')}
-IB, WF0, YB, OWN, ZB1, YAG, YA, ZA0, ZB0, FINE = 1, 4, 2, 1, 1536, True, 1, 512, 0, (2, 2, 2, 2)
-NFA, TILED, YAG, YB = 2, True, False, 1
-PLAN = {'start': (0.0, 0.2, 'sv'), 'za': (0.0, 0.01, 's'), 'biasA': (0.5, 0.2, 'v'), 'wf0': (1.35, 0.2, 'ssv'), 'ssA': (3.35, 0.05, 'v'), 'front': (1.65, 0.14, 'svsvsvss'), 'l1': (4.2, 0, 'ssvs'), 'l2': (0.5, 0.1, 'svv'), 'l3': (7.15, 0.01, 'ssv'), 'l0': (4.96, 0.3, 'ssv'), 'placeA': (5.35, 0.3, 'svs'), 'wf1': (5.3, 0.5, 'svv'), 'putA': (4.9, 0.5, 'ssvs'), 'c0': (7.45, 0.05, 's'), 'b0': (7.25, 0.3, 'ssv'), 'vex': (4.7, 0.5, 'ssv'), 'next': (6.8, 0.4, 'vss'), 'runsA': (6.85, 0, 'svs'), 'jc': (6.65, 0.5, 'svv'), 'tm': (7.4, 0.01, 's'), 'lr': (9.4, 0.01, 'vs'), 'c1': (7.95, 0.01, 'svv'), 'b1': (10.85, 0, 'svv'), 'c2': (9.55, 0.05, 'sv'), 'b2': (10.2, 0.05, 'sv'), 'c3': (10.5, 0.3, 'vsss'), 'b3': (11.25, 0.1, 'vs'), 'vc': (7.5, 0.3, 'sssv'), 'w1': (12.15, 0.3, 'vss'), 'r': (14.25, 0, 's'), 'rs': (1.0, 0.4, 'vss'), 'zero': (1.05, 0.01, 'ssvs'), 'redA': (14.65, 0.3, 'vsss'), 'la': (12.75, 0.3, 'sssv'), 'ownA': (17.35, 0.1, 'vv'), 'idx': (17.6, 0.5, 'ssvs'), 'fas': (15.85, 0.75, 'vss'), 'ac0': (16.2, 0.75, 'v'), 'p1': (20.15, 0.01, 's'), 'ac1': (19.2, 0.4, 'sssv'), 'p2': (20.25, 0.1, 's'), 'ac2': (18.25, 0.01, 'vss'), 'p3': (21.15, 0.1, 'svs'), 'ot': (23.4, 0.4, 'vss'), 'inva': (24.0, 0.3, 'svs'), 'ssB': (12.7, 0.05, 'v'), 'ob': (15.55, 0.05, 'svs'), 'tab': (16.3, 0.75, 'sv'), 'turn': (19.65, 0.2, 'sssv'), 'runsB': (26.6, 0.01, 'ssvs'), 'ja': (26.65, 0.01, 'vs'), 'vco': (26.15, 0.1, 'ssv'), 'n0': (25.25, 0.01, 'sssv'), 'n1': (27.8, 0.4, 'vsss'), 'n2': (29.55, 0.2, 's'), 'n3': (31.75, 0.15, 'svv'), 'placeB': (26.65, 0.01, 'ssv'), 'putB': (27.45, 0, 'svv'), 'invb': (33.3, 0.15, 'v'), 'w2': (30.65, 0.75, 'svv'), 'ya0': (32.85, 0.15, 'sv'), 'ya': (34.2, 0.3, 'sssv'), 'redB': (33.6, 0.3, 's'), 'ownB': (34.6, 0.1, 'ssv'), 'yb0': (32.35, 0.3, 'sssv'), 'q1': (35.5, 0, 'v'), 'yb1': (37.4, 0.15, 'ssvs'), 'q2': (35.7, 0.2, 'sssv'), 'yb2': (41.9, 0.3, 'vsss'), 'q3': (40.25, 0.4, 'sssv'), 'yb3': (35.25, 0.05, 'v'), 'lf': (2.85, 0.3, 'vs')}
-FULL = {'n': ('pt', 'pp', 'tp', 'pp'), 'q': ('', 'pp', 'ss', 'st'), 'p': ('', 'pt', 'pt', 'pt')}
-NFA, WF0 = 3, 3
-TILA, VDMA, TM, REP = True, False, 8, 0
-PLAN.update({"idx0": (19.0, 0, "v"), "idx1": (19.0, 0, "v"), "idx2": (19.0, 0, "v"),
-             "tmm": (9.5, 0, "v"), "x0": (6, .1, "s"), "x1": (9, .1, "s"), "x2": (10.2, .1, "s"), "x3": (11.4, .1, "sv")})
-PLAN = {'start': (0.58, 0.05, 'vss'), 'za': (0.1, 0.01, 'sssv'), 'biasA': (0.83, 0.1, 's'), 'wf0': (1.1, 0.01, 'vsss'), 'ssA': (3.05, 0.3, 'sv'), 'front': (2.23, 0.01, 'svsvsvss'), 'l1': (3.67, 0.9, 'v'), 'l2': (4.27, 0.15, 's'), 'l3': (4.87, 0.15, 'svv'), 'l0': (3.65, 0.2, 's'), 'placeA': (4.6, 0.15, 'vs'), 'wf1': (4.62, 0.15, 'ssv'), 'putA': (6.12, 0, 'v'), 'c0': (6.38, 0, 'v'), 'b0': (6.37, 0.15, 'v'), 'vex': (0.02, 0.3, 'vss'), 'next': (0.8, 0.4, 's'), 'runsA': (4.65, 0.15, 'ssv'), 'jc': (5.46, 0.1, 'vsss'), 'tm': (5.73, 0.001, 's'), 'lr': (4.55, 0, 's'), 'c1': (1.65, 0.01, 'vs'), 'b1': (5.88, 0.15, 'v'), 'c2': (7.25, 0.01, 'svs'), 'b2': (5.22, 0.75, 'v'), 'c3': (7.49, 0.15, 'v'), 'b3': (7.79, 0, 'sssv'), 'vc': (5.49, 0.75, 'sssv'), 'w1': (3.43, 0.2, 'vs'), 'r': (12.18, 0.1, 'sssssvss'), 'rs': (1.0, 0.1, 'sssv'), 'zero': (1.05, 0.4, 'ssvs'), 'redA': (12.5, 0.1, 'ssv'), 'la': (7.77, 0.05, 'svv'), 'ownA': (13.04, 0.15, 'ssv'), 'idx': (18.49, 0, 'svv'), 'fas': (18.45, 0.2, 'vss'), 'ac0': (10.12, 0.1, 'vss'), 'p1': (18.73, 0.2, 'sv'), 'ac1': (20.2, 0.3, 'vss'), 'p2': (20.48, 0.15, 'ssv'), 'ac2': (21.32, 0.05, 's'), 'p3': (21.42, 0, 'ssv'), 'ot': (22.2, 0.4, 'sssv'), 'inva': (24.52, 0.3, 'vs'), 'ssB': (9.25, 0.5, 's'), 'ob': (13.18, 0.3, 's'), 'tab': (19.87, 0.75, 'svv'), 'turn': (19.53, 0.75, 'vsss'), 'runsB': (26.65, 0.01, 'sv'), 'ja': (26.52, 0.2, 'ssv'), 'vco': (21.8, 0.3, 'svs'), 'n0': (24.57, 0.01, 's'), 'n1': (27.12, 0.01, 'svs'), 'n2': (29.85, 0.2, 'ssvs'), 'n3': (32.13, 0.05, 'svv'), 'placeB': (26.63, 0.01, 'svs'), 'putB': (26.97, 0.2, 'ssvs'), 'invb': (32.7, 0.3, 'vss'), 'w2': (29.35, 0.75, 'svv'), 'ya0': (33.4, 0.1, 's'), 'ya': (33.82, 0.3, 'v'), 'redB': (33.18, 0.3, 'vs'), 'ownB': (38.45, 0.01, 's'), 'yb0': (23.7, 0.01, 'vsss'), 'q1': (38.77, 0.05, 'svv'), 'yb1': (44.6, 0.1, 'ssvs'), 'q2': (42.85, 0.15, 'ssv'), 'yb2': (45.9, 0.01, 'vsss'), 'q3': (47.05, 0.75, 'svv'), 'yb3': (42.33, 0.4, 'vs'), 'lf': (5.42, 0.2, 'sssv'), 'idx0': (6.8, 0, 'vsss'), 'idx1': (14.67, 0.4, 'vss'), 'idx2': (14.78, 0, 'v'), 'tmm': (7.78, 0.1, 'svs'), 'x0': (4.81, 0.15, 'ssv'), 'x1': (6.75, 0.05, 'sssv'), 'x2': (6.97, 0, 's'), 'x3': (7.35, 0.01, 'sv')}
-FULL = {'n': ('pp', 'pp', 'ps', 'ps'), 'q': ('', 'pp', 'sp', 'ps'), 'p': ('', 'sp', 'sp', 'ps')}
-TILED, TILA, TM, VDMA, NFA, ZA0, IB, ZB1, YB, FINE, ZB0, YA, WF0, REP, OWN = False, True, 8, True, 0, 512, 1, 1536, 1, (2, 2, 1, 1), 0, 1, 3, 0, 1
+CROSS = {"p": ("", "pp", "pp", "pp"), "n": ("dp", "dd", "pp", "pppp"), "q": ("", "pppp", "ppps", "pppp")}
+BY_DMA = ("c0", "b0", "c1", "b1")
+SPREAD = 1536
+FILLS = 4
+ZA, ZB = 1024, 2048
 
 
 def meet(a, b):
@@ -89,7 +79,7 @@ def covers(a, b):
 
 
 def order(ops):
-    turn, last, tail = [], {}, {}
+    turn, last, tail = [], {}, ()
     for i, op in enumerate(ops):
         pred = set(op["after"])
         both = [(v, True) for v in op["outs"] if v[0]] + [(v, False) for v in op["ins"] if v[0]]
@@ -100,10 +90,9 @@ def order(ops):
             if w:
                 rec[:] = [x for x in rec if not covers(v, x[0])]
             rec.append((v, w, i))
-        c = "g" if op["eng"] == "g" else "d" if op["kind"] == "dma" else None
-        if c:
-            pred.update(tail.get(c, ()))
-            tail[c] = (i,)
+        if op["eng"] == "g":
+            pred.update(tail)
+            tail = (i,)
         turn.append(max([op["turn"]] + [turn[j] for j in pred if j != i]))
     return sorted(range(len(ops)), key=lambda i: (turn[i], i))
 
@@ -121,7 +110,7 @@ def rank_program(g, core, T, topo):
     banks = {"pb%d" % b: {} for b in range(8)}
     where = {}
     ops = []
-    part = {"turn": 0.0, "step": 0.0, "queues": "v", "n": 0, "tiles": 0}
+    part = {"turn": 0.0, "step": 0.0, "queues": "", "n": 0, "tiles": 0, "dmas": 0}
     sent = {}
 
     def wait(e, tok):
@@ -179,13 +168,17 @@ def rank_program(g, core, T, topo):
         for e, o, i in items:
             after([o] if o[0] else [], [i] if i[0] else [], tok)
 
+    def engines(src, dst, sem):
+        first = sem == "c" and (T.rank_of(dst) - T.rank_of(src)) % N == 1
+        return topo.engines(src, dst)[::2 if first else 1]
+
     def emit_send(q, src, dst, sem):
         to = T.cores[q]
         before("g", [], [src])
         rid, pid, _ = topo.addr(to)
         g.remote_dma(out_ap=dst, in_ap=src[5](), remote_sem=T.sem["%s%d" % (sem, (q - me) % N)], local_sem=T.sem["l" + sem],
-                     pid=pid, routing_id=rid, dma_engine_mask=topo.mask(core, to))
-        count["l" + sem] = count.get("l" + sem, 0) + len(topo.engines(core, to))
+                     pid=pid, routing_id=rid, dma_engine_mask=sum(1 << e for e in engines(core, to, sem)))
+        count["l" + sem] = count.get("l" + sem, 0) + len(engines(core, to, sem))
 
     def emit_come(v, s, n):
         count[s] = n or count[s]
@@ -233,7 +226,7 @@ def rank_program(g, core, T, topo):
             eng = part["queues"][part["n"] % len(part["queues"])]
             part["n"] += 1
         ops.append({"eng": eng, "outs": outs, "ins": ins, "subs": subs, "kind": kind, "after": list(needs),
-                    "turn": part["turn"] if eng in "vst" else 0.0})
+                    "turn": part["turn"] if eng in "vsty" else 0.0})
         if eng in "vst":
             part["turn"] += part["step"]
         return len(ops) - 1
@@ -249,27 +242,27 @@ def rank_program(g, core, T, topo):
     def copy(o, i, e="vs"):
         copies([(o, i)], e)
 
-    def scaled(o, i, sc, b=None, e="vs"):
+    def line(o, i, a, b=0.0):
         def call(q, x):
+            a1 = a[5]() if isinstance(a, tuple) else a
+            b1 = b[5]() if isinstance(b, tuple) else b
             if x == "v":
-                if b is None:
-                    return q.tensor_scalar(o[5](), i[5](), sc[5](), None, OP.mult)
-                return q.tensor_scalar(o[5](), i[5](), sc[5](), b[5](), OP.mult, OP.add)
-            if b is None:
-                return q.activation(o[5](), i[5](), COPY, scale=sc[5]())
-            return q.activation(o[5](), i[5](), IDENTITY, bias=b[5](), scale=sc[5]())
-        one(e, [o], [i, sc] + ([b] if b else []), call)
+                return q.tensor_scalar(o[5](), i[5](), a1, b1, OP.mult, OP.add)
+            return q.activation(o[5](), i[5](), IDENTITY, bias=b1, scale=a1)
+        one("vs", [o], [i] + [s for s in (a, b) if isinstance(s, tuple)], call)
+
+    def nought(o):
+        one("vs", [o], [V("G")], lambda q, x: q.memset(o[5](), 0.0) if x == "v"
+            else q.activation(o[5](), V("G")[5](), COPY, scale=0.0))
 
     def ts(o, i, s1, op0, s2=None, op1=None):
-        rd = [i] + [s for s in (s1, s2) if isinstance(s, tuple)]
-
         def call(q, x):
             a1 = s1[5]() if isinstance(s1, tuple) else s1
             a2 = s2[5]() if isinstance(s2, tuple) else s2
             if op1 is None:
                 return q.tensor_scalar(o[5](), i[5](), a1, None, op0)
             return q.tensor_scalar(o[5](), i[5](), a1, a2, op0, op1)
-        one("v", [o], rd, call)
+        one("v", [o], [i] + [s for s in (s1, s2) if isinstance(s, tuple)], call)
 
     def tt(o, a, b, f):
         one("v", [o], [a, b], lambda q, x: q.tensor_tensor(o[5](), a[5](), b[5](), f))
@@ -279,20 +272,6 @@ def rank_program(g, core, T, topo):
 
     def fill(o, c):
         one("v", [o], [], lambda q, x: q.memset(o[5](), c))
-
-    def line(o, i, a, b=0.0):
-        rd = [i] + [s for s in (a, b) if isinstance(s, tuple)]
-
-        def call(q, x):
-            a1 = a[5]() if isinstance(a, tuple) else a
-            b1 = b[5]() if isinstance(b, tuple) else b
-            if x == "v":
-                return q.tensor_scalar(o[5](), i[5](), a1, b1, OP.mult, OP.add)
-            return q.activation(o[5](), i[5](), IDENTITY, bias=b1, scale=a1)
-        one("vs", [o], rd, call)
-
-    def eight(o, c):
-        line(o, V("E", 0, 8), 0.0, c)
 
     def ind(w, l):
         return w[5]().indirect(l[5]())
@@ -322,11 +301,13 @@ def rank_program(g, core, T, topo):
             one("g", [o], [], lambda q, x: q.iota(o[5](), pattern, base, cm, allow_small_or_imprecise_dtypes=True))
 
     def zeros(name, lo, hi):
-        if lo < hi:
-            iota(V(name, lo, hi), [[0, hi - lo]], 0, 0)
+        iota(V(name, lo, hi), [[0, hi - lo]], 0, 0)
 
     def diagonal(o, ones, pattern, base):
         one("g", [o], [ones], lambda q, x: q.affine_select(o[5](), ones[5](), pattern, OP.is_equal, 0.0, base, 1))
+
+    def selector(name, i):
+        diagonal(X(name, (every, every, i, every), i, i + 1), V("G", 0, 256), [[-16, 4], [0, 4], [-1, 16]], -64 * i)
 
     def dmas(sem, items, extra=()):
         outs = [o for _, o, _ in items if o[0]]
@@ -340,7 +321,7 @@ def rank_program(g, core, T, topo):
         for d in (1, 2, 3):
             q, s = (me - d) % N, "%s%d" % (sem, d)
             v = V(buf, q * width, (q + 1) * width)
-            op("-", [v], [], (v, s, len(topo.engines(T.cores[q], core))), "come", [sent[sem, d]])
+            op("-", [v], [], (v, s, len(engines(T.cores[q], core, sem))), "come", [sent[sem, d]])
 
     def left(sem):
         v = ("left" + sem, 0, 1, 0, 128, None)
@@ -355,52 +336,40 @@ def rank_program(g, core, T, topo):
     def table(t, e):
         dmas("dt" + t, [(e, V("t" + t), H(T[t][:, :]))])
 
-    for i, (lo, hi) in enumerate(zip(CUTS, CUTS[1:])):
-        hi = min(hi, 4096 - REP)
-        if lo < hi:
-            dmas("df%d" % i, [("y", V("CW", 8192 + lo, 8192 + hi, p0=0, p1=16), H(T.fc[:, lo:hi])),
-                              ("s", V("CW", 8192 + lo, 8192 + hi, p0=16, p1=32), H(T.fb[:, lo:hi]))])
+    for i, lo in enumerate(range(0, SPREAD, 1024)):
+        hi = min(lo + 1024, SPREAD)
+        dmas("df%d" % i, [("y", V("CW", 8192 + lo, 8192 + hi, p0=0, p1=16), H(T.fc[:, lo:hi])),
+                          ("s", V("CW", 8192 + lo, 8192 + hi, p0=16, p1=32), H(T.fb[:, lo:hi]))])
     table("lc", "y")
     table("lb", "s")
-    if REP:
-        dmas("drep", [("ys"[b % 2], group("FR", b, 4096 - REP, 4096), H(T["f" + "cb"[b // 4]][:, 4096 - REP:4096]))
-                      for b in range(8)])
-    for t in ("la", "xa"):
+    dmas("drep", [("ys"[b % 2], group("FR", b, SPREAD, 4096), H(T["f" + "cb"[b // 4]][:, SPREAD:4096])) for b in range(8)])
+    for t in ("la", "xa", "xc", "xb", "ob"):
         table(t, "y")
-    if not VDMA:
-        dmas("dv", [("y", V("v8", p0=0, p1=8), H(T.v[:, :]))])
-    for t in ("xc", "xb", "ob"):
-        table(t, "y")
-    if VDMA:
-        dmas("dv", [("y", X("vex", (slice(o, 128, 16), every), 0, 512), H(T.v[:, :])) for o in range(16)])
-    if NFA:
-        dmas("dfa", [("y", group("far", b), H(T.fa[:, :])) for b in range(NFA)])
+    now("vex")
+    dmas("dv", [("y", X("vex", (slice(o, 128, 16), every), 0, 512), H(T.v[:, :])) for o in range(16)])
 
     now("start")
     fill(V("G"), 1.0)
     iota(V("Di"), [[-1, 128]], 128, 1)
     iota(V("kgi"), [[-16, 8]], 0, 1)
     for a in (0, 1):
-        iota(V("Tab", 256 * a, 256 * a + 256), [[1, 32], [32, 4], [128, 2]], 256 * a - 256, 0)
-    iota(quarter("Tab", me, 0, 512), [[1, 512]], -256, 0)
-    if TILED or TILA or not YA:
-        diagonal(V("eye"), V("G", 0, 128), [[-1, 128]], 0)
-    if not VDMA:
-        diagonal(V("vsel", p1=8), V("G", 0, 128, p1=8), [[-1, 8], [0, 16]], 0)
+        iota(V("ramp", 256 * a, 256 * a + 256), [[1, 32], [32, 4], [128, 2]], 256 * a - 256, 0)
+    iota(quarter("ramp", me, 0, 512), [[1, 512]], -256, 0)
+    diagonal(V("eye"), V("G", 0, 128), [[-1, 128]], 0)
     iota(V("trash"), [[16, 32]], 4096, 1)
     iota(V("w01"), [[1, 8]], 0, 0)
-    for i in (0, 1):
-        diagonal(X("SELB", (every, every, i, every), i, i + 1), V("G", 0, 256), [[-16, 4], [0, 4], [-1, 16]], -64 * i)
     ts(V("Ei"), V("Di"), 15, OP.bitwise_and)
     ts(V("kgs"), V("kgi"), 4, OP.arith_shift_right)
     ts(V("E"), V("Ei"), 0, OP.is_equal)
     ts(V("rm8"), V("kgs"), 0, OP.is_equal)
     for f in (0, 1):
         ts(V("E32", 64 * f, 64 * f + 64), V("E", 0, 64), col("rm8", f), OP.mult)
+    now("selb")
+    for b in range(8):
+        line(X("SELB", (every, b % 4, b // 4, every), b, b + 1), V("E", 0, 64), col("rm8", b))
     now("za")
-    for lo in range(0, ZA0, 512):
-        one("vs", [V("zA", lo, lo + 512)], [V("G")], lambda q, x, o=V("zA", lo, lo + 512): q.memset(o[5](), 0.0) if x == "v"
-            else q.activation(o[5](), V("G")[5](), COPY, scale=0.0))
+    for lo in range(0, ZA, 512):
+        nought(V("zA", lo, lo + 512))
     now("zero")
     fill(V("yl", 32, 81, 48), -1.0)
     fill(V("win", 0, 8 * 1032, 1032), 0.0)
@@ -411,42 +380,39 @@ def rank_program(g, core, T, topo):
     ts(V("N2"), V("Di"), 113, OP.is_equal, col("E", 0), OP.mult)
 
     now("front")
-    for i in range(8 - REP // 512):
+    for lo in range(0, SPREAD, 512):
         p = bank()
-        mm(V(p), V("E32", p1=32), V("CW", 8192 + 512 * i, 8704 + 512 * i, p1=32))
-        copy(V("FR", 512 * i, 512 * i + 512), V(p))
+        mm(V(p), V("E32", p1=32), V("CW", 8192 + lo, 8704 + lo, p1=32))
+        copy(V("FR", lo, lo + 512), V(p))
 
     def tiled(dst, src, readers, w):
         p = bank()
         mms([(quarter(p, a, w * r, w * r + w), V("eye", 32 * r, 32 * r + 32), V(src, w * a, w * a + w), True, True)
              for r in readers for a in range(4)])
-        copies([(V(dst, w * r, w * r + w), V(p, w * r, w * r + w)) for r in readers] if len(readers) < 4
-               else [(V(dst), V(p, 0, 4 * w))], "v")
+        pieces = [[r for r in readers if r >= readers[0]], [r for r in readers if r < readers[0]]]
+        copies([(V(dst, w * x[0], w * x[-1] + w), V(p, w * x[0], w * x[-1] + w)) for x in pieces if x], "v")
 
     now("lf")
-    if TILED:
-        copy(V("lf", 0, 32), V("tlc"), "v")
-        copy(V("lf", 32, 64), V("tlb"), "v")
+    copy(V("lf", 0, 32), V("tlc"), "v")
+    copy(V("lf", 32, 64), V("tlb"), "v")
     for r in ring:
+        if r == ring[1]:
+            now("lt")
+            tiled("L2", "lf", ring[1:], 16)
         now("l%d" % ((r - me) % N))
-        if not TILED:
+        if r == ring[0]:
             copies([(quarter("L2", a, 16 * r, 16 * r + 16), quarter("tl" + "cb"[a // 2], r, 16 * (a % 2), 16 * (a % 2) + 16))
                     for a in range(4)], "v")
-        elif r == ring[0]:
-            tiled("L2", "lf", list(range(4)), 16)
         pick(V("CB", 256 * r, 256 * r + 256), V("FR"), V("L2", 16 * r, 16 * r + 16))
         if r != me:
             send(r, V("CB", 256 * r, 256 * r + 256), T["LCB"][:, 256 * me:256 * me + 256], "c")
     expect("LCB", 256, "c")
-    for lo in range(ZA0, 4096, 1024):
+    for lo in range(ZA, 4096, 1024):
         zeros("zA", lo, min(lo + 1024, 4096))
-    diagonal(X("SEL", (every, every, 0, every), 0, 1), V("G"), [[-16, 8], [0, 4], [-1, 16]], 0)
-    diagonal(X("SEL", (every, slice(0, 4), 1, every), 1, 2), V("G", 0, 256), [[-16, 4], [0, 4], [-1, 16]], -64)
-    diagonal(X("SEL", (every, slice(4, 8), 1, every), 2, 3), V("G", 0, 256), [[-16, 4], [0, 4], [-1, 16]], 0)
-    zeros("zB", 0, ZB0)
-
-    if NFA < 8:
-        dmas("dfe", [("y", group("far", b), H(T.fa[:, :])) for b in range(NFA, 8)], [left("c")])
+    for i in (0, 1):
+        selector("SEL", i)
+    now("far")
+    dmas("dfa", [("y", group("far", b), H(T.fa[:, :])) for b in range(8)], [left("c")])
 
     now("biasA")
     one("v", [col("hf")], [V("rm8")], lambda q, x: q.tensor_reduce(col("hf")[5](), V("rm8", 1, 8, 2)[5](), AxisListType.X, OP.add))
@@ -454,27 +420,21 @@ def rank_program(g, core, T, topo):
     line(col("b1"), col("hf"), 512.0, 264.0)
     line(col("b2"), col("hf"), -512.0, 776.0)
     copy(quarter("b2", me, 0, 1), quarter("b1", me, 0, 1))
-    for name, o, b in (("A", 0, "b3"), ("B", 4, "b4")):
+    for name, o, b, c in (("A", 0, "b3", ("c0", "c1")), ("B", 4, "b4", ("c2", "c3"))):
+        now("ss" + name)
         line(col(b), col("b1"), col("E", o + 1))
         line(col("b" + name), col("b2"), col("E", o + 2), col(b))
-    now("rs")
-    for name, o, c in (("A", 0, ("c0", "c1")), ("B", 4, ("c2", "c3"))):
+        line(V("ss" + name), V("ramp"), col("E", o), col("b" + name))
+        now("rs" + name)
         for h in (0, 1):
             line(col(c[h]), col("E", o), 1.0, col("E", o + 1 + h))
             line(V("rs" + name, 4 * h, 4 * h + 4), V("rm4"), col(c[h]))
-    for name, o in (("A", 0), ("B", 4)):
-        now("ss" + name)
-        line(V("ss" + name), V("Tab"), col("E", o), col("b" + name))
+    now("fag")
     dmas("dfg", [("y", group("fag", b), H(T.fa[:, 512 * b:512 * b + 512])) for b in range(8)])
+    now("ramp")
+    dmas("dramp", [("y", V("Tab"), V("ramp"))])
+    now("rows")
     dmas("dtab", [("y", X("Tab", (slice(f, 128, 16), every), 0, 512), H(T["x" + "ab"[f]][:, :])) for f in (0, 1)])
-
-    def places(t, dst, a, b, d, e):
-        ts(V(a), V(t), 0x70, OP.bitwise_and)
-        ts(V(b), V(t), 5, OP.arith_shift_right, 0x70, OP.bitwise_and)
-        tt(V(d), V(a), V(b), OP.subtract)
-        ts(V(d), V(d), 31, OP.mult)
-        tt(V(e), V(d), V(t), OP.add)
-        copy(V(dst), V(e), "v")
 
     def runs(x, yl, sn, tr, snu, off, fl):
         copy(V(yl, 0, 32), x, "v")
@@ -487,59 +447,48 @@ def rank_program(g, core, T, topo):
         tt(V(tr), V(tr), V(yl, 0, 32), OP.max)
         copy(V(off), V(tr), "v")
 
-    def lists(src, rs, dst, parts):
+    def lists(rows, rs, dst, parts):
         p = bank()
-        at = [128 * (4 * (k % 8) + k // 8) for k in range(32)]
         for i, name in enumerate(parts):
             now(name)
-            mms([(V(p, k, 256, 32), V(src, at[k], at[k] + 128), V(rs), True, True) for k in range(32)
-                 if k % 8 * len(parts) // 8 == i])
+            mms([(V(p, k, 256, 32), rows[k], V(rs), True, True) for k in range(32) if k % 8 * len(parts) // 8 == i])
         copies([(V(dst, **low), V(p, 0, 128, **low)), (V(dst, **high), V(p, 128, 256, **high))], "v")
 
-    now("vex")
-    if not VDMA:
-        p = bank()
-        mm(V(p), V("vsel", p1=8), V("v8", p1=8))
-        copy(V("vex"), V(p))
+    def blocks(name):
+        return [V(name, 128 * (4 * (k % 8) + k // 8), 128 * (4 * (k % 8) + k // 8) + 128) for k in range(32)]
+
     now("runsA")
     runs(V("txa"), "yl", "sa", "ta", "snA", "offA", "flA")
     now("jc")
     ts(col("hu"), col("Di"), 192, OP.is_ge, 4096, OP.mult)
     ts(V("jc"), V("txc"), col("hu"), OP.add)
     ts(V("jb"), V("txb"), col("hu"), OP.add)
-    now("la")
-    if TILA:
-        copy(V("laf"), V("tla"), "v")
-        tiled("La", "laf", list(range(4)), 8)
-    for r in range(0 if TILA else 4):
-        copies([(quarter("La", a, 8 * r, 8 * r + 8), quarter("tla", r, 8 * a, 8 * a + 8)) for a in range(4)], "v")
     now("placeA")
-    places("tla", "pia", "ba", "bb", "bd", "pif")
-    now("wf0")
-    for i in range(8):
-        if i == WF0:
-            now("wf1")
-        fill(V("W", 512 * i, 512 * i + 512), 0.0)
+    copy(V("pia"), V("tla"), "v")
+    copy(V("pif"), V("tla"), "v")
+    now("la")
+    tiled("La", "pif", list(range(4)), 8)
+    now("wf")
+    for i in range(FILLS):
+        nought(V("W", 512 * i, 512 * i + 512))
+    now("wd")
+    dmas("dw", [("y", V("W", 512 * i, 512 * i + 512), V("W", 0, 512)) for i in range(FILLS, 8)])
     now("putA")
     put(V("W"), V("pia"), V("ssA"))
     now("tm")
     for b in range(8):
-        scaled(X("tm", (every, b // 2, every, b % 2, every), b, b + 1), V("pif"), col("rm8", b))
+        line(X("tm", (every, b // 2, every, b % 2, every), b, b + 1), V("pif"), col("rm8", b))
     p = bank()
     now("tmm")
-    w = 8 // TM
-    mms([(V(p, 32 * k, 32 * k + 32 * w), V("E"), X("tm", (every,) * 4 + (slice(k, k + w),)), True, True) for k in range(0, 8, w)])
+    mms([(V(p, 32 * k, 32 * k + 32), V("E"), X("tm", (every,) * 4 + (k,)), True, True) for k in range(8)])
     now("lr")
-    if w == 1:
-        copy(V("Lr"), V(p, 0, 256), "v")
-    else:
-        copies([(V("Lr", 32 * k, 256, 1) if 0 else V("Lr", 32 * k, 32 * k + 32),
-                 V(p, 32 * w * (k // w) + k % w, 32 * w * (k // w + 1), w)) for k in range(8)], "v")
-    now("r")
+    copy(V("Lr"), V(p, 0, 256), "v")
     for i in range(8):
+        if i < 2:
+            now("r" if i else "r0")
         pick(V("R", 512 * i, 512 * i + 512), V("W"), V("Lr", 32 * i, 32 * i + 32))
-    lists("R", "rsA", "idx", ["idx0", "idx1", "idx2", "idx"])
-    lists("W", "rsA", "inva", ["inva"])
+    lists(blocks("R"), "rsA", "idx", ["idx0", "idx1", "idx2", "idx3"])
+    lists([V("W", k, 4096, 32) for k in range(32)], "rsA", "inva", ["inva"])
 
     for n, q in enumerate(come):
         buf = "CB" if q == me else "LCB"
@@ -549,13 +498,17 @@ def rank_program(g, core, T, topo):
             mms([(V(p, 256 * c, 256 * c + 256), X("SELB", (every, 2 * c + h, every, every)), V(buf, 256 * q, 256 * q + 256),
                   True, True) for c in range(2)])
             copy(V("CW", at, at + 512), V(p))
-        for name, dx, src, dst in (("c", 4096, low, high), ("b", -4096, high, low)):
-            now(name + str(n))
-            w = 512 * FINE[n]
+        for name, dx, src, dst in (("c" + str(n), 4096, low, high), ("b" + str(n), -4096, high, low)):
+            now(name)
+            w = 1024 if name in BY_DMA else 512
             for at in range(4096 + 1024 * q, 5120 + 1024 * q, w):
-                copy(V("CW", at + dx, at + dx + w, **dst), V("CW", at, at + w, **src))
+                o, i = V("CW", at + dx, at + dx + w, **dst), V("CW", at, at + w, **src)
+                if name in BY_DMA:
+                    dmas("d" + name, [("y", o, i)])
+                else:
+                    copy(o, i)
     now("vc")
-    pick2(V("vc"), X("CW", (every, slice(4096, 12288)), 4096, 12288), V("jc"), V("vex"), OP.mult)
+    pick2(V("vc"), V("CW", 4096, 12288), V("jc"), V("vex"), OP.mult)
 
     def addruns(src, fl, off, z, scn):
         o, a, b = V(scn), V(fl, 7, 519), V(src)
@@ -577,42 +530,44 @@ def rank_program(g, core, T, topo):
             copy(V(win + str(me), 8 + 512 * h, 520 + 512 * h), V(p))
         expect(land, 128, sem)
 
-    def spread(buf, q, win, at, dx, parts, full):
+    def spread(buf, q, win, at, dx, parts, cross):
         src = V(buf, 128 * q, 128 * q + 128)
-        for ms, how in zip(parts, full):
+        for ms, how in zip(parts, cross):
             w = 128 * len(ms)
             here, there = (at[ms[0]], at[ms[0]] + w), (at[ms[0]] + dx, at[ms[0]] + dx + w)
-            for x, to in ((0, here), (4, there))[:2 if how == "t" else 1]:
-                p = bank()
-                mms([(V(p, 128 * j, 128 * j + 128), X("SEL", (every, m + x, every, every)), src, True, True)
-                     for j, m in enumerate(ms)])
-                if how == "p":
-                    copies([(V(win, *here), V(p, 0, w)), (V(win, *there, **low), V(p, 0, w, **high)),
-                            (V(win, *there, **high), V(p, 0, w, **low))])
-                else:
-                    copy(V(win, *to), V(p, 0, w))
+            p = bank()
+            mms([(V(p, 128 * j, 128 * j + 128), X("SEL", (every, m, every, every)), src, True, True) for j, m in enumerate(ms)])
+            if how == "p":
+                copies([(V(win, *here), V(p, 0, w)), (V(win, *there, **low), V(p, 0, w, **high)),
+                        (V(win, *there, **high), V(p, 0, w, **low))])
+                continue
+            copy(V(win, *here), V(p, 0, w))
+            pairs = [(V(win, *there, **low), V(win, *here, **high)), (V(win, *there, **high), V(win, *here, **low))]
             if how == "s":
-                copy(V(win, *there, **low), V(win, *here, **high))
-                copy(V(win, *there, **high), V(win, *here, **low))
+                for o, i in pairs:
+                    copy(o, i)
+            else:
+                part["dmas"] += 1
+                dmas("dx%d" % part["dmas"], [("y", o, i) for o, i in pairs])
 
     def sums(buf, n, win, sem):
-        full = FULL[sem][n]
-        w = 4 // len(full)
+        cross = CROSS[sem][n]
+        w = 4 // len(cross)
         now(sem + str(n))
         spread(buf, come[n], win + str(come[n]), [8 + 128 * m for m in range(4)], 512,
-               [range(i, i + w) for i in range(0, 4, w)], full)
+               [range(i, i + w) for i in range(0, 4, w)], cross)
 
     def factor(buf, n):
-        q, full = come[n], FULL["n"][n]
+        q, cross = come[n], CROSS["n"][n]
         now("n" + str(n))
         spread(buf, q, "Aw", [1024 * q + 512 * (m % 2) + 128 * (m // 2) for m in range(4)], 256,
-               [(0, 2), (1, 3)] if len(full) == 2 else [(m,) for m in range(4)], full)
+               [(0, 2), (1, 3)] if len(cross) == 2 else [(m,) for m in range(4)], cross)
 
     now("w1")
     pick2(V("w1"), V("CW", 0, 8192), V("jb"), V("vc"), OP.mult)
     addruns("w1", "flA", "offA", "zA", "scn")
     reduce("zA", "LP", "p", "PT", "pw", "A")
-    zeros("zB", ZB0, ZB1)
+    zeros("zB", 0, ZB)
 
     def gather(win, n, lst, acc, lo=0, hi=32):
         q = come[n]
@@ -624,21 +579,21 @@ def rank_program(g, core, T, topo):
 
     now("fas")
     pick(V("faS"), V("far"), V("La"))
-    for n in range(4):
-        if n:
-            sums("LP", n, "pw", "p")
-        if n < 3:
-            now("ac%d" % n)
-            gather("pw", n, "idx", "ac")
+    for n in (1, 2, 3):
+        sums("LP", n, "pw", "p")
+    for n in range(3):
+        now("ac%d" % n)
+        gather("pw", n, "idx", "ac")
     now("ot")
-    for r in ring[:OWN] + [me] + ring[OWN:3]:
+    for r in [ring[0], me, ring[1], ring[2]]:
         lo, hi = 128 * r, 128 * r + 128
         gather("pw", 3, "idx", "ac", 8 * r, 8 * r + 8)
         tt(V("OT", lo, hi), V("ac3", lo, hi), V("faS", lo, hi), OP.mult)
         if r != me:
             send(r, V("OT", lo, hi), T["LA"][:, 128 * me:128 * me + 128], "n")
     expect("LA", 128, "n")
-    zeros("zB", ZB1, 4096)
+    iota(V("kp"), [[1, 16], [256, 2]], 0, 0)
+    zeros("zB", ZB, 4096)
 
     now("ob")
     ts(V("oa"), V("tob"), 15, OP.bitwise_and)
@@ -665,28 +620,26 @@ def rank_program(g, core, T, topo):
     now("vco")
     pick(V("vco"), V("vc"), V("jo"))
     now("placeB")
-    places("tlb", "pib", "be", "bf", "bg", "pij")
+    ts(V("be"), V("tlb"), 0x70, OP.bitwise_and)
+    ts(V("bf"), V("tlb"), 5, OP.arith_shift_right, 0x70, OP.bitwise_and)
+    tt(V("bg"), V("be"), V("bf"), OP.subtract)
+    ts(V("bg"), V("bg"), 31, OP.mult)
+    tt(V("pij"), V("bg"), V("tlb"), OP.add)
+    copy(V("pib"), V("pij"), "v")
     now("putB")
-    for lo in range(0, 32, 32 // IB):
-        put(V("W"), V("pib", lo, lo + 32 // IB), V("ssB", 16 * lo, 16 * lo + 512 // IB))
-    lists("W", "rsB", "invb", ["invb"])
+    put(V("W"), V("pib"), V("ssB"))
+    lists(blocks("W"), "rsB", "invb", ["invb"])
 
     now("ya0")
     gather("pw", 0, "inva", "ya")
-    if YA == 0:
-        for n in (1, 2, 3):
-            pick(V("ya%d" % n), V("pw%d" % come[n]), V("inva", 32 * come[n], 32 * come[n] + 32))
-        now("ya")
-        p = bank()
-        for n in range(4):
-            mms([(V(p), V("eye"), V("ya%d" % n), n == 0, n == 3)])
-        tt(V("yo"), V(p), V("fag"), OP.mult)
+    now("jp")
+    ts(col("p16"), col("Ei"), 16, OP.mult)
+    ts(V("jp"), V("kp"), col("p16"), OP.add)
     now("ya")
-    for lo in range(0, 32, 32 // YA) if YA else ():
-        hi = lo + 32 // YA
-        for n in (1, 2, 3):
-            gather("pw", n, "inva", "ya", lo, hi)
-        tt(V("yo", 16 * lo, 16 * hi), V("ya3", 16 * lo, 16 * hi), V("fag", 16 * lo, 16 * hi), OP.mult)
+    for n in (1, 2, 3):
+        gather("pw", n, "inva", "ya")
+    now("yo")
+    pick2(V("yo"), V("ya3"), V("jp"), V("fag"), OP.mult)
 
     for n in range(4):
         factor("LA" if n else "OT", n)
@@ -694,28 +647,31 @@ def rank_program(g, core, T, topo):
     pick2(V("w2"), V("Aw"), V("ja"), V("vco"), OP.mult)
     addruns("w2", "flB", "offB", "zB", "scm")
     reduce("zB", "LQ", "q", "PU", "qw", "B")
-    dmas("dya", [("y", H(T.ya[:, 512 * b:512 * b + 512]), group("yo", b)) for b in range(8)], [left("q")] if YAG else [])
+    now("start")
+    dmas("dya", [("y", H(T.ya[:, 512 * b:512 * b + 512]), group("yo", b)) for b in range(8)])
 
-    for n in range(4):
-        if n:
-            sums("LQ", n, "qw", "q")
+    for n in (1, 2, 3):
+        sums("LQ", n, "qw", "q")
+    for n in range(3):
         now("yb%d" % n)
-        if n < 3:
-            gather("qw", n, "invb", "yb")
-    for h in range(YB):
-        lo, hi = 512 * h // YB, 512 * (h + 1) // YB
+        gather("qw", n, "invb", "yb")
+    now("yb3")
+    for h in (0, 1):
+        lo, hi = 256 * h, 256 * h + 256
         gather("qw", 3, "invb", "yb", lo // 16, hi // 16)
         dmas("dyb%d" % h, [("ys"[b % 2], H(T.yb[:, 512 * b + lo:512 * b + hi]), group("yb3", b, lo, hi)) for b in range(8)])
 
+    def tiles(o):
+        return sorted({v[0] for v in o["outs"] + o["ins"] if v[0] and v[0][0] == "#"})
+
     users = {}
     for o in ops:
-        for n in {v[0] for v in o["outs"] + o["ins"] if v[0] and v[0][0] == "#"}:
+        for n in tiles(o):
             users[n] = users.get(n, 0) + 1
     free = list(banks)
     for i in order(ops):
         o = ops[i]
-        tiles = {v[0] for v in o["outs"] + o["ins"] if v[0] and v[0][0] == "#"}
-        for n in tiles:
+        for n in tiles(o):
             if n not in where:
                 assert free, "no bank"
                 where[n] = free.pop(0)
@@ -728,7 +684,7 @@ def rank_program(g, core, T, topo):
             emit_send(*o["subs"])
         else:
             emit_come(*o["subs"])
-        for n in tiles:
+        for n in tiles(o):
             users[n] -= 1
             if not users[n]:
                 free.append(where[n])

from concourse.mybir import AluOpType, ActivationFunctionType, AxisListType

OP = AluOpType
COPY = ActivationFunctionType.Copy
IDENTITY = ActivationFunctionType.Identity
ZW = 4728
SIZES = {
    "int32": {128: "Di Ei", 32: "tla tlb tlc txa txb txc tob", 512: "Tab ramp"},
    "uint16": {256: "Lr"},
    "bfloat16": {128: "E32", 512: "ssA ssB fag", 1024: "CB LCB", 4096: "FR far W R", 12288: "CW"},
    "float32": {128: "E N1 N2 eye", 9 * 1032 + 520: "win",
                512: "vex vc vco w1 w2 scn scm PT PU LP OT LA LQ faS ac0 ac1 ac2 ac3 ya0 ya1 ya2 ya3 yo G yb0 yb1 yb2 yb3",
                4096: "Aw", ZW: "zA zB"},
}
SMALL = {
    "int32": {8: "kgi kgs", 32: "be bf pij oa oc od nA nx kp"},
    "uint16": {32: "La ja jb jc jo jp jq pia pib snA snB offA offB", 64: "L2", 128: "idx inva invb"},
    "bfloat16": {8: "rsA rsB"},
    "float32": {4: "rm4 hf hu p16 n0 b1 b2 b3 b4 bA bB c0 c1 c2 c3", 8: "rm8 w01",
                32: "trash pif sa ta sb tb bg ny nz", 40: "yl ym", 64: "F lf"},
}
SCRATCH = {n: ("sbuf", [128, c], d) for d, x in SIZES.items() for c, names in x.items() for n in names.split()}
PLACE = {}
for _d, _x in SMALL.items():
    _at = 0
    for _c, _names in _x.items():
        for _n in _names.split():
            PLACE[_n] = ("small_" + _d, _at, _c)
            _at += -(-_c // 16) * 16
    SCRATCH["small_" + _d] = ("sbuf", [128, _at], _d)
for _i, _n in enumerate("pw0 pw1 pw2 pw3 qw0 qw1 qw2 qw3 flA flB".split()):
    PLACE[_n] = ("win", 1032 * _i, 1032 if _i < 8 else 520)
SCRATCH["SEL"] = ("sbuf", [128, 4, 2, 64], "float32")
SCRATCH["SELB"] = ("sbuf", [128, 4, 2, 64], "bfloat16")
SCRATCH["tm"] = ("sbuf", [128, 4, 4, 2, 8], "float32")
SCRATCH["T4"] = ("sbuf", [128, 16, 2, 16], "float32")
SCRATCH["T1"] = ("sbuf", [128, 2, 2, 16], "float32")
for _b in range(8):
    SCRATCH["pb%d" % _b] = ("psum", [128, 512], "float32")
ENG = {"v": "sv", "s": "ss", "t": "st", "g": "sg"}
SEMAPHORES = (list(ENG.values()) + ["dt" + t for t in ("la", "lb", "lc", "xa", "xb", "xc", "ob")]
              + ["df0", "df1", "df2", "df3", "drep", "dv", "dfa", "dfg", "dramp", "dtab", "dw"]
              + ["d" + k + str(n) for k in "cb" for n in range(3)] + ["dx%d" % i for i in range(1, 11)]
              + ["dya", "dyb0", "dyb1"] + ["l" + k for k in "cpnq"] + ["%s%d" % (k, d) for k in "cpnq" for d in (1, 2, 3)])

PLAN = {
    "start": (0, 0, ""), "za": (0, 0, "sv"), "biasA": (0, 0.75, "s"), "next": (0, 0.01, ""), "selb": (0.6, 0.5, "s"),
    "wf": (1, 0, "vsv"), "wd": (1, 0, ""), "vex": (2, 0, ""), "ramp": (2, 0, ""), "ssA": (2, 0, "s"),
    "lf": (3, 0, ""), "front": (3, 0, "sv"), "rsA": (3, 0, "s"), "l1": (3, 0, "v"), "jc": (3.3, 0.15, ""),
    "runsA": (3.4, 0.5, "s"), "l2": (4, 0, "s"), "l3": (4, 0, "s"), "placeA": (4, 0, ""), "zero": (4, 0.5, ""),
    "lt": (4, 0, ""), "l0": (4, 0, "v"),
    "tm": (4.5, 0, "sssv"), "putA": (5, 0, ""), "x0": (5, 0, "s"), "c0": (5, 0, ""), "b0": (5, 0, ""), "rows": (5.1, 0, ""),
    "ob": (6, 0, ""), "tmm": (6, 0, ""), "lr": (6.6, 0, ""), "r0": (7, 0, "v"),
    "x1": (7, 0, "s"), "c1": (7, 0, ""), "b1": (7, 0, ""), "x2": (7, 0.1, "s"), "c2": (7, 0, "v"), "b2": (7, 0, "v"),
    "far": (7.2, 0, ""), "x3": (7.3, 0, "sv"), "c3": (7, 0, "sv"), "vc": (7, 0, ""), "la": (7.4, 0, ""), "b3": (7.5, 0, "s"),
    "w1": (8, 0, ""), "r": (8, 0.5, "ssssssv"), "idx0": (9, 0, ""), "idx1": (10, 0, ""), "fag": (10, 0, ""), "tab": (10, 0, "s"),
    "placeB": (10.7, 0.2, ""), "redA": (11.1, 0.1, ""), "turn": (11.5, 0, ""), "ownA": (12, 0, "s"), "ja": (13, 0, ""),
    "fas": (14, 0, "s"), "idx2": (15, 0, ""), "idx3": (15, 0, ""), "ac0": (15, 0, "v"), "p1": (16, 0, "sv"), "p2": (17, 0, "s"),
    "ac1": (18, 0, ""), "p3": (18.2, 0, "vs"), "ac2": (20, 0, ""), "ot": (22, 0.4, ""), "vco": (22, 0, "s"), "ssB": (23, 0, "s"),
    "inva": (24.4, 0, ""), "runsB": (24.7, 0.4, "s"), "n0": (24.78, 0.15, "vs"), "rsB": (25, 0, "s"), "n1": (26, 0.5, "s"),
    "n2": (28, 0, "sv"), "putB": (28, 0, ""), "n3": (28, 0, "sv"), "w2": (30, 0, ""), "jp": (31, 0, ""), "invb": (32, 0, ""),
    "ya0": (32, 0, "s"), "redB": (33.11, 0.3, ""), "ya": (34, 0.4, ""), "yo": (35, 0, ""), "ownB": (36, 0, "s"),
    "yb0": (37, 0, "v"), "q1": (37.3, 0, "svs"), "q2": (41, 0.15, "svs"), "yb1": (42, 0, ""), "q3": (42, 0.2, "svs"),
    "yb2": (43, 0, ""), "yb3": (44, 0, ""),
}
CROSS = {"p": ("", "pp", "pp", "pp"), "n": ("dp", "dd", "pp", "pppp"), "q": ("", "pppp", "ppps", "pppp")}
BY_DMA = ("c0", "b0", "c1", "b1")
SPREAD = 1536
FILLS = 4
ZA, ZB = 1024, 2048


def meet(a, b):
    return a[1] < b[2] and b[1] < a[2] and a[3] < b[4] and b[3] < a[4]


def covers(a, b):
    return a[1] <= b[1] and b[2] <= a[2] and a[3] <= b[3] and b[4] <= a[4]


def order(ops):
    turn, last, tail = [], {}, ()
    for i, op in enumerate(ops):
        pred = set(op["after"])
        both = [(v, True) for v in op["outs"] if v[0]] + [(v, False) for v in op["ins"] if v[0]]
        for v, w in both:
            pred.update(j for r, w2, j in last.setdefault(v[0], []) if (w or w2 or v[0][0] == "#") and meet(v, r))
        for v, w in both:
            rec = last[v[0]]
            if w:
                rec[:] = [x for x in rec if not covers(v, x[0])]
            rec.append((v, w, i))
        if op["eng"] == "g":
            pred.update(tail)
            tail = (i,)
        turn.append(max([op["turn"]] + [turn[j] for j in pred if j != i]))
    return sorted(range(len(ops)), key=lambda i: (turn[i], i))


def rank_program(g, core, T, topo):
    me = T.rank_of(core)
    if me is None:
        return
    N = len(T.cores)
    queue = {"v": g.vector, "s": g.scalar, "t": g.tensor, "g": g, "y": g.sync}
    count = {}
    know = {e: {} for e in queue}
    waited = {}
    seen = {}
    banks = {"pb%d" % b: {} for b in range(8)}
    where = {}
    ops = []
    part = {"turn": 0.0, "step": 0.0, "queues": "", "n": 0, "tiles": 0, "dmas": 0}
    sent = {}

    def wait(e, tok):
        sem, val, _, kn = tok
        if know[e].get(sem, 0) >= val:
            return
        queue[e].wait_ge(T.sem[sem], val)
        waited[sem] = max(waited.get(sem, 0), val)
        for k2, v2 in kn.items():
            if know[e].get(k2, 0) < v2:
                know[e][k2] = v2
        know[e][sem] = val

    def before(e, outs, ins):
        for v, w in [(x, True) for x in outs] + [(x, False) for x in ins]:
            n = where.get(v[0], v[0])
            if n in banks:
                for e2 in list(banks[n]):
                    if e2 != e:
                        wait(e, banks[n].pop(e2))
                continue
            for r, w2, tok in seen.get(n, []):
                if (w or w2) and meet(v, r):
                    wait(e, tok)

    def after(outs, ins, tok):
        for v, w in [(x, True) for x in outs] + [(x, False) for x in ins]:
            n = where.get(v[0], v[0])
            if n in banks:
                banks[n][tok[2]] = tok
                continue
            old = seen.setdefault(n, [])
            if w:
                old[:] = [x for x in old if not covers(v, x[0])]
            old.append((v, w, tok))

    def emit(e, outs, ins, call):
        before(e, outs, ins)
        sem = ENG[e]
        call(queue[e], e).then_inc(T.sem[sem], 1)
        count[sem] = count.get(sem, 0) + 1
        after(outs, ins, (sem, count[sem], e, dict(know[e])))
        if e == "g" and outs[0][3]:
            wait(e, (sem, count[sem], e, {}))

    def emit_dmas(sem, items, extra):
        kn = {}
        for e, o, i in items:
            before(e, [o] if o[0] else [], ([i] if i[0] else []) + extra)
            queue[e].dma_start(out=o[5](), in_=i[5]()).then_inc(T.sem[sem], 16)
            count[sem] = count.get(sem, 0) + 16
            for k2, v2 in know[e].items():
                kn[k2] = max(kn.get(k2, 0), v2)
        tok = (sem, count[sem], "d", kn)
        for e, o, i in items:
            after([o] if o[0] else [], [i] if i[0] else [], tok)

    def engines(src, dst, sem):
        first = sem == "c" and (T.rank_of(dst) - T.rank_of(src)) % N == 1
        return topo.engines(src, dst)[::2 if first else 1]

    def emit_send(q, src, dst, sem):
        to = T.cores[q]
        before("g", [], [src])
        rid, pid, _ = topo.addr(to)
        g.remote_dma(out_ap=dst, in_ap=src[5](), remote_sem=T.sem["%s%d" % (sem, (q - me) % N)], local_sem=T.sem["l" + sem],
                     pid=pid, routing_id=rid, dma_engine_mask=sum(1 << e for e in engines(core, to, sem)))
        count["l" + sem] = count.get("l" + sem, 0) + len(engines(core, to, sem))

    def emit_come(v, s, n):
        count[s] = n or count[s]
        after([v], [], (s, count[s], "r", {}))

    def V(name, lo=0, hi=None, step=1, p0=0, p1=128):
        at = 0
        if name in PLACE:
            name, at, w = PLACE[name]
            hi = w if hi is None else hi
        elif hi is None:
            hi = 512 if name[0] == "#" else SCRATCH[name][1][1]
        lo, hi = lo + at, hi + at

        def ap():
            t = T[where.get(name, name)]
            return t[p0:p1, lo:hi] if step == 1 else t[p0:p1, lo:hi:step]
        return (name, lo, hi, p0, p1, ap)

    def X(name, index, lo=0, hi=8):
        return (name, lo, hi, 0, 128, lambda: T[name][index])

    def H(ap):
        return (None, 0, 0, 0, 0, lambda: ap)

    def group(name, b, lo=0, hi=None):
        return V(name, lo, hi, p0=16 * b, p1=16 * b + 16)

    def quarter(name, a, lo, hi):
        return V(name, lo, hi, p0=32 * a, p1=32 * a + 32)

    def col(name, j=0):
        return V(name, j, j + 1)

    def bank():
        part["tiles"] += 1
        return "#%d" % part["tiles"]

    def now(name):
        part["turn"], part["step"], part["queues"] = PLAN[name]
        part["n"] = 0

    def op(eng, outs, ins, subs, kind="c", needs=()):
        if eng == "vs":
            eng = part["queues"][part["n"] % len(part["queues"])]
            part["n"] += 1
        ops.append({"eng": eng, "outs": outs, "ins": ins, "subs": subs, "kind": kind, "after": list(needs),
                    "turn": part["turn"] if eng in "vsty" else 0.0})
        if eng in "vst":
            part["turn"] += part["step"]
        return len(ops) - 1

    def one(eng, outs, ins, call):
        op(eng, outs, ins, [(outs, ins, call)])

    def copies(pairs, e="vs"):
        op(e, [o for o, _ in pairs], [i for _, i in pairs],
           [([o], [i], lambda q, x, o=o, i=i: q.tensor_copy(o[5](), i[5]()) if x == "v" else q.activation(o[5](), i[5](), COPY))
            for o, i in pairs])

    def copy(o, i, e="vs"):
        copies([(o, i)], e)

    def line(o, i, a, b=0.0):
        def call(q, x):
            a1 = a[5]() if isinstance(a, tuple) else a
            b1 = b[5]() if isinstance(b, tuple) else b
            if x == "v":
                return q.tensor_scalar(o[5](), i[5](), a1, b1, OP.mult, OP.add)
            return q.activation(o[5](), i[5](), IDENTITY, bias=b1, scale=a1)
        one("vs", [o], [i] + [s for s in (a, b) if isinstance(s, tuple)], call)

    def nought(o):
        one("vs", [o], [V("G")], lambda q, x: q.memset(o[5](), 0.0) if x == "v"
            else q.activation(o[5](), V("G")[5](), COPY, scale=0.0))

    def ts(o, i, s1, op0, s2=None, op1=None):
        def call(q, x):
            a1 = s1[5]() if isinstance(s1, tuple) else s1
            a2 = s2[5]() if isinstance(s2, tuple) else s2
            if op1 is None:
                return q.tensor_scalar(o[5](), i[5](), a1, None, op0)
            return q.tensor_scalar(o[5](), i[5](), a1, a2, op0, op1)
        one("v", [o], [i] + [s for s in (s1, s2) if isinstance(s, tuple)], call)

    def tt(o, a, b, f):
        one("v", [o], [a, b], lambda q, x: q.tensor_tensor(o[5](), a[5](), b[5](), f))

    def turned(o, i):
        one("v", [o], [i], lambda q, x: q.transpose(o[5](), i[5]()))

    def fill(o, c):
        one("v", [o], [], lambda q, x: q.memset(o[5](), c))

    def ind(w, l):
        return w[5]().indirect(l[5]())

    def pick(o, w, l):
        one("vs", [o], [w, l],
            lambda q, x: q.tensor_copy(o[5](), ind(w, l)) if x == "v" else q.activation(o[5](), ind(w, l), COPY))

    def pick2(o, w, l, b, f):
        one("v", [o], [w, l, b], lambda q, x: q.tensor_tensor(o[5](), ind(w, l), b[5](), f))

    def put(w, l, i):
        one("v", [w], [l, i], lambda q, x: q.tensor_copy(ind(w, l), i[5]()))

    def mms(items):
        op("t", [o for o, _, _, _, _ in items], [x for _, l, r, _, _ in items for x in (l, r)],
           [([o], [l, r], lambda q, x, o=o, l=l, r=r, a=a, z=z: q.matmul(o[5](), l[5](), r[5](), a, z))
            for o, l, r, a, z in items])

    def mm(o, l, r):
        mms([(o, l, r, True, True)])

    def iota(o, pattern, base, cm):
        if SCRATCH[o[0]][2] == "int32":
            one("g", [o], [], lambda q, x: q.iota(o[5](), pattern, base, cm))
        else:
            one("g", [o], [], lambda q, x: q.iota(o[5](), pattern, base, cm, allow_small_or_imprecise_dtypes=True))

    def zeros(name, lo, hi):
        iota(V(name, lo, hi), [[0, hi - lo]], 0, 0)

    def diagonal(o, ones, pattern, base):
        one("g", [o], [ones], lambda q, x: q.affine_select(o[5](), ones[5](), pattern, OP.is_equal, 0.0, base, 1))

    def selector(name, i):
        diagonal(X(name, (every, every, i, every), i, i + 1), V("G", 0, 256), [[-16, 4], [0, 4], [-1, 16]], -64 * i)

    def dmas(sem, items, extra=()):
        outs = [o for _, o, _ in items if o[0]]
        ins = list(extra) + [i for _, _, i in items if i[0]]
        op("y", outs, ins, (sem, items, list(extra)), "dma")

    def send(q, src, dst, sem):
        sent[sem, (q - me) % N] = op("g", [], [src], (q, src, dst, sem), "send")

    def expect(buf, width, sem):
        for d in (1, 2, 3):
            q, s = (me - d) % N, "%s%d" % (sem, d)
            v = V(buf, q * width, (q + 1) * width)
            op("-", [v], [], (v, s, len(engines(T.cores[q], core, sem))), "come", [sent[sem, d]])

    def left(sem):
        v = ("left" + sem, 0, 1, 0, 128, None)
        op("-", [v], [], (v, "l" + sem, 0), "come", [sent[sem, d] for d in (1, 2, 3)])
        return v

    ring = [(me + d) % N for d in (1, 2, 3, 0)]
    come = [(me - d) % N for d in (0, 1, 2, 3)]
    low, high = {"p0": 0, "p1": 64}, {"p0": 64, "p1": 128}
    every = slice(None)

    def table(t, e):
        dmas("dt" + t, [(e, V("t" + t), H(T[t][:, :]))])

    for i, lo in enumerate(range(0, SPREAD, 1024)):
        hi = min(lo + 1024, SPREAD)
        dmas("df%d" % i, [("y", V("CW", 8192 + lo, 8192 + hi, p0=0, p1=16), H(T.fc[:, lo:hi])),
                          ("s", V("CW", 8192 + lo, 8192 + hi, p0=16, p1=32), H(T.fb[:, lo:hi]))])
    table("lc", "y")
    table("lb", "s")
    dmas("drep", [("ys"[b % 2], group("FR", b, SPREAD, 4096), H(T["f" + "cb"[b // 4]][:, SPREAD:4096])) for b in range(8)])
    for t in ("la", "xa", "xc", "xb", "ob"):
        table(t, "y")
    now("vex")
    dmas("dv", [("y", X("vex", (slice(o, 128, 16), every), 0, 512), H(T.v[:, :])) for o in range(16)])

    now("start")
    fill(V("G"), 1.0)
    iota(V("Di"), [[-1, 128]], 128, 1)
    iota(V("kgi"), [[-16, 8]], 0, 1)
    for a in (0, 1):
        iota(V("ramp", 256 * a, 256 * a + 256), [[1, 32], [32, 4], [128, 2]], 256 * a - 256, 0)
    iota(quarter("ramp", me, 0, 512), [[1, 512]], -256, 0)
    diagonal(V("eye"), V("G", 0, 128), [[-1, 128]], 0)
    iota(V("trash"), [[16, 32]], 4096, 1)
    iota(V("w01"), [[1, 8]], 0, 0)
    ts(V("Ei"), V("Di"), 15, OP.bitwise_and)
    ts(V("kgs"), V("kgi"), 4, OP.arith_shift_right)
    ts(V("E"), V("Ei"), 0, OP.is_equal)
    ts(V("rm8"), V("kgs"), 0, OP.is_equal)
    for f in (0, 1):
        ts(V("E32", 64 * f, 64 * f + 64), V("E", 0, 64), col("rm8", f), OP.mult)
    now("selb")
    for b in range(8):
        line(X("SELB", (every, b % 4, b // 4, every), b, b + 1), V("E", 0, 64), col("rm8", b))
    now("za")
    for lo in range(0, ZA, 512):
        nought(V("zA", lo, lo + 512))
    now("zero")
    fill(V("yl", 32, 81, 48), -1.0)
    fill(V("win", 0, 8 * 1032, 1032), 0.0)
    fill(V("win", 8 * 1032 + 7, 9 * 1032 + 8, 1032), 0.0)
    now("next")
    ts(col("n0"), col("E", 0), 0, OP.is_equal)
    ts(V("N1"), V("Di"), 129, OP.is_equal, col("n0"), OP.mult)
    ts(V("N2"), V("Di"), 113, OP.is_equal, col("E", 0), OP.mult)

    now("front")
    for lo in range(0, SPREAD, 512):
        p = bank()
        mm(V(p), V("E32", p1=32), V("CW", 8192 + lo, 8704 + lo, p1=32))
        copy(V("FR", lo, lo + 512), V(p))

    def tiled(dst, src, readers, w):
        p = bank()
        mms([(quarter(p, a, w * r, w * r + w), V("eye", 32 * r, 32 * r + 32), V(src, w * a, w * a + w), True, True)
             for r in readers for a in range(4)])
        pieces = [[r for r in readers if r >= readers[0]], [r for r in readers if r < readers[0]]]
        copies([(V(dst, w * x[0], w * x[-1] + w), V(p, w * x[0], w * x[-1] + w)) for x in pieces if x], "v")

    now("lf")
    copy(V("lf", 0, 32), V("tlc"), "v")
    copy(V("lf", 32, 64), V("tlb"), "v")
    for r in ring:
        if r == ring[1]:
            now("lt")
            tiled("L2", "lf", ring[1:], 16)
        now("l%d" % ((r - me) % N))
        if r == ring[0]:
            copies([(quarter("L2", a, 16 * r, 16 * r + 16), quarter("tl" + "cb"[a // 2], r, 16 * (a % 2), 16 * (a % 2) + 16))
                    for a in range(4)], "v")
        pick(V("CB", 256 * r, 256 * r + 256), V("FR"), V("L2", 16 * r, 16 * r + 16))
        if r != me:
            send(r, V("CB", 256 * r, 256 * r + 256), T["LCB"][:, 256 * me:256 * me + 256], "c")
    expect("LCB", 256, "c")
    for lo in range(ZA, 4096, 1024):
        zeros("zA", lo, min(lo + 1024, 4096))
    for i in (0, 1):
        selector("SEL", i)
    now("far")
    dmas("dfa", [("y", group("far", b), H(T.fa[:, :])) for b in range(8)], [left("c")])

    now("biasA")
    one("v", [col("hf")], [V("rm8")], lambda q, x: q.tensor_reduce(col("hf")[5](), V("rm8", 1, 8, 2)[5](), AxisListType.X, OP.add))
    tt(V("rm4"), V("rm8", 0, 8, 2), V("rm8", 1, 8, 2), OP.add)
    line(col("b1"), col("hf"), 512.0, 264.0)
    line(col("b2"), col("hf"), -512.0, 776.0)
    copy(quarter("b2", me, 0, 1), quarter("b1", me, 0, 1))
    for name, o, b, c in (("A", 0, "b3", ("c0", "c1")), ("B", 4, "b4", ("c2", "c3"))):
        now("ss" + name)
        line(col(b), col("b1"), col("E", o + 1))
        line(col("b" + name), col("b2"), col("E", o + 2), col(b))
        line(V("ss" + name), V("ramp"), col("E", o), col("b" + name))
        now("rs" + name)
        for h in (0, 1):
            line(col(c[h]), col("E", o), 1.0, col("E", o + 1 + h))
            line(V("rs" + name, 4 * h, 4 * h + 4), V("rm4"), col(c[h]))
    now("fag")
    dmas("dfg", [("y", group("fag", b), H(T.fa[:, 512 * b:512 * b + 512])) for b in range(8)])
    now("ramp")
    dmas("dramp", [("y", V("Tab"), V("ramp"))])
    now("rows")
    dmas("dtab", [("y", X("Tab", (slice(f, 128, 16), every), 0, 512), H(T["x" + "ab"[f]][:, :])) for f in (0, 1)])

    def runs(x, yl, sn, tr, snu, off, fl):
        copy(V(yl, 0, 32), x, "v")
        p = bank()
        mms([(V(p, 0, 32), V("N1"), V(yl, 0, 32), True, False), (V(p, 0, 32), V("N2"), V(yl, 1, 33), False, True)])
        tt(V(sn), V(p, 0, 32), V(yl, 0, 32), OP.is_equal)
        copy(V(snu), V(sn), "v")
        pick(V(fl, 8, 520), V("w01"), V(snu))
        tt(V(tr), V(sn), V("trash"), OP.mult)
        tt(V(tr), V(tr), V(yl, 0, 32), OP.max)
        copy(V(off), V(tr), "v")

    def lists(rows, rs, dst, parts):
        p = bank()
        for i, name in enumerate(parts):
            now(name)
            mms([(V(p, k, 256, 32), rows[k], V(rs), True, True) for k in range(32) if k % 8 * len(parts) // 8 == i])
        copies([(V(dst, **low), V(p, 0, 128, **low)), (V(dst, **high), V(p, 128, 256, **high))], "v")

    def blocks(name):
        return [V(name, 128 * (4 * (k % 8) + k // 8), 128 * (4 * (k % 8) + k // 8) + 128) for k in range(32)]

    now("runsA")
    runs(V("txa"), "yl", "sa", "ta", "snA", "offA", "flA")
    now("jc")
    ts(col("hu"), col("Di"), 192, OP.is_ge, 4096, OP.mult)
    ts(V("jc"), V("txc"), col("hu"), OP.add)
    ts(V("jb"), V("txb"), col("hu"), OP.add)
    now("placeA")
    copy(V("pia"), V("tla"), "v")
    copy(V("pif"), V("tla"), "v")
    now("la")
    tiled("La", "pif", list(range(4)), 8)
    now("wf")
    for i in range(FILLS):
        nought(V("W", 512 * i, 512 * i + 512))
    now("wd")
    dmas("dw", [("y", V("W", 512 * i, 512 * i + 512), V("W", 0, 512)) for i in range(FILLS, 8)])
    now("putA")
    put(V("W"), V("pia"), V("ssA"))
    now("tm")
    for b in range(8):
        line(X("tm", (every, b // 2, every, b % 2, every), b, b + 1), V("pif"), col("rm8", b))
    p = bank()
    now("tmm")
    mms([(V(p, 32 * k, 32 * k + 32), V("E"), X("tm", (every,) * 4 + (k,)), True, True) for k in range(8)])
    now("lr")
    copy(V("Lr"), V(p, 0, 256), "v")
    for i in range(8):
        if i < 2:
            now("r" if i else "r0")
        pick(V("R", 512 * i, 512 * i + 512), V("W"), V("Lr", 32 * i, 32 * i + 32))
    lists(blocks("R"), "rsA", "idx", ["idx0", "idx1", "idx2", "idx3"])
    lists([V("W", k, 4096, 32) for k in range(32)], "rsA", "inva", ["inva"])

    for n, q in enumerate(come):
        buf = "CB" if q == me else "LCB"
        now("x" + str(n))
        for h in range(2):
            p, at = bank(), 4096 + 1024 * q + 512 * h
            mms([(V(p, 256 * c, 256 * c + 256), X("SELB", (every, 2 * c + h, every, every)), V(buf, 256 * q, 256 * q + 256),
                  True, True) for c in range(2)])
            copy(V("CW", at, at + 512), V(p))
        for name, dx, src, dst in (("c" + str(n), 4096, low, high), ("b" + str(n), -4096, high, low)):
            now(name)
            w = 1024 if name in BY_DMA else 512
            for at in range(4096 + 1024 * q, 5120 + 1024 * q, w):
                o, i = V("CW", at + dx, at + dx + w, **dst), V("CW", at, at + w, **src)
                if name in BY_DMA:
                    dmas("d" + name, [("y", o, i)])
                else:
                    copy(o, i)
    now("vc")
    pick2(V("vc"), V("CW", 4096, 12288), V("jc"), V("vex"), OP.mult)

    def addruns(src, fl, off, z, scn):
        o, a, b = V(scn), V(fl, 7, 519), V(src)
        one("v", [o], [a, b], lambda q, x: q.tensor_tensor_scan(o[5](), a[5](), b[5](), 0.0, OP.mult, OP.add))
        put(V(z), V(off), V(scn))

    def reduce(z, land, sem, PT, win, name):
        now("red" + name)
        for q in ring[:3]:
            p = bank()
            mms([(V(p, 16 * b, 16 * b + 16), V(z, 1024 * q + b, 1024 * q + 1024, 8), V("E", 0, 16), True, True)
                 for b in range(8)])
            turned(V(PT, 128 * q, 128 * q + 128), V(p, 0, 128))
            send(q, V(PT, 128 * q, 128 * q + 128), T[land][:, 128 * me:128 * me + 128], sem)
        now("own" + name)
        for h in range(2):
            p = bank()
            mm(V(p), V("E"), V(z, 1024 * me + 512 * h, 1024 * me + 512 * h + 512))
            copy(V(win + str(me), 8 + 512 * h, 520 + 512 * h), V(p))
        expect(land, 128, sem)

    def spread(buf, q, win, at, dx, parts, cross):
        src = V(buf, 128 * q, 128 * q + 128)
        for ms, how in zip(parts, cross):
            w = 128 * len(ms)
            here, there = (at[ms[0]], at[ms[0]] + w), (at[ms[0]] + dx, at[ms[0]] + dx + w)
            p = bank()
            mms([(V(p, 128 * j, 128 * j + 128), X("SEL", (every, m, every, every)), src, True, True) for j, m in enumerate(ms)])
            if how == "p":
                copies([(V(win, *here), V(p, 0, w)), (V(win, *there, **low), V(p, 0, w, **high)),
                        (V(win, *there, **high), V(p, 0, w, **low))])
                continue
            copy(V(win, *here), V(p, 0, w))
            pairs = [(V(win, *there, **low), V(win, *here, **high)), (V(win, *there, **high), V(win, *here, **low))]
            if how == "s":
                for o, i in pairs:
                    copy(o, i)
            else:
                part["dmas"] += 1
                dmas("dx%d" % part["dmas"], [("y", o, i) for o, i in pairs])

    def sums(buf, n, win, sem):
        cross = CROSS[sem][n]
        w = 4 // len(cross)
        now(sem + str(n))
        spread(buf, come[n], win + str(come[n]), [8 + 128 * m for m in range(4)], 512,
               [range(i, i + w) for i in range(0, 4, w)], cross)

    def factor(buf, n):
        q, cross = come[n], CROSS["n"][n]
        now("n" + str(n))
        spread(buf, q, "Aw", [1024 * q + 512 * (m % 2) + 128 * (m // 2) for m in range(4)], 256,
               [(0, 2), (1, 3)] if len(cross) == 2 else [(m,) for m in range(4)], cross)

    now("w1")
    pick2(V("w1"), V("CW", 0, 8192), V("jb"), V("vc"), OP.mult)
    addruns("w1", "flA", "offA", "zA", "scn")
    reduce("zA", "LP", "p", "PT", "pw", "A")
    zeros("zB", 0, ZB)

    def gather(win, n, lst, acc, lo=0, hi=32):
        q = come[n]
        o, w, l = V(acc + str(n), 16 * lo, 16 * hi), V(win + str(q)), V(lst, 32 * q + lo, 32 * q + hi)
        if n == 0:
            pick(o, w, l)
        else:
            pick2(o, w, l, V(acc + str(n - 1), 16 * lo, 16 * hi), OP.add)

    now("fas")
    pick(V("faS"), V("far"), V("La"))
    for n in (1, 2, 3):
        sums("LP", n, "pw", "p")
    for n in range(3):
        now("ac%d" % n)
        gather("pw", n, "idx", "ac")
    now("ot")
    for r in [ring[0], me, ring[1], ring[2]]:
        lo, hi = 128 * r, 128 * r + 128
        gather("pw", 3, "idx", "ac", 8 * r, 8 * r + 8)
        tt(V("OT", lo, hi), V("ac3", lo, hi), V("faS", lo, hi), OP.mult)
        if r != me:
            send(r, V("OT", lo, hi), T["LA"][:, 128 * me:128 * me + 128], "n")
    expect("LA", 128, "n")
    iota(V("kp"), [[1, 16], [256, 2]], 0, 0)
    zeros("zB", ZB, 4096)

    now("ob")
    ts(V("oa"), V("tob"), 15, OP.bitwise_and)
    ts(V("oc"), V("tob"), 4, OP.arith_shift_right)
    ts(V("oa"), V("oa"), 32, OP.mult)
    tt(V("od"), V("oa"), V("oc"), OP.add)
    copies([(V("jq", h, 32, 2), V("od", 16 * h, 16 * h + 16)) for h in (0, 1)] + [(V("jo"), V("tob"))], "v")
    now("tab")
    pick(V("G"), V("Tab"), V("jq"))
    now("turn")
    turned(X("T4", (every,) * 4), V("G"))
    for h in (0, 1):
        turned(X("T1", (every, h, every, every), h, h + 1), X("T4", (every, every, h, slice(0, 2))))
    for h in (0, 1):
        turned(V("F", 32 * h, 32 * h + 32), X("T1", (every, every, h, every)))
    now("runsB")
    runs(V("F", 1, 64, 2), "ym", "sb", "tb", "snB", "offB", "flB")
    now("ja")
    copy(V("nA", **high), V("F", 0, 64, 2, **high), "v")
    ts(V("nx", **high), V("nA", **high), 256, OP.bitwise_and)
    ts(V("ny", **high), V("nx", **high), -2, OP.mult, 256, OP.add)
    tt(V("nz", **high), V("ny", **high), V("F", 0, 64, 2, **high), OP.add)
    copies([(V("ja", **low), V("F", 0, 64, 2, **low)), (V("ja", **high), V("nz", **high))], "v")
    now("vco")
    pick(V("vco"), V("vc"), V("jo"))
    now("placeB")
    ts(V("be"), V("tlb"), 0x70, OP.bitwise_and)
    ts(V("bf"), V("tlb"), 5, OP.arith_shift_right, 0x70, OP.bitwise_and)
    tt(V("bg"), V("be"), V("bf"), OP.subtract)
    ts(V("bg"), V("bg"), 31, OP.mult)
    tt(V("pij"), V("bg"), V("tlb"), OP.add)
    copy(V("pib"), V("pij"), "v")
    now("putB")
    put(V("W"), V("pib"), V("ssB"))
    lists(blocks("W"), "rsB", "invb", ["invb"])

    now("ya0")
    gather("pw", 0, "inva", "ya")
    now("jp")
    ts(col("p16"), col("Ei"), 16, OP.mult)
    ts(V("jp"), V("kp"), col("p16"), OP.add)
    now("ya")
    for n in (1, 2, 3):
        gather("pw", n, "inva", "ya")
    now("yo")
    pick2(V("yo"), V("ya3"), V("jp"), V("fag"), OP.mult)

    for n in range(4):
        factor("LA" if n else "OT", n)
    now("w2")
    pick2(V("w2"), V("Aw"), V("ja"), V("vco"), OP.mult)
    addruns("w2", "flB", "offB", "zB", "scm")
    reduce("zB", "LQ", "q", "PU", "qw", "B")
    now("start")
    dmas("dya", [("y", H(T.ya[:, 512 * b:512 * b + 512]), group("yo", b)) for b in range(8)])

    for n in (1, 2, 3):
        sums("LQ", n, "qw", "q")
    for n in range(3):
        now("yb%d" % n)
        gather("qw", n, "invb", "yb")
    now("yb3")
    for h in (0, 1):
        lo, hi = 256 * h, 256 * h + 256
        gather("qw", 3, "invb", "yb", lo // 16, hi // 16)
        dmas("dyb%d" % h, [("ys"[b % 2], H(T.yb[:, 512 * b + lo:512 * b + hi]), group("yb3", b, lo, hi)) for b in range(8)])

    def tiles(o):
        return sorted({v[0] for v in o["outs"] + o["ins"] if v[0] and v[0][0] == "#"})

    users = {}
    for o in ops:
        for n in tiles(o):
            users[n] = users.get(n, 0) + 1
    free = list(banks)
    for i in order(ops):
        o = ops[i]
        for n in tiles(o):
            if n not in where:
                assert free, "no bank"
                where[n] = free.pop(0)
        if o["kind"] == "c":
            for outs, ins, call in o["subs"]:
                emit(o["eng"], outs, ins, call)
        elif o["kind"] == "dma":
            emit_dmas(*o["subs"])
        elif o["kind"] == "send":
            emit_send(*o["subs"])
        else:
            emit_come(*o["subs"])
        for n in tiles(o):
            users[n] -= 1
            if not users[n]:
                free.append(where[n])
    for sem, n in count.items():
        if waited.get(sem, 0) < n:
            g.wait_ge(T.sem[sem], n)
